import numpy as np
import ml_dtypes


def mxq(x, axis, fmt="e4m3"):
    dtype, down = {"e4m3": (ml_dtypes.float8_e4m3fn, 7), "e5m2": (ml_dtypes.float8_e5m2, 14)}[fmt]
    v = np.moveaxis(np.asarray(x, np.float32).astype(ml_dtypes.bfloat16).astype(np.float64), axis, -1)
    blocks = v.reshape(v.shape[:-1] + (-1, 32))
    amax = np.abs(blocks).max(-1, keepdims=True)
    byte = np.maximum(np.where(amax > 0, np.frexp(amax)[1] - 1 + 127, 0) - down, 1)
    scale = np.exp2(byte - 127.0)
    codes = (blocks / scale).astype(np.float32).astype(dtype).astype(np.float64)
    return np.moveaxis((codes * scale).reshape(v.shape), -1, axis)


WIDE = False


def mx_kscale(k):
    if not WIDE:
        return np.ones(k)
    levels = np.array([10, -10, 5, -5, 0])
    if k % 512:
        return np.exp2(np.random.permutation(np.resize(levels, k // 32))).repeat(32)
    a = np.empty((k // 512, 16))
    for p in range(k // 512):
        a[p, :8] = np.random.permutation(np.resize(levels, 8))
        for g in range(8):
            far = levels[np.abs(levels - a[p, g]) >= 10]
            a[p, g + 8] = far[np.random.randint(len(far))]
    return np.exp2(a.ravel()).repeat(32)


def f64(x):
    return np.asarray(x).astype(np.float64)


def striped(idx):
    return np.tile(np.asarray(idx).reshape(-1, 16).T, (8, 1)).astype(np.uint16)


def unstriped(offs):
    return offs[:16].T.reshape(-1).astype(np.int64)


B, N, T, D, DV, NQ = 1, 1024, 4096, 512, 256, 128
PAGE = 128
CAP = 2.0


def setup_inputs():
    n = np.random.standard_normal
    pages = np.random.permutation(T // PAGE)[:B * N // PAGE]
    idx = (pages[:, None] * PAGE + np.arange(PAGE)[None, :]).reshape(-1)
    s = mx_kscale(D)[:, None]
    u = np.ones(T)
    u[idx] = mx_kscale(B * N)
    r = np.random.uniform(0.5, 2.0, T)
    k = n((D, T)) / s
    v = n((DV, T)) / (u * r)
    return {
        "qT": (n((B, D, NQ)) * s * (1.00 / np.sqrt(D))).astype(np.float32),
        "kT": k.astype(np.float32),
        "vT": v.astype(np.float32),
        "vs": np.tile(u * r, (128, 1)).astype(np.float32),
        "sink": (2.0 + 3.0 * n((B, NQ, 1))).astype(np.float32),
        "offs": striped(idx),
    }


def reference(qT, kT, vT, vs, sink, offs):
    idx = unstriped(offs)
    k = f64(kT)
    v = f64(vT)
    pick = lambda x: x[:, idx].reshape(x.shape[0], B, N).transpose(1, 0, 2)
    q = f64(qT)
    score = mxq(q, 1, "e4m3").transpose(0, 2, 1) @ mxq(pick(k), 1, "e4m3")
    score = CAP * np.tanh(score / CAP)
    m = np.maximum(score.max(-1, keepdims=True), f64(sink))
    p = np.exp(score - m)
    total = p.sum(-1, keepdims=True) + np.exp(f64(sink) - m)
    w = p * pick(f64(vs))[:, :1, :]
    y = mxq(w, 2, "e4m3") @ mxq(pick(v).transpose(0, 2, 1), 1, "e4m3")
    y = y / total
    return y

@@ -1,0 +1,260 @@
+import concourse.mybir as mybir
+from concourse.masks import make_identity
+
+NQ, D, DV, T, N = 128, 512, 256, 4096, 1024
+P = 128
+PACK = 4
+PASS = P * PACK
+PASSES = N // PASS
+LIST_ROWS = 16
+
+FLOPS = 2 * NQ * N * (D + DV)
+BYTES = 4 * (D * T + DV * T + D * NQ + T + NQ + NQ * DV) + 2 * P * (N // 16)
+
+F32 = mybir.dt.float32
+BF16 = mybir.dt.bfloat16
+U32 = mybir.dt.uint32
+U16 = mybir.dt.uint16
+U8 = mybir.dt.uint8
+FP8X4 = mybir.dt.float8_e4m3fn_x4
+ACT = mybir.ActivationFunctionType
+ALU = mybir.AluOpType
+PIECES = ((0, 512), (512, 1024))
+
+
+def tile_attend_x_cap_sink_kernel(tc, qT, kT, vT, vs, sink, offs, out):
+    nc = tc.nc
+    with (
+        tc.tile_pool(name="held", bufs=1) as held,
+        tc.tile_pool(name="shared0", bufs=1) as shared0,
+        tc.tile_pool(name="shared1", bufs=1) as shared1,
+        tc.psum_pool(name="turned", bufs=4) as turned_pool,
+        tc.psum_pool(name="sums", bufs=1) as sums_pool,
+    ):
+        offsets = held.tile([P, N // LIST_ROWS], U16, name="offsets")
+        nc.sync.dma_start(offsets[:], offs)
+
+        def listed(window, start, stop):
+            return window[:].indirect(offsets[:, start // LIST_ROWS : stop // LIST_ROWS])
+
+        tiny = held.tile([P, 1], F32, name="tiny")
+        nc.vector.memset(tiny[:], 0.0)
+        tiny_out = held.tile([P, 1], F32, name="tiny_out")
+        nc.scalar.activation(tiny_out[:], tiny[:], ACT.Exp)
+
+        vs_pool = held.tile([P, T], F32, name="vs_pool")
+        sink_row = held.tile([P, P], F32, name="sink_row")
+        nc.vector.memset(sink_row[:], 0.0)
+        nc.vector.memset(vs_pool[:], 0.0)
+        ident = held.tile([P, P], F32, name="ident")
+        make_identity(nc, ident[:])
+        ident_bf = held.tile([P, P], BF16, name="ident_bf")
+        make_identity(nc, ident_bf[:])
+
+        k_rows = kT.rearrange("(p j) t -> p j t", j=PACK)
+        k_pool = [held.tile([P, T], F32, name=f"k_pool{j}") for j in range(PACK)]
+        v_pool = [
+            shared0.tile([P, T], F32, align_bytes=64, offset=0, name="v_pool0"),
+            shared1.tile([P, T], F32, align_bytes=64, offset=0, name="v_pool1"),
+        ]
+        q_raw = held.tile([P, PACK, NQ], F32, name="q_raw")
+
+        nc.sync.dma_start(k_pool[0][:], k_rows[:, 0, :])
+        nc.sync.dma_start(k_pool[1][:], k_rows[:, 1, :])
+        nc.sync.dma_start(sink_row[0:1, :], sink[0].rearrange("q o -> o q"))
+        nc.sync.dma_start(vs_pool[0:1, :], vs[0:1, :])
+        nc.sync.dma_start(k_pool[2][:], k_rows[:, 2, :])
+        nc.sync.dma_start(k_pool[3][:], k_rows[:, 3, :])
+        nc.sync.dma_start(q_raw[:], qT[0].rearrange("(p j) w -> p j w", j=PACK))
+        nc.sync.dma_start(v_pool[0][:], vT[0 * P : 1 * P, :])
+        nc.sync.dma_start(v_pool[1][:], vT[1 * P : 2 * P, :])
+
+        q_grouped = held.tile([P, NQ, PACK], BF16, align_bytes=64, name="q_grouped")
+        q_codes = held.tile([P, NQ], U32, align_bytes=64, name="q_codes")
+        q_scales = held.tile([P, NQ], U8, align_bytes=64, name="q_scales")
+        neg_sink = held.tile([P, 1], F32, name="neg_sink")
+        sink_col = held.tile([P, 1], F32, name="sink_col")
+        vs_picked = held.tile([P, N], F32, name="vs_picked")
+        vs_cols = held.tile([P, PASSES, PACK], F32, name="vs_cols")
+        k_grouped = held.tile([P, N, PACK], BF16, align_bytes=64, name="k_grouped")
+        k_codes = [held.tile([P, b - a], U32, align_bytes=64, name=f"k_codes{i}") for i, (a, b) in enumerate(PIECES)]
+        k_scales = [held.tile([P, b - a], U8, align_bytes=64, name=f"k_scales{i}") for i, (a, b) in enumerate(PIECES)]
+        score = [sums_pool.tile([NQ, b - a], F32, name=f"score{i}") for i, (a, b) in enumerate(PIECES)]
+        capped = held.tile([NQ, N], F32, name="capped")
+        neg_max = [held.tile([NQ, 1], F32, name=f"neg_max{i}") for i in range(len(PIECES))]
+        p = held.tile([NQ, PASSES, PACK, P], F32, name="p")
+        terms = held.tile([NQ, PASSES + 1], F32, name="terms")
+        w_codes = [held.tile([P, NQ], U32, align_bytes=64, name=f"w_codes{g}") for g in range(PASSES)]
+        w_scales = [held.tile([P, NQ], U8, align_bytes=64, name=f"w_scales{g}") for g in range(PASSES)]
+        recip = held.tile([NQ, 1], F32, name="recip")
+        v0_picked = held.tile([P, N], F32, name="v0_picked")
+        v1_picked = held.tile([P, PASSES, PACK, P], BF16, name="v1_picked")
+        v_grouped = [held.tile([P, PASSES, P, PACK], BF16, align_bytes=64, name=f"v_grouped{b}") for b in range(2)]
+        v_scales = [held.tile([P, PASSES * P], U8, align_bytes=64, name=f"v_scales{b}") for b in range(2)]
+
+        def queries():
+            nc.scalar.copy(q_grouped[:], q_raw[:].rearrange("p j w -> p w j"))
+            nc.vector.quantize_mx(
+                out=q_codes[:].bitcast(FP8X4), scales=q_scales[:], in_=q_grouped[:].rearrange("p w j -> p (w j)")
+            )
+
+        def sinks():
+            sink_turned = turned_pool.tile([P, PACK, P], F32, tag="turned", name="sink_turned")
+            nc.tensor.transpose(sink_turned[:, 0, :], sink_row[:], ident[:])
+            nc.vector.tensor_scalar(neg_sink[:], sink_turned[:, 0, 0:1], -1.0, None, ALU.mult)
+            nc.vector.tensor_scalar(sink_col[:], neg_sink[:], -1.0, None, ALU.mult)
+
+        def token_scales():
+            nc.vector.tensor_copy(vs_picked[:], listed(vs_pool, 0, N))
+            for g in range(PASSES):
+                vs_turned = turned_pool.tile([P, PACK, P], F32, tag="turned", name="vs_turned")
+                for t in range(PACK):
+                    nc.tensor.transpose(
+                        vs_turned[:, t, :], vs_picked[:, g * PASS + t : (g + 1) * PASS : PACK], ident[:]
+                    )
+                nc.scalar.copy(vs_cols[:, g, :], vs_turned[:, :, 0])
+
+        def keys(j, start=0, stop=N):
+            nc.vector.tensor_copy(k_grouped[:, start:stop, j], listed(k_pool[j], start, stop))
+
+        def scores(i):
+            start, stop = PIECES[i]
+            nc.vector.quantize_mx(
+                out=k_codes[i][:].bitcast(FP8X4),
+                scales=k_scales[i][:],
+                in_=k_grouped[:, start:stop, :].rearrange("p s j -> p (s j)"),
+            )
+            nc.tensor.matmul_mx(
+                out=score[i][:],
+                lhsT=q_codes[:].bitcast(FP8X4),
+                lhsT_scale=q_scales[:],
+                rhs=k_codes[i][:].bitcast(FP8X4),
+                rhs_scale=k_scales[i][:],
+                start=True,
+                stop=True,
+            )
+            nc.scalar.activation(capped[:, start:stop], score[i][:], ACT.Tanh, scale=0.5)
+
+        def maxima(i):
+            start, stop = PIECES[i]
+            before = neg_sink if i == 0 else neg_max[i - 1]
+            nc.vector.tensor_scalar(
+                minus_capped[:, start:stop],
+                capped[:, start:stop],
+                -2.0,
+                before[:],
+                ALU.mult,
+                ALU.min,
+                accum_out=neg_max[i][:],
+            )
+
+        def exps(g):
+            nc.scalar.activation(
+                p[:, g].rearrange("q t s -> q s t"),
+                capped[:, g * PASS : (g + 1) * PASS].rearrange("q (s t) -> q s t", t=PACK),
+                ACT.Exp,
+                bias=neg_max[-1][:],
+                scale=2.0,
+                accum_out=terms[:, g : g + 1],
+            )
+
+        def weights(g):
+            p_turned = turned_pool.tile([P, PACK, P], F32, tag="turned", name="p_turned")
+            for t in range(PACK):
+                nc.tensor.transpose(p_turned[:, t, :], p[:, g, t, :], ident[:])
+            w_grouped = shared1.tile([P, NQ, PACK], BF16, align_bytes=64, offset=g * NQ * PACK * 2, name=f"w_grouped{g}")
+            nc.vector.tensor_tensor(
+                w_grouped[:],
+                p_turned[:].rearrange("p j q -> p q j"),
+                vs_cols[:, g, :].unsqueeze(1).to_broadcast([P, NQ, PACK]),
+                ALU.mult,
+            )
+            return w_grouped
+
+        def weight_codes(g, w_grouped):
+            nc.vector.quantize_mx(
+                out=w_codes[g][:].bitcast(FP8X4),
+                scales=w_scales[g][:],
+                in_=w_grouped[:].rearrange("p q j -> p (q j)"),
+            )
+
+        def totals():
+            nc.scalar.activation(terms[:, PASSES : PASSES + 1], sink_col[:], ACT.Exp, bias=neg_max[-1][:])
+            nc.vector.reduce_sum(total[:], terms[:], mybir.AxisListType.X)
+            nc.vector.reciprocal(recip[:], total[:])
+
+        def values(b, g):
+            picked = v1_picked[:, g].rearrange("p t s -> p s t") if b else v0_picked[:, g * PASS : (g + 1) * PASS]
+            nc.vector.tensor_copy(picked, listed(v_pool[b], g * PASS, (g + 1) * PASS))
+
+        def turn_values(b, g):
+            v_turned = turned_pool.tile([P, PACK, P], BF16 if b else F32, tag="turned", name="v_turned")
+            for t in range(PACK):
+                if b:
+                    nc.tensor.transpose(v_turned[:, t, :], v1_picked[:, g, t, :], ident_bf[:])
+                else:
+                    nc.tensor.transpose(v_turned[:, t, :], v0_picked[:, g * PASS + t : (g + 1) * PASS : PACK], ident[:])
+            nc.scalar.copy(v_grouped[b][:, g], v_turned[:].rearrange("p j e -> p e j"))
+
+        def value_codes(b, v_codes, first, last):
+            nc.vector.quantize_mx(
+                out=v_codes[:, first * P : last * P].bitcast(FP8X4),
+                scales=v_scales[b][:, first * P : last * P],
+                in_=v_grouped[b][:, first:last].rearrange("p g e j -> p (g e j)"),
+            )
+
+        def products(b, v_codes):
+            y = sums_pool.tile([NQ, P], F32, name=f"y{b}")
+            for g in range(PASSES):
+                nc.tensor.matmul_mx(
+                    out=y[:],
+                    lhsT=w_codes[g][:].bitcast(FP8X4),
+                    lhsT_scale=w_scales[g][:],
+                    rhs=v_codes[:, g * P : (g + 1) * P].bitcast(FP8X4),
+                    rhs_scale=v_scales[b][:, g * P : (g + 1) * P],
+                    start=(g == 0),
+                    stop=(g == PASSES - 1),
+                )
+            result(y, b * P, (b + 1) * P)
+
+        def result(y, first, last):
+            y_out = held.tile([NQ, last - first], F32, name=f"y_out{first}")
+            nc.scalar.activation(y_out[:], y[:], ACT.Copy, scale=recip[:])
+            nc.sync.dma_start(out[0, :, first:last], y_out[:])
+
+        keys(0)
+        queries()
+        keys(1)
+        sinks()
+        token_scales()
+        keys(2)
+        keys(3, 0, 512)
+        scores(0)
+        keys(3, 512, 1024)
+        scores(1)
+        values(0, 0)
+        values(0, 1)
+        minus_capped = shared0.tile([NQ, N], F32, align_bytes=64, offset=0, name="minus_capped")
+        maxima(0)
+        maxima(1)
+        exps(0)
+        exps(1)
+        values(1, 0)
+        values(1, 1)
+        w0 = weights(0)
+        w1 = weights(1)
+        turn_values(0, 0)
+        turn_values(0, 1)
+        turn_values(1, 0)
+        turn_values(1, 1)
+        weight_codes(0, w0)
+        weight_codes(1, w1)
+        total = shared1.tile([NQ, 1], F32, align_bytes=64, offset=2 * NQ * PACK * 2, name="total")
+        totals()
+        v_codes0 = held.tile([P, PASSES * P], U32, align_bytes=64, name="v_codes0")
+        value_codes(0, v_codes0, 0, 2)
+        v_codes1 = held.tile([P, PASSES * P], U32, align_bytes=64, name="v_codes1")
+        value_codes(1, v_codes1, 0, 1)
+        value_codes(1, v_codes1, 1, 2)
+        products(0, v_codes0)
+        products(1, v_codes1)

@@ -7,6 +7,8 @@ PACK = 4
 PASS = P * PACK
 PASSES = N // PASS
 LIST_ROWS = 16
+PIECE = 256
+PIECES = N // PIECE
 
 FLOPS = 2 * NQ * N * (D + DV)
 BYTES = 4 * (D * T + DV * T + D * NQ + T + NQ + NQ * DV) + 2 * P * (N // 16)
@@ -19,20 +21,28 @@ U8 = mybir.dt.uint8
 FP8X4 = mybir.dt.float8_e4m3fn_x4
 ACT = mybir.ActivationFunctionType
 ALU = mybir.AluOpType
-PIECES = ((0, 512), (512, 1024))
 
 
 def tile_attend_x_cap_sink_kernel(tc, qT, kT, vT, vs, sink, offs, out):
     nc = tc.nc
     with (
         tc.tile_pool(name="held", bufs=1) as held,
-        tc.tile_pool(name="shared0", bufs=1) as shared0,
-        tc.tile_pool(name="shared1", bufs=1) as shared1,
-        tc.psum_pool(name="turned", bufs=4) as turned_pool,
-        tc.psum_pool(name="sums", bufs=1) as sums_pool,
+        tc.tile_pool(name="after_q", bufs=1) as after_q,
+        tc.tile_pool(name="after_exp", bufs=1) as after_exp,
+        tc.tile_pool(name="after_v0", bufs=1) as after_v0,
+        tc.tile_pool(name="after_v1", bufs=1) as after_v1,
+        tc.psum_pool(name="banks", bufs=1) as banks,
     ):
         offsets = held.tile([P, N // LIST_ROWS], U16, name="offsets")
-        nc.sync.dma_start(offsets[:], offs)
+        k_rows = kT.rearrange("(p j) t -> p j t", j=PACK)
+        k_pool = [held.tile([P, T], F32, name=f"k_pool{j}") for j in range(PACK)]
+        v_pool = [
+            after_v0.tile([P, T], F32, align_bytes=64, offset=0, name="v_pool0"),
+            after_v1.tile([P, T], F32, align_bytes=64, offset=0, name="v_pool1"),
+        ]
+        q_raw = after_q.tile([P, PACK, NQ], F32, align_bytes=64, offset=0, name="q_raw")
+        vs_pool = held.tile([P, T], F32, name="vs_pool")
+        sink_col = held.tile([P, 1], F32, name="sink_col")
 
         def listed(window, start, stop):
             return window[:].indirect(offsets[:, start // LIST_ROWS : stop // LIST_ROWS])
@@ -41,27 +51,14 @@ def tile_attend_x_cap_sink_kernel(tc, qT, kT, vT, vs, sink, offs, out):
         nc.vector.memset(tiny[:], 0.0)
         tiny_out = held.tile([P, 1], F32, name="tiny_out")
         nc.scalar.activation(tiny_out[:], tiny[:], ACT.Exp)
-
-        vs_pool = held.tile([P, T], F32, name="vs_pool")
-        sink_row = held.tile([P, P], F32, name="sink_row")
-        nc.vector.memset(sink_row[:], 0.0)
         nc.vector.memset(vs_pool[:], 0.0)
         ident = held.tile([P, P], F32, name="ident")
         make_identity(nc, ident[:])
-        ident_bf = held.tile([P, P], BF16, name="ident_bf")
-        make_identity(nc, ident_bf[:])
-
-        k_rows = kT.rearrange("(p j) t -> p j t", j=PACK)
-        k_pool = [held.tile([P, T], F32, name=f"k_pool{j}") for j in range(PACK)]
-        v_pool = [
-            shared0.tile([P, T], F32, align_bytes=64, offset=0, name="v_pool0"),
-            shared1.tile([P, T], F32, align_bytes=64, offset=0, name="v_pool1"),
-        ]
-        q_raw = held.tile([P, PACK, NQ], F32, name="q_raw")
 
         nc.sync.dma_start(k_pool[0][:], k_rows[:, 0, :])
+        nc.sync.dma_start(offsets[:], offs)
         nc.sync.dma_start(k_pool[1][:], k_rows[:, 1, :])
-        nc.sync.dma_start(sink_row[0:1, :], sink[0].rearrange("q o -> o q"))
+        nc.sync.dma_start(sink_col[:], sink[0])
         nc.sync.dma_start(vs_pool[0:1, :], vs[0:1, :])
         nc.sync.dma_start(k_pool[2][:], k_rows[:, 2, :])
         nc.sync.dma_start(k_pool[3][:], k_rows[:, 3, :])
@@ -72,25 +69,33 @@ def tile_attend_x_cap_sink_kernel(tc, qT, kT, vT, vs, sink, offs, out):
         q_grouped = held.tile([P, NQ, PACK], BF16, align_bytes=64, name="q_grouped")
         q_codes = held.tile([P, NQ], U32, align_bytes=64, name="q_codes")
         q_scales = held.tile([P, NQ], U8, align_bytes=64, name="q_scales")
-        neg_sink = held.tile([P, 1], F32, name="neg_sink")
-        sink_col = held.tile([P, 1], F32, name="sink_col")
         vs_picked = held.tile([P, N], F32, name="vs_picked")
         vs_cols = held.tile([P, PASSES, PACK], F32, name="vs_cols")
         k_grouped = held.tile([P, N, PACK], BF16, align_bytes=64, name="k_grouped")
-        k_codes = [held.tile([P, b - a], U32, align_bytes=64, name=f"k_codes{i}") for i, (a, b) in enumerate(PIECES)]
-        k_scales = [held.tile([P, b - a], U8, align_bytes=64, name=f"k_scales{i}") for i, (a, b) in enumerate(PIECES)]
-        score = [sums_pool.tile([NQ, b - a], F32, name=f"score{i}") for i, (a, b) in enumerate(PIECES)]
-        capped = held.tile([NQ, N], F32, name="capped")
-        neg_max = [held.tile([NQ, 1], F32, name=f"neg_max{i}") for i in range(len(PIECES))]
-        p = held.tile([NQ, PASSES, PACK, P], F32, name="p")
-        terms = held.tile([NQ, PASSES + 1], F32, name="terms")
-        w_codes = [held.tile([P, NQ], U32, align_bytes=64, name=f"w_codes{g}") for g in range(PASSES)]
-        w_scales = [held.tile([P, NQ], U8, align_bytes=64, name=f"w_scales{g}") for g in range(PASSES)]
-        recip = held.tile([NQ, 1], F32, name="recip")
-        v0_picked = held.tile([P, N], F32, name="v0_picked")
-        v1_picked = held.tile([P, PASSES, PACK, P], BF16, name="v1_picked")
-        v_grouped = [held.tile([P, PASSES, P, PACK], BF16, align_bytes=64, name=f"v_grouped{b}") for b in range(2)]
-        v_scales = [held.tile([P, PASSES * P], U8, align_bytes=64, name=f"v_scales{b}") for b in range(2)]
+        k_codes = [held.tile([P, PIECE], U32, align_bytes=64, name=f"k_codes{i}") for i in range(PIECES)]
+        k_scales = [
+            after_q.tile([P, PIECE], U8, align_bytes=64, offset=i * PIECE, name=f"k_scales{i}") for i in range(PIECES)
+        ]
+        capped = [
+            held.tile([NQ, PASS], F32, name="capped0"),
+            after_exp.tile([NQ, PASS + 1], F32, align_bytes=64, offset=0, name="capped1"),
+        ]
+        doubled = held.tile([NQ, N + 1], F32, name="doubled")
+        neg_max = [held.tile([NQ, 1], F32, name=f"neg_max{g}") for g in range(PASSES)]
+        p = held.tile([NQ, N + 1], F32, name="p")
+        terms = held.tile([NQ, PASSES], F32, name="terms")
+        total = held.tile([NQ, 1], F32, name="total")
+        w_scales = held.tile([P, PASSES * NQ], U8, align_bytes=64, name="w_scales")
+        v_picked = [
+            [held.tile([P, 2, P, 2], BF16, name=f"v_picked{b}{g}") for g in range(PASSES)] for b in range(2)
+        ]
+        v0_scales = held.tile([P, PASSES * P], U8, align_bytes=64, name="v0_scales")
+        v1_grouped = [held.tile([P, P * PACK], BF16, align_bytes=64, name=f"v1_grouped{g}") for g in range(PASSES)]
+        v1_codes = [held.tile([P, P], U32, align_bytes=64, name=f"v1_codes{g}") for g in range(PASSES)]
+        v1_scales = [held.tile([P, P], U8, align_bytes=64, name=f"v1_scales{g}") for g in range(PASSES)]
+
+        def span(g):
+            return slice(g * PASS, (g + 1) * PASS + (1 if g == PASSES - 1 else 0))
 
         def queries():
             nc.scalar.copy(q_grouped[:], q_raw[:].rearrange("p j w -> p w j"))
@@ -99,15 +104,12 @@ def tile_attend_x_cap_sink_kernel(tc, qT, kT, vT, vs, sink, offs, out):
             )
 
         def sinks():
-            sink_turned = turned_pool.tile([P, PACK, P], F32, tag="turned", name="sink_turned")
-            nc.tensor.transpose(sink_turned[:, 0, :], sink_row[:], ident[:])
-            nc.vector.tensor_scalar(neg_sink[:], sink_turned[:, 0, 0:1], -1.0, None, ALU.mult)
-            nc.vector.tensor_scalar(sink_col[:], neg_sink[:], -1.0, None, ALU.mult)
+            nc.scalar.activation(capped[1][:, PASS : PASS + 1], sink_col[:], ACT.Copy, scale=0.5)
 
         def token_scales():
             nc.vector.tensor_copy(vs_picked[:], listed(vs_pool, 0, N))
             for g in range(PASSES):
-                vs_turned = turned_pool.tile([P, PACK, P], F32, tag="turned", name="vs_turned")
+                vs_turned = banks.tile([P, PACK, P], F32, tag=f"bank{2 + g}", name="vs_turned")
                 for t in range(PACK):
                     nc.tensor.transpose(
                         vs_turned[:, t, :], vs_picked[:, g * PASS + t : (g + 1) * PASS : PACK], ident[:]
@@ -118,14 +120,14 @@ def tile_attend_x_cap_sink_kernel(tc, qT, kT, vT, vs, sink, offs, out):
             nc.vector.tensor_copy(k_grouped[:, start:stop, j], listed(k_pool[j], start, stop))
 
         def scores(i):
-            start, stop = PIECES[i]
             nc.vector.quantize_mx(
                 out=k_codes[i][:].bitcast(FP8X4),
                 scales=k_scales[i][:],
-                in_=k_grouped[:, start:stop, :].rearrange("p s j -> p (s j)"),
+                in_=k_grouped[:, i * PIECE : (i + 1) * PIECE, :].rearrange("p s j -> p (s j)"),
             )
+            score = banks.tile([NQ, PIECE], F32, tag=f"bank{(0, 1, 4, 5)[i]}", name="score")
             nc.tensor.matmul_mx(
-                out=score[i][:],
+                out=score[:],
                 lhsT=q_codes[:].bitcast(FP8X4),
                 lhsT_scale=q_scales[:],
                 rhs=k_codes[i][:].bitcast(FP8X4),
@@ -133,128 +135,106 @@ def tile_attend_x_cap_sink_kernel(tc, qT, kT, vT, vs, sink, offs, out):
                 start=True,
                 stop=True,
             )
-            nc.scalar.activation(capped[:, start:stop], score[i][:], ACT.Tanh, scale=0.5)
+            g, h = divmod(i, PASS // PIECE)
+            dealt = capped[g][:, 0:PASS].rearrange("q (t s) -> q t s", t=PACK)
+            run = PIECE // PACK
+            nc.scalar.activation(
+                dealt[:, :, h * run : (h + 1) * run],
+                score[:].rearrange("q (s t) -> q t s", t=PACK),
+                ACT.Tanh,
+                scale=0.5,
+            )
 
-        def maxima(i):
-            start, stop = PIECES[i]
-            before = neg_sink if i == 0 else neg_max[i - 1]
+        def maxima(g):
+            before = neg_max[g - 1][:] if g else None
             nc.vector.tensor_scalar(
-                minus_capped[:, start:stop],
-                capped[:, start:stop],
-                -2.0,
-                before[:],
-                ALU.mult,
-                ALU.min,
-                accum_out=neg_max[i][:],
+                doubled[:, span(g)], capped[g][:], -2.0, before, ALU.mult, ALU.min, accum_out=neg_max[g][:]
             )
 
         def exps(g):
             nc.scalar.activation(
-                p[:, g].rearrange("q t s -> q s t"),
-                capped[:, g * PASS : (g + 1) * PASS].rearrange("q (s t) -> q s t", t=PACK),
-                ACT.Exp,
-                bias=neg_max[-1][:],
-                scale=2.0,
-                accum_out=terms[:, g : g + 1],
+                p[:, span(g)], capped[g][:], ACT.Exp, bias=neg_max[-1][:], scale=2.0, accum_out=terms[:, g : g + 1]
             )
 
         def weights(g):
-            p_turned = turned_pool.tile([P, PACK, P], F32, tag="turned", name="p_turned")
+            p_turned = banks.tile([P, PACK, P], F32, tag=f"bank{2 + g}", name="p_turned")
             for t in range(PACK):
-                nc.tensor.transpose(p_turned[:, t, :], p[:, g, t, :], ident[:])
-            w_grouped = shared1.tile([P, NQ, PACK], BF16, align_bytes=64, offset=g * NQ * PACK * 2, name=f"w_grouped{g}")
+                nc.tensor.transpose(p_turned[:, t, :], p[:, g * PASS + t * P : g * PASS + (t + 1) * P], ident[:])
             nc.vector.tensor_tensor(
-                w_grouped[:],
+                w_grouped[:, g],
                 p_turned[:].rearrange("p j q -> p q j"),
                 vs_cols[:, g, :].unsqueeze(1).to_broadcast([P, NQ, PACK]),
                 ALU.mult,
             )
-            return w_grouped
-
-        def weight_codes(g, w_grouped):
-            nc.vector.quantize_mx(
-                out=w_codes[g][:].bitcast(FP8X4),
-                scales=w_scales[g][:],
-                in_=w_grouped[:].rearrange("p q j -> p (q j)"),
-            )
-
-        def totals():
-            nc.scalar.activation(terms[:, PASSES : PASSES + 1], sink_col[:], ACT.Exp, bias=neg_max[-1][:])
-            nc.vector.reduce_sum(total[:], terms[:], mybir.AxisListType.X)
-            nc.vector.reciprocal(recip[:], total[:])
 
         def values(b, g):
-            picked = v1_picked[:, g].rearrange("p t s -> p s t") if b else v0_picked[:, g * PASS : (g + 1) * PASS]
-            nc.vector.tensor_copy(picked, listed(v_pool[b], g * PASS, (g + 1) * PASS))
-
-        def turn_values(b, g):
-            v_turned = turned_pool.tile([P, PACK, P], BF16 if b else F32, tag="turned", name="v_turned")
-            for t in range(PACK):
-                if b:
-                    nc.tensor.transpose(v_turned[:, t, :], v1_picked[:, g, t, :], ident_bf[:])
-                else:
-                    nc.tensor.transpose(v_turned[:, t, :], v0_picked[:, g * PASS + t : (g + 1) * PASS : PACK], ident[:])
-            nc.scalar.copy(v_grouped[b][:, g], v_turned[:].rearrange("p j e -> p e j"))
-
-        def value_codes(b, v_codes, first, last):
-            nc.vector.quantize_mx(
-                out=v_codes[:, first * P : last * P].bitcast(FP8X4),
-                scales=v_scales[b][:, first * P : last * P],
-                in_=v_grouped[b][:, first:last].rearrange("p g e j -> p (g e j)"),
+            nc.vector.tensor_copy(
+                v_picked[b][g][:].rearrange("e u p i -> e p u i"), listed(v_pool[b], g * PASS, (g + 1) * PASS)
             )
 
-        def products(b, v_codes):
-            y = sums_pool.tile([NQ, P], F32, name=f"y{b}")
+        def turn_values(b, g, grouped, bank):
+            v_turned = banks.tile([P, 2, P], F32, tag=bank, name="v_turned")
+            for u in range(2):
+                nc.tensor.transpose(
+                    v_turned[:, u, :], v_picked[b][g][:, u].rearrange("e p i -> e (p i)").bitcast(F32), ident[:]
+                )
+            nc.scalar.copy(
+                grouped.bitcast(F32).rearrange("p (e u) -> p e u", u=2), v_turned[:].rearrange("p u e -> p e u")
+            )
+
+        def products(b, w_codes, codes, scales, bank):
+            y = banks.tile([NQ, P], F32, tag=bank, name="y")
             for g in range(PASSES):
                 nc.tensor.matmul_mx(
                     out=y[:],
-                    lhsT=w_codes[g][:].bitcast(FP8X4),
-                    lhsT_scale=w_scales[g][:],
-                    rhs=v_codes[:, g * P : (g + 1) * P].bitcast(FP8X4),
-                    rhs_scale=v_scales[b][:, g * P : (g + 1) * P],
+                    lhsT=w_codes[:, g * NQ : (g + 1) * NQ].bitcast(FP8X4),
+                    lhsT_scale=w_scales[:, g * NQ : (g + 1) * NQ],
+                    rhs=codes[g].bitcast(FP8X4),
+                    rhs_scale=scales[g],
                     start=(g == 0),
                     stop=(g == PASSES - 1),
                 )
-            result(y, b * P, (b + 1) * P)
-
-        def result(y, first, last):
-            y_out = held.tile([NQ, last - first], F32, name=f"y_out{first}")
+            y_out = held.tile([NQ, P], F32, name=f"y_out{b}")
             nc.scalar.activation(y_out[:], y[:], ACT.Copy, scale=recip[:])
-            nc.sync.dma_start(out[0, :, first:last], y_out[:])
+            nc.sync.dma_start(out[0, :, b * P : (b + 1) * P], y_out[:])
 
         keys(0)
-        queries()
         keys(1)
-        sinks()
         token_scales()
         keys(2)
-        keys(3, 0, 512)
-        scores(0)
-        keys(3, 512, 1024)
-        scores(1)
-        values(0, 0)
-        values(0, 1)
-        minus_capped = shared0.tile([NQ, N], F32, align_bytes=64, offset=0, name="minus_capped")
+        keys(3, 0, PASS)
+        keys(3, PASS, N)
+        queries()
+        sinks()
+        for i in range(PIECES):
+            scores(i)
         maxima(0)
         maxima(1)
+        values(0, 0)
+        values(0, 1)
         exps(0)
         exps(1)
+        w_grouped = after_v0.tile([P, PASSES, NQ, PACK], BF16, align_bytes=64, offset=0, name="w_grouped")
+        weights(0)
+        weights(1)
+        nc.scalar.activation(total[:], terms[:, 0:1], ACT.Identity, bias=terms[:, 1:2])
+        v0_grouped = after_exp.tile([P, PASSES * PASS], BF16, align_bytes=64, offset=0, name="v0_grouped")
+        turn_values(0, 0, v0_grouped[:, 0:PASS], "bank6")
+        turn_values(0, 1, v0_grouped[:, PASS:N], "bank2")
         values(1, 0)
         values(1, 1)
-        w0 = weights(0)
-        w1 = weights(1)
-        turn_values(0, 0)
-        turn_values(0, 1)
-        turn_values(1, 0)
-        turn_values(1, 1)
-        weight_codes(0, w0)
-        weight_codes(1, w1)
-        total = shared1.tile([NQ, 1], F32, align_bytes=64, offset=2 * NQ * PACK * 2, name="total")
-        totals()
-        v_codes0 = held.tile([P, PASSES * P], U32, align_bytes=64, name="v_codes0")
-        value_codes(0, v_codes0, 0, 2)
-        v_codes1 = held.tile([P, PASSES * P], U32, align_bytes=64, name="v_codes1")
-        value_codes(1, v_codes1, 0, 1)
-        value_codes(1, v_codes1, 1, 2)
-        products(0, v_codes0)
-        products(1, v_codes1)
+        turn_values(1, 0, v1_grouped[0][:], "bank7")
+        turn_values(1, 1, v1_grouped[1][:], "bank4")
+        w_codes = after_v1.tile([P, PASSES * NQ], U32, align_bytes=64, offset=0, name="w_codes")
+        nc.vector.quantize_mx(
+            out=w_codes[:].bitcast(FP8X4), scales=w_scales[:], in_=w_grouped[:].rearrange("p g q j -> p (g q j)")
+        )
+        v0_codes = after_v1.tile([P, PASSES * P], U32, align_bytes=64, offset=1024, name="v0_codes")
+        nc.vector.quantize_mx(out=v0_codes[:].bitcast(FP8X4), scales=v0_scales[:], in_=v0_grouped[:])
+        recip = after_v1.tile([NQ, 1], F32, align_bytes=64, offset=2048, name="recip")
+        nc.vector.reciprocal(recip[:], total[:])
+        for g in range(PASSES):
+            nc.vector.quantize_mx(out=v1_codes[g][:].bitcast(FP8X4), scales=v1_scales[g][:], in_=v1_grouped[g][:])
+        halves = [slice(g * P, (g + 1) * P) for g in range(PASSES)]
+        products(0, w_codes, [v0_codes[:, h] for h in halves], [v0_scales[:, h] for h in halves], "bank0")
+        products(1, w_codes, [c[:] for c in v1_codes], [s[:] for s in v1_scales], "bank1")

@@ -71,7 +71,8 @@ def tile_attend_x_cap_sink_kernel(tc, qT, kT, vT, vs, sink, offs, out):
         q_scales = held.tile([P, NQ], U8, align_bytes=64, name="q_scales")
         vs_picked = held.tile([P, N], F32, name="vs_picked")
         vs_cols = held.tile([P, PASSES, PACK], F32, name="vs_cols")
-        k_grouped = held.tile([P, N, PACK], BF16, align_bytes=64, name="k_grouped")
+        k_picked = [held.tile([P, PACK, PASS], BF16, name=f"k_picked{g}") for g in range(PASSES)]
+        k_grouped = [held.tile([P, PIECE, PACK], BF16, align_bytes=64, name=f"k_grouped{i}") for i in range(PIECES)]
         k_codes = [held.tile([P, PIECE], U32, align_bytes=64, name=f"k_codes{i}") for i in range(PIECES)]
         k_scales = [
             after_q.tile([P, PIECE], U8, align_bytes=64, offset=i * PIECE, name=f"k_scales{i}") for i in range(PIECES)
@@ -98,7 +99,7 @@ def tile_attend_x_cap_sink_kernel(tc, qT, kT, vT, vs, sink, offs, out):
             return slice(g * PASS, (g + 1) * PASS + (1 if g == PASSES - 1 else 0))
 
         def queries():
-            nc.scalar.copy(q_grouped[:], q_raw[:].rearrange("p j w -> p w j"))
+            nc.gpsimd.tensor_scalar(q_grouped[:], q_raw[:].rearrange("p j w -> p w j"), 1.0, 0.0, ALU.mult, ALU.add)
             nc.vector.quantize_mx(
                 out=q_codes[:].bitcast(FP8X4), scales=q_scales[:], in_=q_grouped[:].rearrange("p w j -> p (w j)")
             )
@@ -116,14 +117,23 @@ def tile_attend_x_cap_sink_kernel(tc, qT, kT, vT, vs, sink, offs, out):
                     )
                 nc.scalar.copy(vs_cols[:, g, :], vs_turned[:, :, 0])
 
-        def keys(j, start=0, stop=N):
-            nc.vector.tensor_copy(k_grouped[:, start:stop, j], listed(k_pool[j], start, stop))
+        def keys(j):
+            for g in range(PASSES):
+                nc.vector.tensor_copy(k_picked[g][:, j, :], listed(k_pool[j], g * PASS, (g + 1) * PASS))
+
+        def weave(i):
+            g, h = divmod(i, PASS // PIECE)
+            planes = k_picked[g][:, :, h * PIECE : (h + 1) * PIECE].rearrange("p j s -> p s j")
+            if h == 0:
+                nc.scalar.copy(k_grouped[i][:], planes)
+            else:
+                nc.vector.tensor_copy(k_grouped[i][:], planes)
 
         def scores(i):
             nc.vector.quantize_mx(
                 out=k_codes[i][:].bitcast(FP8X4),
                 scales=k_scales[i][:],
-                in_=k_grouped[:, i * PIECE : (i + 1) * PIECE, :].rearrange("p s j -> p (s j)"),
+                in_=k_grouped[i][:].rearrange("p s j -> p (s j)"),
             )
             score = banks.tile([NQ, PIECE], F32, tag=f"bank{(0, 1, 4, 5)[i]}", name="score")
             nc.tensor.matmul_mx(
@@ -202,11 +212,12 @@ def tile_attend_x_cap_sink_kernel(tc, qT, kT, vT, vs, sink, offs, out):
         keys(1)
         token_scales()
         keys(2)
-        keys(3, 0, PASS)
-        keys(3, PASS, N)
-        queries()
         sinks()
+        keys(3)
         for i in range(PIECES):
+            weave(i)
+        queries()
+        for i in (0, 1, 3, 2):
             scores(i)
         maxima(0)
         maxima(1)

@@ -123,11 +123,12 @@ def tile_attend_x_cap_sink_kernel(tc, qT, kT, vT, vs, sink, offs, out):
 
         def weave(i):
             g, h = divmod(i, PASS // PIECE)
-            planes = k_picked[g][:, :, h * PIECE : (h + 1) * PIECE].rearrange("p j s -> p s j")
+            planes = k_picked[g][:, :, h * PIECE : (h + 1) * PIECE].rearrange("p j (c i) -> p c j i", i=PACK)
+            woven = k_grouped[i][:].rearrange("p (c i) j -> p c j i", i=PACK)
             if h == 0:
-                nc.scalar.copy(k_grouped[i][:], planes)
+                nc.scalar.copy(woven, planes)
             else:
-                nc.vector.tensor_copy(k_grouped[i][:], planes)
+                nc.vector.tensor_copy(woven, planes)
 
         def scores(i):
             nc.vector.quantize_mx(
@@ -146,11 +147,11 @@ def tile_attend_x_cap_sink_kernel(tc, qT, kT, vT, vs, sink, offs, out):
                 stop=True,
             )
             g, h = divmod(i, PASS // PIECE)
-            dealt = capped[g][:, 0:PASS].rearrange("q (t s) -> q t s", t=PACK)
+            dealt = capped[g][:, 0:PASS].rearrange("q (t s) -> q s t", t=PACK)
             run = PIECE // PACK
             nc.scalar.activation(
-                dealt[:, :, h * run : (h + 1) * run],
-                score[:].rearrange("q (s t) -> q t s", t=PACK),
+                dealt[:, h * run : (h + 1) * run, :],
+                score[:].rearrange("q (s t) -> q s t", t=PACK),
                 ACT.Tanh,
                 scale=0.5,
             )
@@ -171,9 +172,9 @@ def tile_attend_x_cap_sink_kernel(tc, qT, kT, vT, vs, sink, offs, out):
             for t in range(PACK):
                 nc.tensor.transpose(p_turned[:, t, :], p[:, g * PASS + t * P : g * PASS + (t + 1) * P], ident[:])
             nc.vector.tensor_tensor(
-                w_grouped[:, g],
-                p_turned[:].rearrange("p j q -> p q j"),
-                vs_cols[:, g, :].unsqueeze(1).to_broadcast([P, NQ, PACK]),
+                w_grouped[:, g].rearrange("p (c i) j -> p c j i", i=PACK),
+                p_turned[:].rearrange("p j (c i) -> p c j i", i=PACK),
+                vs_cols[:, g, :].unsqueeze(1).unsqueeze(3).to_broadcast([P, NQ // PACK, PACK, PACK]),
                 ALU.mult,
             )
 

@@ -7,6 +7,8 @@ PACK = 4
 PASS = P * PACK
 PASSES = N // PASS
 LIST_ROWS = 16
+VS_ROWS = 4
+PORT_ROWS = 4
 PIECE = 256
 PIECES = N // PIECE
 
@@ -59,7 +61,9 @@ def tile_attend_x_cap_sink_kernel(tc, qT, kT, vT, vs, sink, offs, out):
         nc.sync.dma_start(offsets[:], offs)
         nc.sync.dma_start(k_pool[1][:], k_rows[:, 1, :])
         nc.sync.dma_start(sink_col[:], sink[0])
-        nc.sync.dma_start(vs_pool[0:1, :], vs[0:1, :])
+        for r in range(VS_ROWS):
+            part = slice(r * T // VS_ROWS, (r + 1) * T // VS_ROWS)
+            nc.sync.dma_start(vs_pool[PORT_ROWS * r : PORT_ROWS * r + 1, part], vs[r : r + 1, part])
         nc.sync.dma_start(k_pool[2][:], k_rows[:, 2, :])
         nc.sync.dma_start(k_pool[3][:], k_rows[:, 3, :])
         nc.sync.dma_start(q_raw[:], qT[0].rearrange("(p j) w -> p j w", j=PACK))
@@ -115,7 +119,9 @@ def tile_attend_x_cap_sink_kernel(tc, qT, kT, vT, vs, sink, offs, out):
                     nc.tensor.transpose(
                         vs_turned[:, t, :], vs_picked[:, g * PASS + t : (g + 1) * PASS : PACK], ident[:]
                     )
-                nc.scalar.copy(vs_cols[:, g, :], vs_turned[:, :, 0])
+                nc.vector.reduce_sum(
+                    vs_cols[:, g, :], vs_turned[:, :, 0 : VS_ROWS * PORT_ROWS : PORT_ROWS], mybir.AxisListType.X
+                )
 
         def keys(j):
             for g in range(PASSES):

@@ -30,6 +30,7 @@ def tile_attend_x_cap_sink_kernel(tc, qT, kT, vT, vs, sink, offs, out):
     with (
         tc.tile_pool(name="held", bufs=1) as held,
         tc.tile_pool(name="after_q", bufs=1) as after_q,
+        tc.tile_pool(name="after_max", bufs=1) as after_max,
         tc.tile_pool(name="after_exp", bufs=1) as after_exp,
         tc.tile_pool(name="after_v0", bufs=1) as after_v0,
         tc.tile_pool(name="after_v1", bufs=1) as after_v1,
@@ -74,42 +75,45 @@ def tile_attend_x_cap_sink_kernel(tc, qT, kT, vT, vs, sink, offs, out):
         q_codes = held.tile([P, NQ], U32, align_bytes=64, name="q_codes")
         q_scales = held.tile([P, NQ], U8, align_bytes=64, name="q_scales")
         vs_picked = held.tile([P, N], F32, name="vs_picked")
+        vs_parts = held.tile([P, PASSES, PACK, VS_ROWS], F32, name="vs_parts")
         vs_cols = held.tile([P, PASSES, PACK], F32, name="vs_cols")
-        k_picked = [held.tile([P, PACK, PASS], BF16, name=f"k_picked{g}") for g in range(PASSES)]
-        k_grouped = [held.tile([P, PIECE, PACK], BF16, align_bytes=64, name=f"k_grouped{i}") for i in range(PIECES)]
+        k_last = [held.tile([P, PASS], BF16, name=f"k_last{g}") for g in range(PASSES)]
+        k_grouped = [held.tile([P, PASS, PACK], BF16, align_bytes=64, name=f"k_grouped{g}") for g in range(PASSES)]
         k_codes = [held.tile([P, PIECE], U32, align_bytes=64, name=f"k_codes{i}") for i in range(PIECES)]
         k_scales = [
             after_q.tile([P, PIECE], U8, align_bytes=64, offset=i * PIECE, name=f"k_scales{i}") for i in range(PIECES)
         ]
         capped = [
-            held.tile([NQ, PASS], F32, name="capped0"),
-            after_exp.tile([NQ, PASS + 1], F32, align_bytes=64, offset=0, name="capped1"),
+            held.tile([NQ, PASS + 1], F32, name="capped0"),
+            after_exp.tile([NQ, PASS], F32, align_bytes=64, offset=0, name="capped1"),
         ]
-        doubled = held.tile([NQ, N + 1], F32, name="doubled")
-        neg_max = [held.tile([NQ, 1], F32, name=f"neg_max{g}") for g in range(PASSES)]
-        p = held.tile([NQ, N + 1], F32, name="p")
-        terms = held.tile([NQ, PASSES], F32, name="terms")
+        doubled = [
+            held.tile([NQ, PASS + 1], F32, name="doubled0"),
+            after_max.tile([NQ, PASS], F32, offset=0, name="doubled1"),
+        ]
+        neg_max = [held.tile([NQ, 1], F32, name=f"neg_max{i}") for i in range(PASSES)]
+        p = [held.tile([NQ, PIECE + (i == 1)], F32, name=f"p{i}") for i in range(PIECES)]
+        terms = held.tile([NQ, PIECES], F32, name="terms")
+        terms_out = held.tile([NQ, PIECES], F32, name="terms_out")
         total = held.tile([NQ, 1], F32, name="total")
         w_scales = held.tile([P, PASSES * NQ], U8, align_bytes=64, name="w_scales")
         v_picked = [
-            [held.tile([P, 2, P, 2], BF16, name=f"v_picked{b}{g}") for g in range(PASSES)] for b in range(2)
+            [after_max.tile([P, 2, P, 2], BF16, offset=1024 * g, name=f"v_picked0{g}") for g in range(PASSES)],
+            [held.tile([P, 2, P, 2], BF16, name=f"v_picked1{g}") for g in range(PASSES)],
         ]
         v0_scales = held.tile([P, PASSES * P], U8, align_bytes=64, name="v0_scales")
         v1_grouped = [held.tile([P, P * PACK], BF16, align_bytes=64, name=f"v1_grouped{g}") for g in range(PASSES)]
         v1_codes = [held.tile([P, P], U32, align_bytes=64, name=f"v1_codes{g}") for g in range(PASSES)]
         v1_scales = [held.tile([P, P], U8, align_bytes=64, name=f"v1_scales{g}") for g in range(PASSES)]
 
-        def span(g):
-            return slice(g * PASS, (g + 1) * PASS + (1 if g == PASSES - 1 else 0))
-
         def queries():
-            nc.gpsimd.tensor_scalar(q_grouped[:], q_raw[:].rearrange("p j w -> p w j"), 1.0, 0.0, ALU.mult, ALU.add)
+            nc.scalar.copy(q_grouped[:], q_raw[:].rearrange("p j w -> p w j"))
             nc.vector.quantize_mx(
                 out=q_codes[:].bitcast(FP8X4), scales=q_scales[:], in_=q_grouped[:].rearrange("p w j -> p (w j)")
             )
 
         def sinks():
-            nc.scalar.activation(capped[1][:, PASS : PASS + 1], sink_col[:], ACT.Copy, scale=0.5)
+            nc.scalar.activation(capped[0][:, PASS : PASS + 1], sink_col[:], ACT.Copy, scale=0.5)
 
         def token_scales():
             nc.vector.tensor_copy(vs_picked[:], listed(vs_pool, 0, N))
@@ -119,28 +123,33 @@ def tile_attend_x_cap_sink_kernel(tc, qT, kT, vT, vs, sink, offs, out):
                     nc.tensor.transpose(
                         vs_turned[:, t, :], vs_picked[:, g * PASS + t : (g + 1) * PASS : PACK], ident[:]
                     )
-                nc.vector.reduce_sum(
-                    vs_cols[:, g, :], vs_turned[:, :, 0 : VS_ROWS * PORT_ROWS : PORT_ROWS], mybir.AxisListType.X
-                )
+                for t in range(PACK):
+                    nc.scalar.activation(
+                        vs_parts[:, g, t, :],
+                        vs_turned[:, t, 0 : VS_ROWS * PORT_ROWS : PORT_ROWS],
+                        ACT.Copy,
+                        accum_out=vs_cols[:, g, t : t + 1],
+                    )
 
         def keys(j):
             for g in range(PASSES):
-                nc.vector.tensor_copy(k_picked[g][:, j, :], listed(k_pool[j], g * PASS, (g + 1) * PASS))
+                picked = k_last[g][:] if j == PACK - 1 else k_grouped[g][:, :, j]
+                nc.vector.tensor_copy(picked, listed(k_pool[j], g * PASS, (g + 1) * PASS))
 
-        def weave(i):
+        def place_last(i):
             g, h = divmod(i, PASS // PIECE)
-            planes = k_picked[g][:, :, h * PIECE : (h + 1) * PIECE].rearrange("p j (c i) -> p c j i", i=PACK)
-            woven = k_grouped[i][:].rearrange("p (c i) j -> p c j i", i=PACK)
-            if h == 0:
-                nc.scalar.copy(woven, planes)
+            cols = slice(h * PIECE, (h + 1) * PIECE)
+            if g == 0:
+                nc.vector.tensor_copy(k_grouped[g][:, cols, PACK - 1], k_last[g][:, cols])
             else:
-                nc.vector.tensor_copy(woven, planes)
+                nc.scalar.copy(k_grouped[g][:, cols, PACK - 1], k_last[g][:, cols])
 
         def scores(i):
+            g, h = divmod(i, PASS // PIECE)
             nc.vector.quantize_mx(
                 out=k_codes[i][:].bitcast(FP8X4),
                 scales=k_scales[i][:],
-                in_=k_grouped[i][:].rearrange("p s j -> p (s j)"),
+                in_=k_grouped[g][:, h * PIECE : (h + 1) * PIECE, :].rearrange("p s j -> p (s j)"),
             )
             score = banks.tile([NQ, PIECE], F32, tag=f"bank{(0, 1, 4, 5)[i]}", name="score")
             nc.tensor.matmul_mx(
@@ -152,7 +161,6 @@ def tile_attend_x_cap_sink_kernel(tc, qT, kT, vT, vs, sink, offs, out):
                 start=True,
                 stop=True,
             )
-            g, h = divmod(i, PASS // PIECE)
             dealt = capped[g][:, 0:PASS].rearrange("q (t s) -> q s t", t=PACK)
             run = PIECE // PACK
             nc.scalar.activation(
@@ -162,21 +170,28 @@ def tile_attend_x_cap_sink_kernel(tc, qT, kT, vT, vs, sink, offs, out):
                 scale=0.5,
             )
 
-        def maxima(g):
-            before = neg_max[g - 1][:] if g else None
-            nc.vector.tensor_scalar(
-                doubled[:, span(g)], capped[g][:], -2.0, before, ALU.mult, ALU.min, accum_out=neg_max[g][:]
-            )
+        def maxima():
+            for g in range(PASSES):
+                before = neg_max[g - 1][:] if g else None
+                nc.vector.tensor_scalar(
+                    doubled[g][:], capped[g][:], -2.0, before, ALU.mult, ALU.min, accum_out=neg_max[g][:]
+                )
 
-        def exps(g):
+        def exps(i):
+            g, u = divmod(i, 2)
             nc.scalar.activation(
-                p[:, span(g)], capped[g][:], ACT.Exp, bias=neg_max[-1][:], scale=2.0, accum_out=terms[:, g : g + 1]
+                p[i][:],
+                capped[g][:, u * PIECE : (u + 1) * PIECE + (i == 1)],
+                ACT.Exp,
+                bias=neg_max[-1][:],
+                scale=2.0,
+                accum_out=terms[:, i : i + 1],
             )
 
         def weights(g):
             p_turned = banks.tile([P, PACK, P], F32, tag=f"bank{2 + g}", name="p_turned")
             for t in range(PACK):
-                nc.tensor.transpose(p_turned[:, t, :], p[:, g * PASS + t * P : g * PASS + (t + 1) * P], ident[:])
+                nc.tensor.transpose(p_turned[:, t, :], p[2 * g + t // 2][:, (t % 2) * P : (t % 2 + 1) * P], ident[:])
             nc.vector.tensor_tensor(
                 w_grouped[:, g].rearrange("p (c i) j -> p c j i", i=PACK),
                 p_turned[:].rearrange("p j (c i) -> p c j i", i=PACK),
@@ -221,21 +236,20 @@ def tile_attend_x_cap_sink_kernel(tc, qT, kT, vT, vs, sink, offs, out):
         keys(2)
         sinks()
         keys(3)
-        for i in range(PIECES):
-            weave(i)
         queries()
-        for i in (0, 1, 3, 2):
+        for i in range(PIECES):
+            place_last(i)
+        for i in range(PIECES):
             scores(i)
-        maxima(0)
-        maxima(1)
+        maxima()
         values(0, 0)
         values(0, 1)
-        exps(0)
-        exps(1)
+        for i in range(PIECES):
+            exps(i)
         w_grouped = after_v0.tile([P, PASSES, NQ, PACK], BF16, align_bytes=64, offset=0, name="w_grouped")
         weights(0)
         weights(1)
-        nc.scalar.activation(total[:], terms[:, 0:1], ACT.Identity, bias=terms[:, 1:2])
+        nc.scalar.activation(terms_out[:], terms[:], ACT.Copy, accum_out=total[:])
         v0_grouped = after_exp.tile([P, PASSES * PASS], BF16, align_bytes=64, offset=0, name="v0_grouped")
         turn_values(0, 0, v0_grouped[:, 0:PASS], "bank6")
         turn_values(0, 1, v0_grouped[:, PASS:N], "bank2")

@@ -95,6 +95,7 @@ def tile_attend_x_cap_sink_kernel(tc, qT, kT, vT, vs, sink, offs, out):
         p = [held.tile([NQ, PIECE + (i == 1)], F32, name=f"p{i}") for i in range(PIECES)]
         terms = held.tile([NQ, PIECES], F32, name="terms")
         terms_out = held.tile([NQ, PIECES], F32, name="terms_out")
+        y_out = held.tile([NQ, DV], F32, name="y_out")
         total = held.tile([NQ, 1], F32, name="total")
         w_scales = held.tile([P, PASSES * NQ], U8, align_bytes=64, name="w_scales")
         v_picked = [
@@ -226,9 +227,7 @@ def tile_attend_x_cap_sink_kernel(tc, qT, kT, vT, vs, sink, offs, out):
                     start=(g == 0),
                     stop=(g == PASSES - 1),
                 )
-            y_out = held.tile([NQ, P], F32, name=f"y_out{b}")
-            nc.scalar.activation(y_out[:], y[:], ACT.Copy, scale=recip[:])
-            nc.sync.dma_start(out[0, :, b * P : (b + 1) * P], y_out[:])
+            nc.scalar.activation(y_out[:, b * P : (b + 1) * P], y[:], ACT.Copy, scale=recip[:])
 
         keys(0)
         keys(1)
@@ -270,3 +269,4 @@ def tile_attend_x_cap_sink_kernel(tc, qT, kT, vT, vs, sink, offs, out):
         halves = [slice(g * P, (g + 1) * P) for g in range(PASSES)]
         products(0, w_codes, [v0_codes[:, h] for h in halves], [v0_scales[:, h] for h in halves], "bank0")
         products(1, w_codes, [c[:] for c in v1_codes], [s[:] for s in v1_scales], "bank1")
+        nc.sync.dma_start(out[0], y_out[:])

@@ -77,7 +77,7 @@ def tile_attend_x_cap_sink_kernel(tc, qT, kT, vT, vs, sink, offs, out):
         vs_picked = held.tile([P, N], F32, name="vs_picked")
         vs_parts = held.tile([P, PASSES, PACK, VS_ROWS], F32, name="vs_parts")
         vs_cols = held.tile([P, PASSES, PACK], F32, name="vs_cols")
-        k_last = [held.tile([P, PASS], BF16, name=f"k_last{g}") for g in range(PASSES)]
+        k_picked = [[held.tile([P, PASS], BF16, name=f"k_picked{j}{g}") for g in range(PASSES)] for j in range(PACK)]
         k_grouped = [held.tile([P, PASS, PACK], BF16, align_bytes=64, name=f"k_grouped{g}") for g in range(PASSES)]
         k_codes = [held.tile([P, PIECE], U32, align_bytes=64, name=f"k_codes{i}") for i in range(PIECES)]
         k_scales = [
@@ -108,7 +108,7 @@ def tile_attend_x_cap_sink_kernel(tc, qT, kT, vT, vs, sink, offs, out):
         v1_scales = [held.tile([P, P], U8, align_bytes=64, name=f"v1_scales{g}") for g in range(PASSES)]
 
         def queries():
-            nc.scalar.copy(q_grouped[:], q_raw[:].rearrange("p j w -> p w j"))
+            nc.gpsimd.tensor_scalar(q_grouped[:], q_raw[:].rearrange("p j w -> p w j"), 1.0, 0.0, ALU.mult, ALU.add)
             nc.vector.quantize_mx(
                 out=q_codes[:].bitcast(FP8X4), scales=q_scales[:], in_=q_grouped[:].rearrange("p w j -> p (w j)")
             )
@@ -134,16 +134,21 @@ def tile_attend_x_cap_sink_kernel(tc, qT, kT, vT, vs, sink, offs, out):
 
         def keys(j):
             for g in range(PASSES):
-                picked = k_last[g][:] if j == PACK - 1 else k_grouped[g][:, :, j]
-                nc.vector.tensor_copy(picked, listed(k_pool[j], g * PASS, (g + 1) * PASS))
+                nc.vector.tensor_copy(
+                    k_picked[j][g][:].rearrange("p (t s) -> p s t", t=PACK), listed(k_pool[j], g * PASS, (g + 1) * PASS)
+                )
+                if (j, g) == (PACK - 2, 0):
+                    nc.vector.tensor_copy(k_grouped[g][:, :, j], k_picked[j][g][:])
+                elif j < PACK - 1:
+                    nc.scalar.copy(k_grouped[g][:, :, j], k_picked[j][g][:])
 
         def place_last(i):
             g, h = divmod(i, PASS // PIECE)
             cols = slice(h * PIECE, (h + 1) * PIECE)
             if g == 0:
-                nc.vector.tensor_copy(k_grouped[g][:, cols, PACK - 1], k_last[g][:, cols])
+                nc.vector.tensor_copy(k_grouped[g][:, cols, PACK - 1], k_picked[PACK - 1][g][:, cols])
             else:
-                nc.scalar.copy(k_grouped[g][:, cols, PACK - 1], k_last[g][:, cols])
+                nc.scalar.copy(k_grouped[g][:, cols, PACK - 1], k_picked[PACK - 1][g][:, cols])
 
         def scores(i):
             g, h = divmod(i, PASS // PIECE)
@@ -162,14 +167,7 @@ def tile_attend_x_cap_sink_kernel(tc, qT, kT, vT, vs, sink, offs, out):
                 start=True,
                 stop=True,
             )
-            dealt = capped[g][:, 0:PASS].rearrange("q (t s) -> q s t", t=PACK)
-            run = PIECE // PACK
-            nc.scalar.activation(
-                dealt[:, h * run : (h + 1) * run, :],
-                score[:].rearrange("q (s t) -> q s t", t=PACK),
-                ACT.Tanh,
-                scale=0.5,
-            )
+            nc.scalar.activation(capped[g][:, h * PIECE : (h + 1) * PIECE], score[:], ACT.Tanh, scale=0.5)
 
         def maxima():
             for g in range(PASSES):

@@ -34,6 +34,7 @@ def tile_attend_x_cap_sink_kernel(tc, qT, kT, vT, vs, sink, offs, out):
         tc.tile_pool(name="after_exp", bufs=1) as after_exp,
         tc.tile_pool(name="after_v0", bufs=1) as after_v0,
         tc.tile_pool(name="after_v1", bufs=1) as after_v1,
+        tc.tile_pool(name="after_w", bufs=1) as after_w,
         tc.psum_pool(name="banks", bufs=1) as banks,
     ):
         offsets = held.tile([P, N // LIST_ROWS], U16, name="offsets")
@@ -51,7 +52,7 @@ def tile_attend_x_cap_sink_kernel(tc, qT, kT, vT, vs, sink, offs, out):
             return window[:].indirect(offsets[:, start // LIST_ROWS : stop // LIST_ROWS])
 
         tiny = held.tile([P, 1], F32, name="tiny")
-        nc.vector.memset(tiny[:], 0.0)
+        nc.gpsimd.memset(tiny[:], 0.0)
         tiny_out = held.tile([P, 1], F32, name="tiny_out")
         nc.scalar.activation(tiny_out[:], tiny[:], ACT.Exp)
         nc.vector.memset(vs_pool[:], 0.0)
@@ -76,9 +77,11 @@ def tile_attend_x_cap_sink_kernel(tc, qT, kT, vT, vs, sink, offs, out):
         q_scales = held.tile([P, NQ], U8, align_bytes=64, name="q_scales")
         vs_picked = held.tile([P, N], F32, name="vs_picked")
         vs_parts = held.tile([P, PASSES, PACK, VS_ROWS], F32, name="vs_parts")
-        vs_cols = held.tile([P, PASSES, PACK], F32, name="vs_cols")
-        k_picked = [[held.tile([P, PASS], BF16, name=f"k_picked{j}{g}") for g in range(PASSES)] for j in range(PACK)]
-        k_grouped = [held.tile([P, PASS, PACK], BF16, align_bytes=64, name=f"k_grouped{g}") for g in range(PASSES)]
+        vs_pairs = held.tile([P, PASSES, PACK, 2], F32, name="vs_pairs")
+        vs_cols = after_w.tile([P, PASSES, PACK], F32, offset=0, name="vs_cols")
+        k_picked = [held.tile([P, N], BF16, name=f"k_picked{j}") for j in range(PACK - 1)]
+        k_last = [held.tile([P, PASS], BF16, name=f"k_last{g}") for g in range(PASSES)]
+        k_grouped = held.tile([P, N, PACK], BF16, align_bytes=64, name="k_grouped")
         k_codes = [held.tile([P, PIECE], U32, align_bytes=64, name=f"k_codes{i}") for i in range(PIECES)]
         k_scales = [
             after_q.tile([P, PIECE], U8, align_bytes=64, offset=i * PIECE, name=f"k_scales{i}") for i in range(PIECES)
@@ -94,14 +97,16 @@ def tile_attend_x_cap_sink_kernel(tc, qT, kT, vT, vs, sink, offs, out):
         neg_max = [held.tile([NQ, 1], F32, name=f"neg_max{i}") for i in range(PASSES)]
         p = [held.tile([NQ, PIECE + (i == 1)], F32, name=f"p{i}") for i in range(PIECES)]
         terms = held.tile([NQ, PIECES], F32, name="terms")
-        terms_out = held.tile([NQ, PIECES], F32, name="terms_out")
+        term_pairs = held.tile([NQ, 2], F32, name="term_pairs")
         y_out = held.tile([NQ, DV], F32, name="y_out")
         total = held.tile([NQ, 1], F32, name="total")
         w_scales = held.tile([P, PASSES * NQ], U8, align_bytes=64, name="w_scales")
-        v_picked = [
-            [after_max.tile([P, 2, P, 2], BF16, offset=1024 * g, name=f"v_picked0{g}") for g in range(PASSES)],
-            [held.tile([P, 2, P, 2], BF16, name=f"v_picked1{g}") for g in range(PASSES)],
+        v0_picked = after_max.tile([P, PASSES, 2, P, 2], BF16, offset=0, name="v0_picked")
+        v1_picked = [
+            after_w.tile([P, 2, P, 2], BF16, offset=0, name="v1_picked0"),
+            held.tile([P, 2, P, 2], BF16, name="v1_picked1"),
         ]
+        v_picked = [[v0_picked[:, g] for g in range(PASSES)], [v1_picked[g][:] for g in range(PASSES)]]
         v0_scales = held.tile([P, PASSES * P], U8, align_bytes=64, name="v0_scales")
         v1_grouped = [held.tile([P, P * PACK], BF16, align_bytes=64, name=f"v1_grouped{g}") for g in range(PASSES)]
         v1_codes = [held.tile([P, P], U32, align_bytes=64, name=f"v1_codes{g}") for g in range(PASSES)]
@@ -114,7 +119,7 @@ def tile_attend_x_cap_sink_kernel(tc, qT, kT, vT, vs, sink, offs, out):
             )
 
         def sinks():
-            nc.scalar.activation(capped[0][:, PASS : PASS + 1], sink_col[:], ACT.Copy, scale=0.5)
+            nc.gpsimd.tensor_scalar(capped[0][:, PASS : PASS + 1], sink_col[:], 0.5, 0.0, ALU.mult, ALU.add)
 
         def token_scales():
             nc.vector.tensor_copy(vs_picked[:], listed(vs_pool, 0, N))
@@ -124,38 +129,39 @@ def tile_attend_x_cap_sink_kernel(tc, qT, kT, vT, vs, sink, offs, out):
                     nc.tensor.transpose(
                         vs_turned[:, t, :], vs_picked[:, g * PASS + t : (g + 1) * PASS : PACK], ident[:]
                     )
-                for t in range(PACK):
-                    nc.scalar.activation(
-                        vs_parts[:, g, t, :],
-                        vs_turned[:, t, 0 : VS_ROWS * PORT_ROWS : PORT_ROWS],
-                        ACT.Copy,
-                        accum_out=vs_cols[:, g, t : t + 1],
-                    )
+                nc.scalar.copy(vs_parts[:, g], vs_turned[:, :, 0 : VS_ROWS * PORT_ROWS : PORT_ROWS])
+            nc.gpsimd.tensor_tensor(vs_pairs[:], vs_parts[:, :, :, 0:2], vs_parts[:, :, :, 2:4], ALU.add)
+            nc.gpsimd.tensor_tensor(vs_cols[:], vs_pairs[:, :, :, 0], vs_pairs[:, :, :, 1], ALU.add)
 
         def keys(j):
+            nc.vector.tensor_copy(
+                k_picked[j][:].rearrange("p (g t s) -> p g s t", g=PASSES, t=PACK), listed(k_pool[j], 0, N)
+            )
+            if j < PACK - 2:
+                nc.scalar.copy(k_grouped[:, :, j], k_picked[j][:])
+            else:
+                nc.vector.tensor_copy(k_grouped[:, 0:PASS, j], k_picked[j][:, 0:PASS])
+                nc.scalar.copy(k_grouped[:, PASS:N, j], k_picked[j][:, PASS:N])
+
+        def last_keys():
             for g in range(PASSES):
                 nc.vector.tensor_copy(
-                    k_picked[j][g][:].rearrange("p (t s) -> p s t", t=PACK), listed(k_pool[j], g * PASS, (g + 1) * PASS)
+                    k_last[g][:].rearrange("p (t s) -> p s t", t=PACK),
+                    listed(k_pool[PACK - 1], g * PASS, (g + 1) * PASS),
                 )
-                if (j, g) == (PACK - 2, 0):
-                    nc.vector.tensor_copy(k_grouped[g][:, :, j], k_picked[j][g][:])
-                elif j < PACK - 1:
-                    nc.scalar.copy(k_grouped[g][:, :, j], k_picked[j][g][:])
 
-        def place_last(i):
-            g, h = divmod(i, PASS // PIECE)
-            cols = slice(h * PIECE, (h + 1) * PIECE)
-            if g == 0:
-                nc.vector.tensor_copy(k_grouped[g][:, cols, PACK - 1], k_picked[PACK - 1][g][:, cols])
-            else:
-                nc.scalar.copy(k_grouped[g][:, cols, PACK - 1], k_picked[PACK - 1][g][:, cols])
+        def place_last():
+            nc.vector.tensor_copy(k_grouped[:, 0:PASS, PACK - 1], k_last[0][:])
+            for h in range(PASS // PIECE):
+                cols = slice(h * PIECE, (h + 1) * PIECE)
+                nc.scalar.copy(k_grouped[:, PASS + h * PIECE : PASS + (h + 1) * PIECE, PACK - 1], k_last[1][:, cols])
 
         def scores(i):
             g, h = divmod(i, PASS // PIECE)
             nc.vector.quantize_mx(
                 out=k_codes[i][:].bitcast(FP8X4),
                 scales=k_scales[i][:],
-                in_=k_grouped[g][:, h * PIECE : (h + 1) * PIECE, :].rearrange("p s j -> p (s j)"),
+                in_=k_grouped[:, i * PIECE : (i + 1) * PIECE, :].rearrange("p s j -> p (s j)"),
             )
             score = banks.tile([NQ, PIECE], F32, tag=f"bank{(0, 1, 4, 5)[i]}", name="score")
             nc.tensor.matmul_mx(
@@ -198,9 +204,12 @@ def tile_attend_x_cap_sink_kernel(tc, qT, kT, vT, vs, sink, offs, out):
                 ALU.mult,
             )
 
+        def first_values():
+            nc.vector.tensor_copy(v0_picked[:].rearrange("e g u p i -> e g p u i"), listed(v_pool[0], 0, N))
+
         def values(b, g):
             nc.vector.tensor_copy(
-                v_picked[b][g][:].rearrange("e u p i -> e p u i"), listed(v_pool[b], g * PASS, (g + 1) * PASS)
+                v_picked[b][g].rearrange("e u p i -> e p u i"), listed(v_pool[b], g * PASS, (g + 1) * PASS)
             )
 
         def turn_values(b, g, grouped, bank):
@@ -232,21 +241,20 @@ def tile_attend_x_cap_sink_kernel(tc, qT, kT, vT, vs, sink, offs, out):
         token_scales()
         keys(2)
         sinks()
-        keys(3)
+        last_keys()
         queries()
-        for i in range(PIECES):
-            place_last(i)
+        place_last()
         for i in range(PIECES):
             scores(i)
         maxima()
-        values(0, 0)
-        values(0, 1)
+        first_values()
         for i in range(PIECES):
             exps(i)
         w_grouped = after_v0.tile([P, PASSES, NQ, PACK], BF16, align_bytes=64, offset=0, name="w_grouped")
         weights(0)
         weights(1)
-        nc.scalar.activation(terms_out[:], terms[:], ACT.Copy, accum_out=total[:])
+        nc.gpsimd.tensor_tensor(term_pairs[:], terms[:, 0:2], terms[:, 2:4], ALU.add)
+        nc.gpsimd.tensor_tensor(total[:], term_pairs[:, 0:1], term_pairs[:, 1:2], ALU.add)
         v0_grouped = after_exp.tile([P, PASSES * PASS], BF16, align_bytes=64, offset=0, name="v0_grouped")
         turn_values(0, 0, v0_grouped[:, 0:PASS], "bank6")
         turn_values(0, 1, v0_grouped[:, PASS:N], "bank2")

@@ -34,7 +34,6 @@ def tile_attend_x_cap_sink_kernel(tc, qT, kT, vT, vs, sink, offs, out):
         tc.tile_pool(name="after_exp", bufs=1) as after_exp,
         tc.tile_pool(name="after_v0", bufs=1) as after_v0,
         tc.tile_pool(name="after_v1", bufs=1) as after_v1,
-        tc.tile_pool(name="after_w", bufs=1) as after_w,
         tc.psum_pool(name="banks", bufs=1) as banks,
     ):
         offsets = held.tile([P, N // LIST_ROWS], U16, name="offsets")
@@ -78,7 +77,7 @@ def tile_attend_x_cap_sink_kernel(tc, qT, kT, vT, vs, sink, offs, out):
         vs_picked = held.tile([P, N], F32, name="vs_picked")
         vs_parts = held.tile([P, PASSES, PACK, VS_ROWS], F32, name="vs_parts")
         vs_pairs = held.tile([P, PASSES, PACK, 2], F32, name="vs_pairs")
-        vs_cols = after_w.tile([P, PASSES, PACK], F32, offset=0, name="vs_cols")
+        vs_cols = held.tile([P, PASSES, PACK], F32, name="vs_cols")
         k_picked = [held.tile([P, N], BF16, name=f"k_picked{j}") for j in range(PACK - 1)]
         k_last = [held.tile([P, PASS], BF16, name=f"k_last{g}") for g in range(PASSES)]
         k_grouped = held.tile([P, N, PACK], BF16, align_bytes=64, name="k_grouped")
@@ -98,14 +97,11 @@ def tile_attend_x_cap_sink_kernel(tc, qT, kT, vT, vs, sink, offs, out):
         p = [held.tile([NQ, PIECE + (i == 1)], F32, name=f"p{i}") for i in range(PIECES)]
         terms = held.tile([NQ, PIECES], F32, name="terms")
         term_pairs = held.tile([NQ, 2], F32, name="term_pairs")
-        y_out = held.tile([NQ, DV], F32, name="y_out")
+        y_out = [held.tile([NQ, P], F32, name=f"y_out{b}") for b in range(DV // P)]
         total = held.tile([NQ, 1], F32, name="total")
         w_scales = held.tile([P, PASSES * NQ], U8, align_bytes=64, name="w_scales")
         v0_picked = after_max.tile([P, PASSES, 2, P, 2], BF16, offset=0, name="v0_picked")
-        v1_picked = [
-            after_w.tile([P, 2, P, 2], BF16, offset=0, name="v1_picked0"),
-            held.tile([P, 2, P, 2], BF16, name="v1_picked1"),
-        ]
+        v1_picked = [held.tile([P, 2, P, 2], BF16, name=f"v1_picked{g}") for g in range(PASSES)]
         v_picked = [[v0_picked[:, g] for g in range(PASSES)], [v1_picked[g][:] for g in range(PASSES)]]
         v0_scales = held.tile([P, PASSES * P], U8, align_bytes=64, name="v0_scales")
         v1_grouped = [held.tile([P, P * PACK], BF16, align_bytes=64, name=f"v1_grouped{g}") for g in range(PASSES)]
@@ -151,10 +147,12 @@ def tile_attend_x_cap_sink_kernel(tc, qT, kT, vT, vs, sink, offs, out):
                 )
 
         def place_last():
-            nc.vector.tensor_copy(k_grouped[:, 0:PASS, PACK - 1], k_last[0][:])
-            for h in range(PASS // PIECE):
-                cols = slice(h * PIECE, (h + 1) * PIECE)
-                nc.scalar.copy(k_grouped[:, PASS + h * PIECE : PASS + (h + 1) * PIECE, PACK - 1], k_last[1][:, cols])
+            for i in range(PIECES):
+                g, h = divmod(i, PASS // PIECE)
+                engine_copy = nc.vector.tensor_copy if g == 0 else nc.scalar.copy
+                engine_copy(
+                    k_grouped[:, i * PIECE : (i + 1) * PIECE, PACK - 1], k_last[g][:, h * PIECE : (h + 1) * PIECE]
+                )
 
         def scores(i):
             g, h = divmod(i, PASS // PIECE)
@@ -234,7 +232,11 @@ def tile_attend_x_cap_sink_kernel(tc, qT, kT, vT, vs, sink, offs, out):
                     start=(g == 0),
                     stop=(g == PASSES - 1),
                 )
-            nc.scalar.activation(y_out[:, b * P : (b + 1) * P], y[:], ACT.Copy, scale=recip[:])
+            if b == 0:
+                nc.scalar.activation(y_out[b][:], y[:], ACT.Copy, scale=recip[:])
+            else:
+                nc.vector.tensor_scalar(y_out[b][:], y[:], recip[:], None, ALU.mult)
+            nc.sync.dma_start(out[0][:, b * P : (b + 1) * P], y_out[b][:])
 
         keys(0)
         keys(1)
@@ -275,4 +277,3 @@ def tile_attend_x_cap_sink_kernel(tc, qT, kT, vT, vs, sink, offs, out):
         halves = [slice(g * P, (g + 1) * P) for g in range(PASSES)]
         products(0, w_codes, [v0_codes[:, h] for h in halves], [v0_scales[:, h] for h in halves], "bank0")
         products(1, w_codes, [c[:] for c in v1_codes], [s[:] for s in v1_scales], "bank1")
-        nc.sync.dma_start(out[0], y_out[:])

@@ -6,14 +6,15 @@ P = 128
 PACK = 4
 PASS = P * PACK
 PASSES = N // PASS
-LIST_ROWS = 16
-VS_ROWS = 4
-PORT_ROWS = 4
-PIECE = 256
+PAIR = 2
+PIECE = P * PAIR
 PIECES = N // PIECE
+LIST_ROWS = 16
+QUARTERS = 4
+PORT_ROWS = 4
 
 FLOPS = 2 * NQ * N * (D + DV)
-BYTES = 4 * (D * T + DV * T + D * NQ + T + NQ + NQ * DV) + 2 * P * (N // 16)
+BYTES = 4 * (D * T + DV * T + D * NQ + T + NQ + NQ * DV) + 2 * P * (N // LIST_ROWS)
 
 F32 = mybir.dt.float32
 BF16 = mybir.dt.bfloat16
@@ -37,151 +38,145 @@ def tile_attend_x_cap_sink_kernel(tc, qT, kT, vT, vs, sink, offs, out):
         tc.psum_pool(name="banks", bufs=1) as banks,
     ):
         offsets = held.tile([P, N // LIST_ROWS], U16, name="offsets")
-        k_rows = kT.rearrange("(p j) t -> p j t", j=PACK)
         k_pool = [held.tile([P, T], F32, name=f"k_pool{j}") for j in range(PACK)]
         v_pool = [
             after_v0.tile([P, T], F32, align_bytes=64, offset=0, name="v_pool0"),
             after_v1.tile([P, T], F32, align_bytes=64, offset=0, name="v_pool1"),
         ]
-        q_raw = after_q.tile([P, PACK, NQ], F32, align_bytes=64, offset=0, name="q_raw")
         vs_pool = held.tile([P, T], F32, name="vs_pool")
+        q_raw = after_q.tile([P, PACK, NQ], F32, align_bytes=64, offset=0, name="q_raw")
         sink_col = held.tile([P, 1], F32, name="sink_col")
-
-        def listed(window, start, stop):
-            return window[:].indirect(offsets[:, start // LIST_ROWS : stop // LIST_ROWS])
-
-        tiny = held.tile([P, 1], F32, name="tiny")
-        nc.gpsimd.memset(tiny[:], 0.0)
-        tiny_out = held.tile([P, 1], F32, name="tiny_out")
-        nc.scalar.activation(tiny_out[:], tiny[:], ACT.Exp)
-        nc.vector.memset(vs_pool[:], 0.0)
         ident = held.tile([P, P], F32, name="ident")
+        zero = held.tile([P, 1], F32, name="zero")
+        warm = held.tile([P, 1], F32, name="warm")
+
+        nc.gpsimd.memset(zero[:], 0.0)
+        nc.scalar.activation(warm[:], zero[:], ACT.Exp)
+        nc.vector.memset(vs_pool[:], 0.0)
         make_identity(nc, ident[:])
 
+        k_rows = kT.rearrange("(p j) t -> p j t", j=PACK)
         nc.sync.dma_start(k_pool[0][:], k_rows[:, 0, :])
         nc.sync.dma_start(offsets[:], offs)
         nc.sync.dma_start(k_pool[1][:], k_rows[:, 1, :])
         nc.sync.dma_start(sink_col[:], sink[0])
-        for r in range(VS_ROWS):
-            part = slice(r * T // VS_ROWS, (r + 1) * T // VS_ROWS)
+        for r in range(QUARTERS):
+            part = slice(r * T // QUARTERS, (r + 1) * T // QUARTERS)
             nc.sync.dma_start(vs_pool[PORT_ROWS * r : PORT_ROWS * r + 1, part], vs[r : r + 1, part])
         nc.sync.dma_start(k_pool[2][:], k_rows[:, 2, :])
         nc.sync.dma_start(k_pool[3][:], k_rows[:, 3, :])
         nc.sync.dma_start(q_raw[:], qT[0].rearrange("(p j) w -> p j w", j=PACK))
-        nc.sync.dma_start(v_pool[0][:], vT[0 * P : 1 * P, :])
-        nc.sync.dma_start(v_pool[1][:], vT[1 * P : 2 * P, :])
+        nc.sync.dma_start(v_pool[0][:], vT[0:P, :])
+        nc.sync.dma_start(v_pool[1][:], vT[P : 2 * P, :])
 
-        q_grouped = held.tile([P, NQ, PACK], BF16, align_bytes=64, name="q_grouped")
-        q_codes = held.tile([P, NQ], U32, align_bytes=64, name="q_codes")
-        q_scales = held.tile([P, NQ], U8, align_bytes=64, name="q_scales")
+        def gather(dealt, window, first, count):
+            nc.vector.tensor_copy(
+                dealt.rearrange("p (g u s i) -> p g s u i", u=PAIR, s=P, i=PAIR),
+                window[:].indirect(offsets[:, first // LIST_ROWS : (first + count) // LIST_ROWS]),
+            )
+
+        def quantise(codes, scales, grouped):
+            nc.vector.quantize_mx(out=codes.bitcast(FP8X4), scales=scales, in_=grouped)
+
+        def multiply(sums, left, left_scales, right, right_scales, start, stop):
+            nc.tensor.matmul_mx(
+                out=sums,
+                lhsT=left.bitcast(FP8X4),
+                lhsT_scale=left_scales,
+                rhs=right.bitcast(FP8X4),
+                rhs_scale=right_scales,
+                start=start,
+                stop=stop,
+            )
+
+        def turn(dealt, grouped, bank):
+            turned = banks.tile([P, PAIR, P], F32, tag=bank, name="turned")
+            for u in range(PAIR):
+                nc.tensor.transpose(turned[:, u, :], dealt[u].bitcast(F32), ident[:])
+            nc.scalar.copy(
+                grouped.bitcast(F32).rearrange("p (e u) -> p e u", u=PAIR), turned[:].rearrange("p u e -> p e u")
+            )
+
+        def piece(i):
+            return slice(i * PIECE, (i + 1) * PIECE)
+
+        k_grouped = held.tile([P, N, PACK], BF16, align_bytes=64, name="k_grouped")
+        k_picked = [held.tile([P, N], BF16, name=f"k_picked{j}") for j in range(PACK - 1)]
+        for j in range(PACK - 2):
+            gather(k_picked[j][:], k_pool[j], 0, N)
+            nc.scalar.copy(k_grouped[:, :, j], k_picked[j][:])
+
         vs_picked = held.tile([P, N], F32, name="vs_picked")
-        vs_parts = held.tile([P, PASSES, PACK, VS_ROWS], F32, name="vs_parts")
+        vs_parts = held.tile([P, PASSES, PACK, QUARTERS], F32, name="vs_parts")
         vs_pairs = held.tile([P, PASSES, PACK, 2], F32, name="vs_pairs")
         vs_cols = held.tile([P, PASSES, PACK], F32, name="vs_cols")
-        k_picked = [held.tile([P, N], BF16, name=f"k_picked{j}") for j in range(PACK - 1)]
-        k_last = [held.tile([P, PASS], BF16, name=f"k_last{g}") for g in range(PASSES)]
-        k_grouped = held.tile([P, N, PACK], BF16, align_bytes=64, name="k_grouped")
-        k_codes = [held.tile([P, PIECE], U32, align_bytes=64, name=f"k_codes{i}") for i in range(PIECES)]
-        k_scales = [
-            after_q.tile([P, PIECE], U8, align_bytes=64, offset=i * PIECE, name=f"k_scales{i}") for i in range(PIECES)
-        ]
+        nc.vector.tensor_copy(vs_picked[:], vs_pool[:].indirect(offsets[:]))
+        for g in range(PASSES):
+            vs_turned = banks.tile([P, PACK, P], F32, tag=f"bank{6 + g}", name="vs_turned")
+            for t in range(PACK):
+                nc.tensor.transpose(vs_turned[:, t, :], vs_picked[:, g * PASS + t : (g + 1) * PASS : PACK], ident[:])
+            nc.scalar.copy(vs_parts[:, g], vs_turned[:, :, 0 : QUARTERS * PORT_ROWS : PORT_ROWS])
+        nc.gpsimd.tensor_tensor(vs_pairs[:], vs_parts[:, :, :, 0:2], vs_parts[:, :, :, 2:4], ALU.add)
+        nc.gpsimd.tensor_tensor(vs_cols[:], vs_pairs[:, :, :, 0], vs_pairs[:, :, :, 1], ALU.add)
+        vs_spread = []
+        for g in range(PASSES):
+            vs_spread.append(banks.tile([NQ, PAIR, P, PAIR], F32, tag=f"bank{2 + g}", name="vs_spread"))
+            for t in range(PACK):
+                u, i = divmod(t, PAIR)
+                nc.tensor.transpose(vs_spread[g][:, u, :, i], vs_cols[:, g, t : t + 1].to_broadcast([P, NQ]), ident[:])
+
+        gather(k_picked[2][:], k_pool[2], 0, N)
+        nc.vector.tensor_copy(k_grouped[:, 0:PASS, 2], k_picked[2][:, 0:PASS])
+        nc.scalar.copy(k_grouped[:, PASS:N, 2], k_picked[2][:, PASS:N])
+
         capped = [
             held.tile([NQ, PASS + 1], F32, name="capped0"),
             after_exp.tile([NQ, PASS], F32, align_bytes=64, offset=0, name="capped1"),
         ]
+        nc.gpsimd.tensor_scalar(capped[0][:, PASS : PASS + 1], sink_col[:], 0.5, 0.0, ALU.mult, ALU.add)
+
+        k_last = [held.tile([P, PASS], BF16, name=f"k_last{g}") for g in range(PASSES)]
+        for g in range(PASSES):
+            gather(k_last[g][:], k_pool[3], g * PASS, PASS)
+
+        q_grouped = held.tile([P, NQ, PACK], BF16, align_bytes=64, name="q_grouped")
+        q_codes = held.tile([P, NQ], U32, align_bytes=64, name="q_codes")
+        q_scales = held.tile([P, NQ], U8, align_bytes=64, name="q_scales")
+        nc.gpsimd.tensor_scalar(q_grouped[:], q_raw[:].rearrange("p j w -> p w j"), 1.0, 0.0, ALU.mult, ALU.add)
+        quantise(q_codes[:], q_scales[:], q_grouped[:].rearrange("p w j -> p (w j)"))
+
+        for i in range(PIECES):
+            g, u = divmod(i, PAIR)
+            place = nc.vector.tensor_copy if g == 0 else nc.scalar.copy
+            place(k_grouped[:, piece(i), 3], k_last[g][:, piece(u)])
+
+        for i in range(PIECES):
+            g, u = divmod(i, PAIR)
+            k_codes = held.tile([P, PIECE], U32, align_bytes=64, name=f"k_codes{i}")
+            k_scales = after_q.tile([P, PIECE], U8, align_bytes=64, offset=i * PIECE, name=f"k_scales{i}")
+            quantise(k_codes[:], k_scales[:], k_grouped[:, piece(i), :].rearrange("p s j -> p (s j)"))
+            score = banks.tile([NQ, PIECE], F32, tag=f"bank{(0, 1, 4, 5)[i]}", name="score")
+            multiply(score[:], q_codes[:], q_scales[:], k_codes[:], k_scales[:], True, True)
+            nc.scalar.activation(capped[g][:, piece(u)], score[:], ACT.Tanh, scale=0.5)
+
         doubled = [
             held.tile([NQ, PASS + 1], F32, name="doubled0"),
             after_max.tile([NQ, PASS], F32, offset=0, name="doubled1"),
         ]
-        neg_max = [held.tile([NQ, 1], F32, name=f"neg_max{i}") for i in range(PASSES)]
+        neg_max = [held.tile([NQ, 1], F32, name=f"neg_max{g}") for g in range(PASSES)]
+        for g in range(PASSES):
+            before = neg_max[g - 1][:] if g else None
+            nc.vector.tensor_scalar(
+                doubled[g][:], capped[g][:], -2.0, before, ALU.mult, ALU.min, accum_out=neg_max[g][:]
+            )
+
+        v0_picked = after_max.tile([P, N], BF16, offset=0, name="v0_picked")
+        gather(v0_picked[:], v_pool[0], 0, N)
+
         p = [held.tile([NQ, PIECE + (i == 1)], F32, name=f"p{i}") for i in range(PIECES)]
         terms = held.tile([NQ, PIECES], F32, name="terms")
-        term_pairs = held.tile([NQ, 2], F32, name="term_pairs")
-        y_out = [held.tile([NQ, P], F32, name=f"y_out{b}") for b in range(DV // P)]
-        total = held.tile([NQ, 1], F32, name="total")
-        w_scales = held.tile([P, PASSES * NQ], U8, align_bytes=64, name="w_scales")
-        v0_picked = after_max.tile([P, PASSES, 2, P, 2], BF16, offset=0, name="v0_picked")
-        v1_picked = [held.tile([P, 2, P, 2], BF16, name=f"v1_picked{g}") for g in range(PASSES)]
-        v_picked = [[v0_picked[:, g] for g in range(PASSES)], [v1_picked[g][:] for g in range(PASSES)]]
-        v0_scales = held.tile([P, PASSES * P], U8, align_bytes=64, name="v0_scales")
-        v1_grouped = [held.tile([P, P * PACK], BF16, align_bytes=64, name=f"v1_grouped{g}") for g in range(PASSES)]
-        v1_codes = [held.tile([P, P], U32, align_bytes=64, name=f"v1_codes{g}") for g in range(PASSES)]
-        v1_scales = [held.tile([P, P], U8, align_bytes=64, name=f"v1_scales{g}") for g in range(PASSES)]
-
-        def queries():
-            nc.gpsimd.tensor_scalar(q_grouped[:], q_raw[:].rearrange("p j w -> p w j"), 1.0, 0.0, ALU.mult, ALU.add)
-            nc.vector.quantize_mx(
-                out=q_codes[:].bitcast(FP8X4), scales=q_scales[:], in_=q_grouped[:].rearrange("p w j -> p (w j)")
-            )
-
-        def sinks():
-            nc.gpsimd.tensor_scalar(capped[0][:, PASS : PASS + 1], sink_col[:], 0.5, 0.0, ALU.mult, ALU.add)
-
-        def token_scales():
-            nc.vector.tensor_copy(vs_picked[:], listed(vs_pool, 0, N))
-            for g in range(PASSES):
-                vs_turned = banks.tile([P, PACK, P], F32, tag=f"bank{2 + g}", name="vs_turned")
-                for t in range(PACK):
-                    nc.tensor.transpose(
-                        vs_turned[:, t, :], vs_picked[:, g * PASS + t : (g + 1) * PASS : PACK], ident[:]
-                    )
-                nc.scalar.copy(vs_parts[:, g], vs_turned[:, :, 0 : VS_ROWS * PORT_ROWS : PORT_ROWS])
-            nc.gpsimd.tensor_tensor(vs_pairs[:], vs_parts[:, :, :, 0:2], vs_parts[:, :, :, 2:4], ALU.add)
-            nc.gpsimd.tensor_tensor(vs_cols[:], vs_pairs[:, :, :, 0], vs_pairs[:, :, :, 1], ALU.add)
-
-        def keys(j):
-            nc.vector.tensor_copy(
-                k_picked[j][:].rearrange("p (g t s) -> p g s t", g=PASSES, t=PACK), listed(k_pool[j], 0, N)
-            )
-            if j < PACK - 2:
-                nc.scalar.copy(k_grouped[:, :, j], k_picked[j][:])
-            else:
-                nc.vector.tensor_copy(k_grouped[:, 0:PASS, j], k_picked[j][:, 0:PASS])
-                nc.scalar.copy(k_grouped[:, PASS:N, j], k_picked[j][:, PASS:N])
-
-        def last_keys():
-            for g in range(PASSES):
-                nc.vector.tensor_copy(
-                    k_last[g][:].rearrange("p (t s) -> p s t", t=PACK),
-                    listed(k_pool[PACK - 1], g * PASS, (g + 1) * PASS),
-                )
-
-        def place_last():
-            for i in range(PIECES):
-                g, h = divmod(i, PASS // PIECE)
-                engine_copy = nc.vector.tensor_copy if g == 0 else nc.scalar.copy
-                engine_copy(
-                    k_grouped[:, i * PIECE : (i + 1) * PIECE, PACK - 1], k_last[g][:, h * PIECE : (h + 1) * PIECE]
-                )
-
-        def scores(i):
-            g, h = divmod(i, PASS // PIECE)
-            nc.vector.quantize_mx(
-                out=k_codes[i][:].bitcast(FP8X4),
-                scales=k_scales[i][:],
-                in_=k_grouped[:, i * PIECE : (i + 1) * PIECE, :].rearrange("p s j -> p (s j)"),
-            )
-            score = banks.tile([NQ, PIECE], F32, tag=f"bank{(0, 1, 4, 5)[i]}", name="score")
-            nc.tensor.matmul_mx(
-                out=score[:],
-                lhsT=q_codes[:].bitcast(FP8X4),
-                lhsT_scale=q_scales[:],
-                rhs=k_codes[i][:].bitcast(FP8X4),
-                rhs_scale=k_scales[i][:],
-                start=True,
-                stop=True,
-            )
-            nc.scalar.activation(capped[g][:, h * PIECE : (h + 1) * PIECE], score[:], ACT.Tanh, scale=0.5)
-
-        def maxima():
-            for g in range(PASSES):
-                before = neg_max[g - 1][:] if g else None
-                nc.vector.tensor_scalar(
-                    doubled[g][:], capped[g][:], -2.0, before, ALU.mult, ALU.min, accum_out=neg_max[g][:]
-                )
-
-        def exps(i):
-            g, u = divmod(i, 2)
+        for i in range(PIECES):
+            g, u = divmod(i, PAIR)
             nc.scalar.activation(
                 p[i][:],
                 capped[g][:, u * PIECE : (u + 1) * PIECE + (i == 1)],
@@ -190,90 +185,61 @@ def tile_attend_x_cap_sink_kernel(tc, qT, kT, vT, vs, sink, offs, out):
                 scale=2.0,
                 accum_out=terms[:, i : i + 1],
             )
-
-        def weights(g):
-            p_turned = banks.tile([P, PACK, P], F32, tag=f"bank{2 + g}", name="p_turned")
-            for t in range(PACK):
-                nc.tensor.transpose(p_turned[:, t, :], p[2 * g + t // 2][:, (t % 2) * P : (t % 2 + 1) * P], ident[:])
+        w_rows = [
+            after_v0.tile([NQ, PIECE], BF16, align_bytes=64, offset=2 * PIECE * i, name=f"w_rows{i}")
+            for i in range(PIECES)
+        ]
+        for i in range(PIECES):
+            g, u = divmod(i, PAIR)
             nc.vector.tensor_tensor(
-                w_grouped[:, g].rearrange("p (c i) j -> p c j i", i=PACK),
-                p_turned[:].rearrange("p j (c i) -> p c j i", i=PACK),
-                vs_cols[:, g, :].unsqueeze(1).unsqueeze(3).to_broadcast([P, NQ // PACK, PACK, PACK]),
-                ALU.mult,
+                w_rows[i][:], p[i][:, 0:PIECE], vs_spread[g][:, u].rearrange("q s i -> q (s i)"), ALU.mult
             )
-
-        def first_values():
-            nc.vector.tensor_copy(v0_picked[:].rearrange("e g u p i -> e g p u i"), listed(v_pool[0], 0, N))
-
-        def values(b, g):
-            nc.vector.tensor_copy(
-                v_picked[b][g].rearrange("e u p i -> e p u i"), listed(v_pool[b], g * PASS, (g + 1) * PASS)
-            )
-
-        def turn_values(b, g, grouped, bank):
-            v_turned = banks.tile([P, 2, P], F32, tag=bank, name="v_turned")
-            for u in range(2):
-                nc.tensor.transpose(
-                    v_turned[:, u, :], v_picked[b][g][:, u].rearrange("e p i -> e (p i)").bitcast(F32), ident[:]
-                )
-            nc.scalar.copy(
-                grouped.bitcast(F32).rearrange("p (e u) -> p e u", u=2), v_turned[:].rearrange("p u e -> p e u")
-            )
-
-        def products(b, w_codes, codes, scales, bank):
-            y = banks.tile([NQ, P], F32, tag=bank, name="y")
-            for g in range(PASSES):
-                nc.tensor.matmul_mx(
-                    out=y[:],
-                    lhsT=w_codes[:, g * NQ : (g + 1) * NQ].bitcast(FP8X4),
-                    lhsT_scale=w_scales[:, g * NQ : (g + 1) * NQ],
-                    rhs=codes[g].bitcast(FP8X4),
-                    rhs_scale=scales[g],
-                    start=(g == 0),
-                    stop=(g == PASSES - 1),
-                )
-            if b == 0:
-                nc.scalar.activation(y_out[b][:], y[:], ACT.Copy, scale=recip[:])
-            else:
-                nc.vector.tensor_scalar(y_out[b][:], y[:], recip[:], None, ALU.mult)
-            nc.sync.dma_start(out[0][:, b * P : (b + 1) * P], y_out[b][:])
-
-        keys(0)
-        keys(1)
-        token_scales()
-        keys(2)
-        sinks()
-        last_keys()
-        queries()
-        place_last()
-        for i in range(PIECES):
-            scores(i)
-        maxima()
-        first_values()
-        for i in range(PIECES):
-            exps(i)
-        w_grouped = after_v0.tile([P, PASSES, NQ, PACK], BF16, align_bytes=64, offset=0, name="w_grouped")
-        weights(0)
-        weights(1)
+        term_pairs = held.tile([NQ, 2], F32, name="term_pairs")
+        total = held.tile([NQ, 1], F32, name="total")
         nc.gpsimd.tensor_tensor(term_pairs[:], terms[:, 0:2], terms[:, 2:4], ALU.add)
         nc.gpsimd.tensor_tensor(total[:], term_pairs[:, 0:1], term_pairs[:, 1:2], ALU.add)
-        v0_grouped = after_exp.tile([P, PASSES * PASS], BF16, align_bytes=64, offset=0, name="v0_grouped")
-        turn_values(0, 0, v0_grouped[:, 0:PASS], "bank6")
-        turn_values(0, 1, v0_grouped[:, PASS:N], "bank2")
-        values(1, 0)
-        values(1, 1)
-        turn_values(1, 0, v1_grouped[0][:], "bank7")
-        turn_values(1, 1, v1_grouped[1][:], "bank4")
+
+        v0_grouped = after_exp.tile([P, N], BF16, align_bytes=64, offset=0, name="v0_grouped")
+        w_grouped = held.tile([P, N], BF16, align_bytes=64, name="w_grouped")
+        for g in range(PASSES):
+            halves = [v0_picked[:, piece(PAIR * g + u)] for u in range(PAIR)]
+            turn(halves, v0_grouped[:, g * PASS : (g + 1) * PASS], f"bank{6 + g}")
+        for g in range(PASSES):
+            halves = [w_rows[PAIR * g + u][:] for u in range(PAIR)]
+            turn(halves, w_grouped[:, g * PASS : (g + 1) * PASS], f"bank{g}")
+
+        v1_picked = [held.tile([P, PASS], BF16, name=f"v1_picked{g}") for g in range(PASSES)]
+        v1_grouped = [held.tile([P, PASS], BF16, align_bytes=64, name=f"v1_grouped{g}") for g in range(PASSES)]
+        for g in range(PASSES):
+            gather(v1_picked[g][:], v_pool[1], g * PASS, PASS)
+        for g in range(PASSES):
+            turn([v1_picked[g][:, piece(u)] for u in range(PAIR)], v1_grouped[g][:], f"bank{4 + g}")
+
         w_codes = after_v1.tile([P, PASSES * NQ], U32, align_bytes=64, offset=0, name="w_codes")
-        nc.vector.quantize_mx(
-            out=w_codes[:].bitcast(FP8X4), scales=w_scales[:], in_=w_grouped[:].rearrange("p g q j -> p (g q j)")
-        )
+        w_scales = held.tile([P, PASSES * NQ], U8, align_bytes=64, name="w_scales")
         v0_codes = after_v1.tile([P, PASSES * P], U32, align_bytes=64, offset=1024, name="v0_codes")
-        nc.vector.quantize_mx(out=v0_codes[:].bitcast(FP8X4), scales=v0_scales[:], in_=v0_grouped[:])
+        v0_scales = held.tile([P, PASSES * P], U8, align_bytes=64, name="v0_scales")
         recip = after_v1.tile([NQ, 1], F32, align_bytes=64, offset=2048, name="recip")
+        v1_codes = [held.tile([P, P], U32, align_bytes=64, name=f"v1_codes{g}") for g in range(PASSES)]
+        v1_scales = [held.tile([P, P], U8, align_bytes=64, name=f"v1_scales{g}") for g in range(PASSES)]
+        quantise(v0_codes[:], v0_scales[:], v0_grouped[:])
+        quantise(w_codes[:], w_scales[:], w_grouped[:])
         nc.vector.reciprocal(recip[:], total[:])
         for g in range(PASSES):
-            nc.vector.quantize_mx(out=v1_codes[g][:].bitcast(FP8X4), scales=v1_scales[g][:], in_=v1_grouped[g][:])
-        halves = [slice(g * P, (g + 1) * P) for g in range(PASSES)]
-        products(0, w_codes, [v0_codes[:, h] for h in halves], [v0_scales[:, h] for h in halves], "bank0")
-        products(1, w_codes, [c[:] for c in v1_codes], [s[:] for s in v1_scales], "bank1")
+            quantise(v1_codes[g][:], v1_scales[g][:], v1_grouped[g][:])
+
+        columns = [slice(g * P, (g + 1) * P) for g in range(PASSES)]
+        values = [
+            [(v0_codes[:, c], v0_scales[:, c]) for c in columns],
+            [(v1_codes[g][:], v1_scales[g][:]) for g in range(PASSES)],
+        ]
+        for b in range(DV // P):
+            y = banks.tile([NQ, P], F32, tag=f"bank{6 + b}", name="y")
+            for g in range(PASSES):
+                multiply(y[:], w_codes[:, columns[g]], w_scales[:, columns[g]], *values[b][g], g == 0, g == PASSES - 1)
+            y_out = held.tile([NQ, P], F32, name=f"y_out{b}")
+            if b == 0:
+                nc.scalar.activation(y_out[:], y[:], ACT.Copy, scale=recip[:])
+            else:
+                nc.vector.tensor_scalar(y_out[:], y[:], recip[:], None, ALU.mult)
+            nc.sync.dma_start(out[0][:, b * P : (b + 1) * P], y_out[:])

@@ -47,11 +47,7 @@ def tile_attend_x_cap_sink_kernel(tc, qT, kT, vT, vs, sink, offs, out):
         q_raw = after_q.tile([P, PACK, NQ], F32, align_bytes=64, offset=0, name="q_raw")
         sink_col = held.tile([P, 1], F32, name="sink_col")
         ident = held.tile([P, P], F32, name="ident")
-        zero = held.tile([P, 1], F32, name="zero")
-        warm = held.tile([P, 1], F32, name="warm")
 
-        nc.gpsimd.memset(zero[:], 0.0)
-        nc.scalar.activation(warm[:], zero[:], ACT.Exp)
         nc.vector.memset(vs_pool[:], 0.0)
         make_identity(nc, ident[:])
 
@@ -67,7 +63,8 @@ def tile_attend_x_cap_sink_kernel(tc, qT, kT, vT, vs, sink, offs, out):
         nc.sync.dma_start(k_pool[3][:], k_rows[:, 3, :])
         nc.sync.dma_start(q_raw[:], qT[0].rearrange("(p j) w -> p j w", j=PACK))
         nc.sync.dma_start(v_pool[0][:], vT[0:P, :])
-        nc.sync.dma_start(v_pool[1][:], vT[P : 2 * P, :])
+        nc.sync.dma_start(v_pool[1][0:P:2, :], vT[P : 2 * P : 2, :])
+        nc.sync.dma_start(v_pool[1][1:P:2, :], vT[P + 1 : 2 * P : 2, :])
 
         def gather(dealt, window, first, count):
             nc.vector.tensor_copy(

@@ -63,8 +63,7 @@ def tile_attend_x_cap_sink_kernel(tc, qT, kT, vT, vs, sink, offs, out):
         nc.sync.dma_start(k_pool[3][:], k_rows[:, 3, :])
         nc.sync.dma_start(q_raw[:], qT[0].rearrange("(p j) w -> p j w", j=PACK))
         nc.sync.dma_start(v_pool[0][:], vT[0:P, :])
-        nc.sync.dma_start(v_pool[1][0:P:2, :], vT[P : 2 * P : 2, :])
-        nc.sync.dma_start(v_pool[1][1:P:2, :], vT[P + 1 : 2 * P : 2, :])
+        nc.sync.dma_start(v_pool[1][:], vT[P : 2 * P, :])
 
         def gather(dealt, window, first, count):
             nc.vector.tensor_copy(
@@ -239,4 +238,7 @@ def tile_attend_x_cap_sink_kernel(tc, qT, kT, vT, vs, sink, offs, out):
                 nc.scalar.activation(y_out[:], y[:], ACT.Copy, scale=recip[:])
             else:
                 nc.vector.tensor_scalar(y_out[:], y[:], recip[:], None, ALU.mult)
-            nc.sync.dma_start(out[0][:, b * P : (b + 1) * P], y_out[:])
+            parts = 2 if b == 0 else 1
+            for h in range(parts):
+                first, last = h * P // parts, (h + 1) * P // parts
+                nc.sync.dma_start(out[0][:, b * P + first : b * P + last], y_out[:, first:last])

@@ -12,6 +12,8 @@ PIECES = N // PIECE
 LIST_ROWS = 16
 QUARTERS = 4
 PORT_ROWS = 4
+HALF = P // 2
+SHARE = 640
 
 FLOPS = 2 * NQ * N * (D + DV)
 BYTES = 4 * (D * T + DV * T + D * NQ + T + NQ + NQ * DV) + 2 * P * (N // LIST_ROWS)
@@ -31,24 +33,22 @@ def tile_attend_x_cap_sink_kernel(tc, qT, kT, vT, vs, sink, offs, out):
     with (
         tc.tile_pool(name="held", bufs=1) as held,
         tc.tile_pool(name="after_q", bufs=1) as after_q,
-        tc.tile_pool(name="after_max", bufs=1) as after_max,
-        tc.tile_pool(name="after_exp", bufs=1) as after_exp,
-        tc.tile_pool(name="after_v0", bufs=1) as after_v0,
-        tc.tile_pool(name="after_v1", bufs=1) as after_v1,
+        tc.tile_pool(name="after_a", bufs=1) as after_a,
+        tc.tile_pool(name="after_c", bufs=1) as after_c,
         tc.psum_pool(name="banks", bufs=1) as banks,
     ):
         offsets = held.tile([P, N // LIST_ROWS], U16, name="offsets")
         k_pool = [held.tile([P, T], F32, name=f"k_pool{j}") for j in range(PACK)]
-        v_pool = [
-            after_v0.tile([P, T], F32, align_bytes=64, offset=0, name="v_pool0"),
-            after_v1.tile([P, T], F32, align_bytes=64, offset=0, name="v_pool1"),
-        ]
+        a_pool = after_a.tile([P, T], F32, align_bytes=64, offset=0, name="a_pool")
+        b_pool = held.tile([P, T], F32, name="b_pool")
+        c_pool = after_c.tile([P, T], F32, align_bytes=64, offset=0, name="c_pool")
         vs_pool = held.tile([P, T], F32, name="vs_pool")
         q_raw = after_q.tile([P, PACK, NQ], F32, align_bytes=64, offset=0, name="q_raw")
         sink_col = held.tile([P, 1], F32, name="sink_col")
         ident = held.tile([P, P], F32, name="ident")
 
-        nc.vector.memset(vs_pool[:], 0.0)
+        for window in (vs_pool, a_pool, c_pool):
+            nc.vector.memset(window[:], 0.0)
         make_identity(nc, ident[:])
 
         k_rows = kT.rearrange("(p j) t -> p j t", j=PACK)
@@ -62,14 +62,15 @@ def tile_attend_x_cap_sink_kernel(tc, qT, kT, vT, vs, sink, offs, out):
         nc.sync.dma_start(k_pool[2][:], k_rows[:, 2, :])
         nc.sync.dma_start(k_pool[3][:], k_rows[:, 3, :])
         nc.sync.dma_start(q_raw[:], qT[0].rearrange("(p j) w -> p j w", j=PACK))
-        nc.sync.dma_start(v_pool[0][:], vT[0:P, :])
-        nc.sync.dma_start(v_pool[1][:], vT[P : 2 * P, :])
+        nc.sync.dma_start(a_pool[0:P:2, :], vT[P : P + HALF, :])
+        nc.sync.dma_start(b_pool[:], vT[0:P, :])
+        nc.sync.dma_start(c_pool[0:P:2, :], vT[P + HALF : DV, :])
 
         def gather(dealt, window, first, count):
-            nc.vector.tensor_copy(
-                dealt.rearrange("p (g u s i) -> p g s u i", u=PAIR, s=P, i=PAIR),
-                window[:].indirect(offsets[:, first // LIST_ROWS : (first + count) // LIST_ROWS]),
-            )
+            nc.vector.tensor_copy(dealt, window[:].indirect(offsets[:, first // LIST_ROWS : (first + count) // LIST_ROWS]))
+
+        def deal(columns):
+            return columns.rearrange("p (g u s i) -> p g s u i", u=PAIR, s=P, i=PAIR)
 
         def quantise(codes, scales, grouped):
             nc.vector.quantize_mx(out=codes.bitcast(FP8X4), scales=scales, in_=grouped)
@@ -85,22 +86,24 @@ def tile_attend_x_cap_sink_kernel(tc, qT, kT, vT, vs, sink, offs, out):
                 stop=stop,
             )
 
-        def turn(dealt, grouped, bank):
+        def turn(dealt, grouped, bank, step):
             turned = banks.tile([P, PAIR, P], F32, tag=bank, name="turned")
             for u in range(PAIR):
                 nc.tensor.transpose(turned[:, u, :], dealt[u].bitcast(F32), ident[:])
             nc.scalar.copy(
-                grouped.bitcast(F32).rearrange("p (e u) -> p e u", u=PAIR), turned[:].rearrange("p u e -> p e u")
+                grouped.bitcast(F32).rearrange("p (e u) -> p e u", u=PAIR),
+                turned[:, :, 0:P:step].rearrange("p u e -> p e u"),
             )
 
         def piece(i):
             return slice(i * PIECE, (i + 1) * PIECE)
 
         k_grouped = held.tile([P, N, PACK], BF16, align_bytes=64, name="k_grouped")
-        k_picked = [held.tile([P, N], BF16, name=f"k_picked{j}") for j in range(PACK - 1)]
-        for j in range(PACK - 2):
-            gather(k_picked[j][:], k_pool[j], 0, N)
-            nc.scalar.copy(k_grouped[:, :, j], k_picked[j][:])
+        k_early = held.tile([P, PAIR, N], BF16, name="k_early")
+        k_late = held.tile([P, PASSES, PAIR, PASS], BF16, name="k_late")
+        for j in range(PAIR):
+            gather(deal(k_early[:, j, :]), k_pool[j], 0, N)
+        nc.scalar.copy(k_grouped[:, :, 0:PAIR], k_early[:].rearrange("p j s -> p s j"))
 
         vs_picked = held.tile([P, N], F32, name="vs_picked")
         vs_parts = held.tile([P, PASSES, PACK, QUARTERS], F32, name="vs_parts")
@@ -116,24 +119,19 @@ def tile_attend_x_cap_sink_kernel(tc, qT, kT, vT, vs, sink, offs, out):
         nc.gpsimd.tensor_tensor(vs_cols[:], vs_pairs[:, :, :, 0], vs_pairs[:, :, :, 1], ALU.add)
         vs_spread = []
         for g in range(PASSES):
-            vs_spread.append(banks.tile([NQ, PAIR, P, PAIR], F32, tag=f"bank{2 + g}", name="vs_spread"))
+            vs_spread.append(banks.tile([NQ, PAIR, P, PAIR], F32, tag=f"bank{4 + g}", name="vs_spread"))
             for t in range(PACK):
                 u, i = divmod(t, PAIR)
                 nc.tensor.transpose(vs_spread[g][:, u, :, i], vs_cols[:, g, t : t + 1].to_broadcast([P, NQ]), ident[:])
 
-        gather(k_picked[2][:], k_pool[2], 0, N)
-        nc.vector.tensor_copy(k_grouped[:, 0:PASS, 2], k_picked[2][:, 0:PASS])
-        nc.scalar.copy(k_grouped[:, PASS:N, 2], k_picked[2][:, PASS:N])
+        gather(k_late[:, :, 0, :].rearrange("p g (u s i) -> p g s u i", u=PAIR, i=PAIR), k_pool[2], 0, N)
 
-        capped = [
-            held.tile([NQ, PASS + 1], F32, name="capped0"),
-            after_exp.tile([NQ, PASS], F32, align_bytes=64, offset=0, name="capped1"),
-        ]
+        capped = [held.tile([NQ, PASS + 1 - g], F32, name=f"capped{g}") for g in range(2)]
+        places = [capped[0][:, piece(0)], capped[1][:, piece(0)], capped[1][:, piece(1)], capped[0][:, piece(1)]]
         nc.gpsimd.tensor_scalar(capped[0][:, PASS : PASS + 1], sink_col[:], 0.5, 0.0, ALU.mult, ALU.add)
 
-        k_last = [held.tile([P, PASS], BF16, name=f"k_last{g}") for g in range(PASSES)]
         for g in range(PASSES):
-            gather(k_last[g][:], k_pool[3], g * PASS, PASS)
+            gather(deal(k_late[:, g, 1, :]), k_pool[3], g * PASS, PASS)
 
         q_grouped = held.tile([P, NQ, PACK], BF16, align_bytes=64, name="q_grouped")
         q_codes = held.tile([P, NQ], U32, align_bytes=64, name="q_codes")
@@ -141,48 +139,43 @@ def tile_attend_x_cap_sink_kernel(tc, qT, kT, vT, vs, sink, offs, out):
         nc.gpsimd.tensor_scalar(q_grouped[:], q_raw[:].rearrange("p j w -> p w j"), 1.0, 0.0, ALU.mult, ALU.add)
         quantise(q_codes[:], q_scales[:], q_grouped[:].rearrange("p w j -> p (w j)"))
 
-        for i in range(PIECES):
-            g, u = divmod(i, PAIR)
-            place = nc.vector.tensor_copy if g == 0 else nc.scalar.copy
-            place(k_grouped[:, piece(i), 3], k_last[g][:, piece(u)])
+        def place(copy, first, last):
+            g = first // PASS
+            late = k_late[:, g, :, first - g * PASS : last - g * PASS]
+            copy(k_grouped[:, first:last, PAIR:PACK], late.rearrange("p j s -> p s j"))
 
-        for i in range(PIECES):
-            g, u = divmod(i, PAIR)
+        for first, last in ((0, PIECE), (PIECE, PASS), (PASS, SHARE)):
+            place(nc.scalar.copy, first, last)
+        place(nc.vector.tensor_copy, SHARE, N)
+
+        for i in (0, 3, 1, 2):
             k_codes = held.tile([P, PIECE], U32, align_bytes=64, name=f"k_codes{i}")
             k_scales = after_q.tile([P, PIECE], U8, align_bytes=64, offset=i * PIECE, name=f"k_scales{i}")
             quantise(k_codes[:], k_scales[:], k_grouped[:, piece(i), :].rearrange("p s j -> p (s j)"))
-            score = banks.tile([NQ, PIECE], F32, tag=f"bank{(0, 1, 4, 5)[i]}", name="score")
+            score = banks.tile([NQ, PIECE], F32, tag=f"bank{i}", name="score")
             multiply(score[:], q_codes[:], q_scales[:], k_codes[:], k_scales[:], True, True)
-            nc.scalar.activation(capped[g][:, piece(u)], score[:], ACT.Tanh, scale=0.5)
+            nc.scalar.activation(places[i], score[:], ACT.Tanh, scale=0.5)
 
-        doubled = [
-            held.tile([NQ, PASS + 1], F32, name="doubled0"),
-            after_max.tile([NQ, PASS], F32, offset=0, name="doubled1"),
-        ]
-        neg_max = [held.tile([NQ, 1], F32, name=f"neg_max{g}") for g in range(PASSES)]
-        for g in range(PASSES):
+        doubled = [held.tile([NQ, PASS + 1 - g], F32, name=f"doubled{g}") for g in range(2)]
+        neg_max = [held.tile([NQ, 1], F32, name=f"neg_max{g}") for g in range(2)]
+        for g in range(2):
             before = neg_max[g - 1][:] if g else None
             nc.vector.tensor_scalar(
                 doubled[g][:], capped[g][:], -2.0, before, ALU.mult, ALU.min, accum_out=neg_max[g][:]
             )
 
-        v0_picked = after_max.tile([P, N], BF16, offset=0, name="v0_picked")
-        gather(v0_picked[:], v_pool[0], 0, N)
+        a_picked = held.tile([P, N], BF16, name="a_picked")
+        gather(deal(a_picked[:]), a_pool, 0, N)
 
-        p = [held.tile([NQ, PIECE + (i == 1)], F32, name=f"p{i}") for i in range(PIECES)]
+        places[3] = capped[0][:, PIECE : PASS + 1]
+        p = [held.tile([NQ, PIECE + (i == 3)], F32, name=f"p{i}") for i in range(PIECES)]
         terms = held.tile([NQ, PIECES], F32, name="terms")
         for i in range(PIECES):
-            g, u = divmod(i, PAIR)
             nc.scalar.activation(
-                p[i][:],
-                capped[g][:, u * PIECE : (u + 1) * PIECE + (i == 1)],
-                ACT.Exp,
-                bias=neg_max[-1][:],
-                scale=2.0,
-                accum_out=terms[:, i : i + 1],
+                p[i][:], places[i], ACT.Exp, bias=neg_max[-1][:], scale=2.0, accum_out=terms[:, i : i + 1]
             )
         w_rows = [
-            after_v0.tile([NQ, PIECE], BF16, align_bytes=64, offset=2 * PIECE * i, name=f"w_rows{i}")
+            after_a.tile([NQ, PIECE], BF16, align_bytes=64, offset=2 * PIECE * i, name=f"w_rows{i}")
             for i in range(PIECES)
         ]
         for i in range(PIECES):
@@ -195,50 +188,51 @@ def tile_attend_x_cap_sink_kernel(tc, qT, kT, vT, vs, sink, offs, out):
         nc.gpsimd.tensor_tensor(term_pairs[:], terms[:, 0:2], terms[:, 2:4], ALU.add)
         nc.gpsimd.tensor_tensor(total[:], term_pairs[:, 0:1], term_pairs[:, 1:2], ALU.add)
 
-        v0_grouped = after_exp.tile([P, N], BF16, align_bytes=64, offset=0, name="v0_grouped")
-        w_grouped = held.tile([P, N], BF16, align_bytes=64, name="w_grouped")
+        ac_grouped = [held.tile([P, PASS], BF16, align_bytes=64, name=f"ac_grouped{g}") for g in range(PASSES)]
+        wb_grouped = [held.tile([P, 2 * PASS], BF16, align_bytes=64, name=f"wb_grouped{g}") for g in range(PASSES)]
         for g in range(PASSES):
-            halves = [v0_picked[:, piece(PAIR * g + u)] for u in range(PAIR)]
-            turn(halves, v0_grouped[:, g * PASS : (g + 1) * PASS], f"bank{6 + g}")
+            halves = [a_picked[:, piece(PAIR * g + u)] for u in range(PAIR)]
+            turn(halves, ac_grouped[g][:, 0:PIECE], f"bank{6 + g}", 2)
         for g in range(PASSES):
             halves = [w_rows[PAIR * g + u][:] for u in range(PAIR)]
-            turn(halves, w_grouped[:, g * PASS : (g + 1) * PASS], f"bank{g}")
+            turn(halves, wb_grouped[g][:, 0:PASS], f"bank{g}", 1)
 
-        v1_picked = [held.tile([P, PASS], BF16, name=f"v1_picked{g}") for g in range(PASSES)]
-        v1_grouped = [held.tile([P, PASS], BF16, align_bytes=64, name=f"v1_grouped{g}") for g in range(PASSES)]
+        b_picked = held.tile([P, N], BF16, name="b_picked")
+        gather(deal(b_picked[:]), b_pool, 0, N)
         for g in range(PASSES):
-            gather(v1_picked[g][:], v_pool[1], g * PASS, PASS)
-        for g in range(PASSES):
-            turn([v1_picked[g][:, piece(u)] for u in range(PAIR)], v1_grouped[g][:], f"bank{4 + g}")
+            halves = [b_picked[:, piece(PAIR * g + u)] for u in range(PAIR)]
+            turn(halves, wb_grouped[g][:, PASS : 2 * PASS], f"bank{2 + g}", 1)
 
-        w_codes = after_v1.tile([P, PASSES * NQ], U32, align_bytes=64, offset=0, name="w_codes")
-        w_scales = held.tile([P, PASSES * NQ], U8, align_bytes=64, name="w_scales")
-        v0_codes = after_v1.tile([P, PASSES * P], U32, align_bytes=64, offset=1024, name="v0_codes")
-        v0_scales = held.tile([P, PASSES * P], U8, align_bytes=64, name="v0_scales")
-        recip = after_v1.tile([NQ, 1], F32, align_bytes=64, offset=2048, name="recip")
-        v1_codes = [held.tile([P, P], U32, align_bytes=64, name=f"v1_codes{g}") for g in range(PASSES)]
-        v1_scales = [held.tile([P, P], U8, align_bytes=64, name=f"v1_scales{g}") for g in range(PASSES)]
-        quantise(v0_codes[:], v0_scales[:], v0_grouped[:])
-        quantise(w_codes[:], w_scales[:], w_grouped[:])
+        c_picked = [held.tile([P, PASS], BF16, name=f"c_picked{g}") for g in range(PASSES)]
+        for g in range(PASSES):
+            gather(deal(c_picked[g][:]), c_pool, g * PASS, PASS)
+        for g in range(PASSES):
+            turn([c_picked[g][:, piece(u)] for u in range(PAIR)], ac_grouped[g][:, PIECE:PASS], f"bank{4 + g}", 2)
+
+        wb_codes = [
+            after_c.tile([P, 2 * P], U32, align_bytes=64, offset=1024 * g, name=f"wb_codes{g}") for g in range(PASSES)
+        ]
+        wb_scales = [held.tile([P, 2 * P], U8, align_bytes=64, name=f"wb_scales{g}") for g in range(PASSES)]
+        recip = after_c.tile([NQ, 1], F32, align_bytes=64, offset=2048, name="recip")
+        ac_codes = [held.tile([P, P], U32, align_bytes=64, name=f"ac_codes{g}") for g in range(PASSES)]
+        ac_scales = [held.tile([P, P], U8, align_bytes=64, name=f"ac_scales{g}") for g in range(PASSES)]
+        quantise(wb_codes[0][:], wb_scales[0][:], wb_grouped[0][:])
         nc.vector.reciprocal(recip[:], total[:])
+        quantise(wb_codes[1][:], wb_scales[1][:], wb_grouped[1][:])
         for g in range(PASSES):
-            quantise(v1_codes[g][:], v1_scales[g][:], v1_grouped[g][:])
+            quantise(ac_codes[g][:], ac_scales[g][:], ac_grouped[g][:])
 
-        columns = [slice(g * P, (g + 1) * P) for g in range(PASSES)]
         values = [
-            [(v0_codes[:, c], v0_scales[:, c]) for c in columns],
-            [(v1_codes[g][:], v1_scales[g][:]) for g in range(PASSES)],
+            [(wb_codes[g][:, P : 2 * P], wb_scales[g][:, P : 2 * P]) for g in range(PASSES)],
+            [(ac_codes[g][:], ac_scales[g][:]) for g in range(PASSES)],
         ]
         for b in range(DV // P):
             y = banks.tile([NQ, P], F32, tag=f"bank{6 + b}", name="y")
             for g in range(PASSES):
-                multiply(y[:], w_codes[:, columns[g]], w_scales[:, columns[g]], *values[b][g], g == 0, g == PASSES - 1)
+                multiply(y[:], wb_codes[g][:, 0:P], wb_scales[g][:, 0:P], *values[b][g], g == 0, g == PASSES - 1)
             y_out = held.tile([NQ, P], F32, name=f"y_out{b}")
             if b == 0:
                 nc.scalar.activation(y_out[:], y[:], ACT.Copy, scale=recip[:])
             else:
                 nc.vector.tensor_scalar(y_out[:], y[:], recip[:], None, ALU.mult)
-            parts = 2 if b == 0 else 1
-            for h in range(parts):
-                first, last = h * P // parts, (h + 1) * P // parts
-                nc.sync.dma_start(out[0][:, b * P + first : b * P + last], y_out[:, first:last])
+            nc.sync.dma_start(out[0][:, b * P : (b + 1) * P], y_out[:])

@@ -33,6 +33,8 @@ def tile_attend_x_cap_sink_kernel(tc, qT, kT, vT, vs, sink, offs, out):
     with (
         tc.tile_pool(name="held", bufs=1) as held,
         tc.tile_pool(name="after_q", bufs=1) as after_q,
+        tc.tile_pool(name="after_scores", bufs=1) as after_scores,
+        tc.tile_pool(name="after_max", bufs=1) as after_max,
         tc.tile_pool(name="after_a", bufs=1) as after_a,
         tc.tile_pool(name="after_c", bufs=1) as after_c,
         tc.psum_pool(name="banks", bufs=1) as banks,
@@ -126,9 +128,8 @@ def tile_attend_x_cap_sink_kernel(tc, qT, kT, vT, vs, sink, offs, out):
 
         gather(k_late[:, :, 0, :].rearrange("p g (u s i) -> p g s u i", u=PAIR, i=PAIR), k_pool[2], 0, N)
 
-        capped = [held.tile([NQ, PASS + 1 - g], F32, name=f"capped{g}") for g in range(2)]
-        places = [capped[0][:, piece(0)], capped[1][:, piece(0)], capped[1][:, piece(1)], capped[0][:, piece(1)]]
-        nc.gpsimd.tensor_scalar(capped[0][:, PASS : PASS + 1], sink_col[:], 0.5, 0.0, ALU.mult, ALU.add)
+        capped = after_max.tile([NQ, N + 1], F32, align_bytes=64, offset=0, name="capped")
+        nc.gpsimd.tensor_scalar(capped[:, N : N + 1], sink_col[:], 0.5, 0.0, ALU.mult, ALU.add)
 
         for g in range(PASSES):
             gather(deal(k_late[:, g, 1, :]), k_pool[3], g * PASS, PASS)
@@ -148,47 +149,59 @@ def tile_attend_x_cap_sink_kernel(tc, qT, kT, vT, vs, sink, offs, out):
             place(nc.scalar.copy, first, last)
         place(nc.vector.tensor_copy, SHARE, N)
 
-        for i in (0, 3, 1, 2):
-            k_codes = held.tile([P, PIECE], U32, align_bytes=64, name=f"k_codes{i}")
-            k_scales = after_q.tile([P, PIECE], U8, align_bytes=64, offset=i * PIECE, name=f"k_scales{i}")
-            quantise(k_codes[:], k_scales[:], k_grouped[:, piece(i), :].rearrange("p s j -> p (s j)"))
-            score = banks.tile([NQ, PIECE], F32, tag=f"bank{i}", name="score")
+        runs = [(0, PIECE), (3 * PIECE, N), (SHARE, 3 * PIECE), (PIECE, PASS), (PASS, SHARE)]
+        for i, (first, last) in enumerate(runs):
+            if i == len(runs) - 1:
+                k_codes = after_scores.tile([P, last - first], U32, align_bytes=64, offset=0, name="k_codes_last")
+            else:
+                k_codes = held.tile([P, last - first], U32, align_bytes=64, name=f"k_codes{i}")
+            k_scales = after_q.tile([P, last - first], U8, align_bytes=64, offset=first, name=f"k_scales{i}")
+            quantise(k_codes[:], k_scales[:], k_grouped[:, first:last, :].rearrange("p s j -> p (s j)"))
+            score = banks.tile([NQ, last - first], F32, tag=f"bank{(0, 1, 2, 3, 7)[i]}", name="score")
             multiply(score[:], q_codes[:], q_scales[:], k_codes[:], k_scales[:], True, True)
-            nc.scalar.activation(places[i], score[:], ACT.Tanh, scale=0.5)
+            nc.scalar.activation(capped[:, first:last], score[:], ACT.Tanh, scale=0.5)
 
-        doubled = [held.tile([NQ, PASS + 1 - g], F32, name=f"doubled{g}") for g in range(2)]
-        neg_max = [held.tile([NQ, 1], F32, name=f"neg_max{g}") for g in range(2)]
-        for g in range(2):
-            before = neg_max[g - 1][:] if g else None
-            nc.vector.tensor_scalar(
-                doubled[g][:], capped[g][:], -2.0, before, ALU.mult, ALU.min, accum_out=neg_max[g][:]
+        lifted = after_scores.tile([NQ, N], F32, align_bytes=64, offset=0, name="lifted")
+        terms = held.tile([NQ, PIECES], F32, name="terms")
+        for i in range(PIECES):
+            nc.scalar.activation(
+                lifted[:, piece(i)], capped[:, piece(i)], ACT.Exp, scale=2.0, accum_out=terms[:, i : i + 1]
             )
 
         a_picked = held.tile([P, N], BF16, name="a_picked")
         gather(deal(a_picked[:]), a_pool, 0, N)
 
-        places[3] = capped[0][:, PIECE : PASS + 1]
-        p = [held.tile([NQ, PIECE + (i == 3)], F32, name=f"p{i}") for i in range(PIECES)]
-        terms = held.tile([NQ, PIECES], F32, name="terms")
-        for i in range(PIECES):
-            nc.scalar.activation(
-                p[i][:], places[i], ACT.Exp, bias=neg_max[-1][:], scale=2.0, accum_out=terms[:, i : i + 1]
-            )
-        w_rows = [
-            after_a.tile([NQ, PIECE], BF16, align_bytes=64, offset=2 * PIECE * i, name=f"w_rows{i}")
-            for i in range(PIECES)
-        ]
-        for i in range(PIECES):
+        half_max = after_a.tile([NQ, 1], F32, align_bytes=64, offset=0, name="half_max")
+        shrink = held.tile([NQ, 1], F32, name="shrink")
+        sink_term = held.tile([NQ, 1], F32, name="sink_term")
+        nc.vector.tensor_reduce(half_max[:], capped[:], mybir.AxisListType.X, ALU.max)
+        nc.scalar.activation(shrink[:], half_max[:], ACT.Exp, scale=-2.0)
+        nc.scalar.activation(sink_term[:], half_max[:], ACT.Exp, scale=-2.0, bias=sink_col[:])
+
+        def token_scales(i):
             g, u = divmod(i, PAIR)
-            nc.vector.tensor_tensor(
-                w_rows[i][:], p[i][:, 0:PIECE], vs_spread[g][:, u].rearrange("q s i -> q (s i)"), ALU.mult
-            )
+            return vs_spread[g][:, u].rearrange("q s i -> q (s i)")
+
+        w_rows = [held.tile([NQ, PIECE], BF16, align_bytes=64, name=f"w_rows{i}") for i in range(PIECES)]
+        for i in (0, 2, 3):
+            scaled = after_a.tile([NQ, PIECE], F32, align_bytes=64, offset=64 + 4 * PIECE * i, name=f"scaled{i}")
+            nc.vector.tensor_tensor(scaled[:], lifted[:, piece(i)], token_scales(i), ALU.mult)
+            nc.scalar.activation(w_rows[i][:], scaled[:], ACT.Copy, scale=shrink[:])
+        nc.vector.scalar_tensor_tensor(
+            w_rows[1][:], lifted[:, piece(1)], shrink[:], token_scales(1), ALU.mult, ALU.mult
+        )
+
         term_pairs = held.tile([NQ, 2], F32, name="term_pairs")
+        lifted_sum = held.tile([NQ, 1], F32, name="lifted_sum")
         total = held.tile([NQ, 1], F32, name="total")
         nc.gpsimd.tensor_tensor(term_pairs[:], terms[:, 0:2], terms[:, 2:4], ALU.add)
-        nc.gpsimd.tensor_tensor(total[:], term_pairs[:, 0:1], term_pairs[:, 1:2], ALU.add)
+        nc.gpsimd.tensor_tensor(lifted_sum[:], term_pairs[:, 0:1], term_pairs[:, 1:2], ALU.add)
+        nc.gpsimd.tensor_scalar(total[:], lifted_sum[:], shrink[:], sink_term[:], ALU.mult, ALU.add)
 
-        ac_grouped = [held.tile([P, PASS], BF16, align_bytes=64, name=f"ac_grouped{g}") for g in range(PASSES)]
+        ac_grouped = [
+            after_max.tile([P, PASS], BF16, align_bytes=64, offset=2 * PASS * g, name=f"ac_grouped{g}")
+            for g in range(PASSES)
+        ]
         wb_grouped = [held.tile([P, 2 * PASS], BF16, align_bytes=64, name=f"wb_grouped{g}") for g in range(PASSES)]
         for g in range(PASSES):
             halves = [a_picked[:, piece(PAIR * g + u)] for u in range(PAIR)]

@@ -34,24 +34,26 @@ def tile_attend_x_cap_sink_kernel(tc, qT, kT, vT, vs, sink, offs, out):
         tc.tile_pool(name="held", bufs=1) as held,
         tc.tile_pool(name="after_q", bufs=1) as after_q,
         tc.tile_pool(name="after_scores", bufs=1) as after_scores,
-        tc.tile_pool(name="after_max", bufs=1) as after_max,
+        tc.tile_pool(name="after_w", bufs=1) as after_w,
         tc.tile_pool(name="after_a", bufs=1) as after_a,
+        tc.tile_pool(name="after_b", bufs=1) as after_b,
         tc.tile_pool(name="after_c", bufs=1) as after_c,
         tc.psum_pool(name="banks", bufs=1) as banks,
     ):
         offsets = held.tile([P, N // LIST_ROWS], U16, name="offsets")
         k_pool = [held.tile([P, T], F32, name=f"k_pool{j}") for j in range(PACK)]
         a_pool = after_a.tile([P, T], F32, align_bytes=64, offset=0, name="a_pool")
-        b_pool = held.tile([P, T], F32, name="b_pool")
+        b_pool = after_b.tile([P, T], F32, align_bytes=64, offset=0, name="b_pool")
         c_pool = after_c.tile([P, T], F32, align_bytes=64, offset=0, name="c_pool")
         vs_pool = held.tile([P, T], F32, name="vs_pool")
         q_raw = after_q.tile([P, PACK, NQ], F32, align_bytes=64, offset=0, name="q_raw")
         sink_col = held.tile([P, 1], F32, name="sink_col")
         ident = held.tile([P, P], F32, name="ident")
 
-        for window in (vs_pool, a_pool, c_pool):
+        for window in (vs_pool, a_pool):
             nc.vector.memset(window[:], 0.0)
         make_identity(nc, ident[:])
+        nc.gpsimd.memset(c_pool[:], 0.0)
 
         k_rows = kT.rearrange("(p j) t -> p j t", j=PACK)
         nc.sync.dma_start(k_pool[0][:], k_rows[:, 0, :])
@@ -128,7 +130,7 @@ def tile_attend_x_cap_sink_kernel(tc, qT, kT, vT, vs, sink, offs, out):
 
         gather(k_late[:, :, 0, :].rearrange("p g (u s i) -> p g s u i", u=PAIR, i=PAIR), k_pool[2], 0, N)
 
-        capped = after_max.tile([NQ, N + 1], F32, align_bytes=64, offset=0, name="capped")
+        capped = held.tile([NQ, N + 1], F32, name="capped")
         nc.gpsimd.tensor_scalar(capped[:, N : N + 1], sink_col[:], 0.5, 0.0, ALU.mult, ALU.add)
 
         for g in range(PASSES):
@@ -182,14 +184,21 @@ def tile_attend_x_cap_sink_kernel(tc, qT, kT, vT, vs, sink, offs, out):
             g, u = divmod(i, PAIR)
             return vs_spread[g][:, u].rearrange("q s i -> q (s i)")
 
-        w_rows = [held.tile([NQ, PIECE], BF16, align_bytes=64, name=f"w_rows{i}") for i in range(PIECES)]
-        for i in (0, 2, 3):
+        w_rows = [
+            after_w.tile([NQ, PIECE], BF16, align_bytes=64, offset=3 * PIECE, name="w_rows1")
+            if i == 1
+            else held.tile([NQ, PIECE], BF16, name=f"w_rows{i}")
+            for i in range(PIECES)
+        ]
+        for i in (0, 2, 1, 3):
+            if i == 1:
+                nc.vector.scalar_tensor_tensor(
+                    w_rows[i][:], lifted[:, piece(i)], shrink[:], token_scales(i), ALU.mult, ALU.mult
+                )
+                continue
             scaled = after_a.tile([NQ, PIECE], F32, align_bytes=64, offset=64 + 4 * PIECE * i, name=f"scaled{i}")
             nc.vector.tensor_tensor(scaled[:], lifted[:, piece(i)], token_scales(i), ALU.mult)
             nc.scalar.activation(w_rows[i][:], scaled[:], ACT.Copy, scale=shrink[:])
-        nc.vector.scalar_tensor_tensor(
-            w_rows[1][:], lifted[:, piece(1)], shrink[:], token_scales(1), ALU.mult, ALU.mult
-        )
 
         term_pairs = held.tile([NQ, 2], F32, name="term_pairs")
         lifted_sum = held.tile([NQ, 1], F32, name="lifted_sum")
@@ -199,22 +208,28 @@ def tile_attend_x_cap_sink_kernel(tc, qT, kT, vT, vs, sink, offs, out):
         nc.gpsimd.tensor_scalar(total[:], lifted_sum[:], shrink[:], sink_term[:], ALU.mult, ALU.add)
 
         ac_grouped = [
-            after_max.tile([P, PASS], BF16, align_bytes=64, offset=2 * PASS * g, name=f"ac_grouped{g}")
+            after_w.tile([P, PASS], BF16, align_bytes=64, offset=2 * PASS * g, name=f"ac_grouped{g}")
             for g in range(PASSES)
         ]
-        wb_grouped = [held.tile([P, 2 * PASS], BF16, align_bytes=64, name=f"wb_grouped{g}") for g in range(PASSES)]
+        w0_grouped = held.tile([P, PASS], BF16, align_bytes=64, name="w0_grouped")
+        b0_grouped = held.tile([P, PASS], BF16, align_bytes=64, name="b0_grouped")
+        wb1_grouped = held.tile([P, 2 * PASS], BF16, align_bytes=64, name="wb1_grouped")
+        turn([w_rows[u][:] for u in range(PAIR)], w0_grouped[:], "bank0", 1)
         for g in range(PASSES):
             halves = [a_picked[:, piece(PAIR * g + u)] for u in range(PAIR)]
             turn(halves, ac_grouped[g][:, 0:PIECE], f"bank{6 + g}", 2)
-        for g in range(PASSES):
-            halves = [w_rows[PAIR * g + u][:] for u in range(PAIR)]
-            turn(halves, wb_grouped[g][:, 0:PASS], f"bank{g}", 1)
+        turn([w_rows[PAIR + u][:] for u in range(PAIR)], wb1_grouped[:, 0:PASS], "bank1", 1)
 
         b_picked = held.tile([P, N], BF16, name="b_picked")
         gather(deal(b_picked[:]), b_pool, 0, N)
-        for g in range(PASSES):
-            halves = [b_picked[:, piece(PAIR * g + u)] for u in range(PAIR)]
-            turn(halves, wb_grouped[g][:, PASS : 2 * PASS], f"bank{2 + g}", 1)
+        for g, grouped in enumerate((b0_grouped[:], wb1_grouped[:, PASS : 2 * PASS])):
+            turn([b_picked[:, piece(PAIR * g + u)] for u in range(PAIR)], grouped, f"bank{2 + g}", 1)
+
+        recip = after_b.tile([NQ, 1], F32, align_bytes=64, offset=0, name="recip")
+        w0_codes = after_b.tile([P, P], U32, align_bytes=64, offset=64, name="w0_codes")
+        w0_scales = held.tile([P, P], U8, align_bytes=64, name="w0_scales")
+        nc.vector.reciprocal(recip[:], total[:])
+        quantise(w0_codes[:], w0_scales[:], w0_grouped[:])
 
         c_picked = [held.tile([P, PASS], BF16, name=f"c_picked{g}") for g in range(PASSES)]
         for g in range(PASSES):
@@ -222,27 +237,26 @@ def tile_attend_x_cap_sink_kernel(tc, qT, kT, vT, vs, sink, offs, out):
         for g in range(PASSES):
             turn([c_picked[g][:, piece(u)] for u in range(PAIR)], ac_grouped[g][:, PIECE:PASS], f"bank{4 + g}", 2)
 
-        wb_codes = [
-            after_c.tile([P, 2 * P], U32, align_bytes=64, offset=1024 * g, name=f"wb_codes{g}") for g in range(PASSES)
-        ]
-        wb_scales = [held.tile([P, 2 * P], U8, align_bytes=64, name=f"wb_scales{g}") for g in range(PASSES)]
-        recip = after_c.tile([NQ, 1], F32, align_bytes=64, offset=2048, name="recip")
+        b0_codes = after_c.tile([P, P], U32, align_bytes=64, offset=0, name="b0_codes")
+        b0_scales = held.tile([P, P], U8, align_bytes=64, name="b0_scales")
+        wb1_codes = after_c.tile([P, 2 * P], U32, align_bytes=64, offset=4 * P, name="wb1_codes")
+        wb1_scales = held.tile([P, 2 * P], U8, align_bytes=64, name="wb1_scales")
         ac_codes = [held.tile([P, P], U32, align_bytes=64, name=f"ac_codes{g}") for g in range(PASSES)]
         ac_scales = [held.tile([P, P], U8, align_bytes=64, name=f"ac_scales{g}") for g in range(PASSES)]
-        quantise(wb_codes[0][:], wb_scales[0][:], wb_grouped[0][:])
-        nc.vector.reciprocal(recip[:], total[:])
-        quantise(wb_codes[1][:], wb_scales[1][:], wb_grouped[1][:])
+        quantise(b0_codes[:], b0_scales[:], b0_grouped[:])
+        quantise(wb1_codes[:], wb1_scales[:], wb1_grouped[:])
         for g in range(PASSES):
             quantise(ac_codes[g][:], ac_scales[g][:], ac_grouped[g][:])
 
+        weights = [(w0_codes[:], w0_scales[:]), (wb1_codes[:, 0:P], wb1_scales[:, 0:P])]
         values = [
-            [(wb_codes[g][:, P : 2 * P], wb_scales[g][:, P : 2 * P]) for g in range(PASSES)],
+            [(b0_codes[:], b0_scales[:]), (wb1_codes[:, P : 2 * P], wb1_scales[:, P : 2 * P])],
             [(ac_codes[g][:], ac_scales[g][:]) for g in range(PASSES)],
         ]
         for b in range(DV // P):
             y = banks.tile([NQ, P], F32, tag=f"bank{6 + b}", name="y")
             for g in range(PASSES):
-                multiply(y[:], wb_codes[g][:, 0:P], wb_scales[g][:, 0:P], *values[b][g], g == 0, g == PASSES - 1)
+                multiply(y[:], *weights[g], *values[b][g], g == 0, g == PASSES - 1)
             y_out = held.tile([NQ, P], F32, name=f"y_out{b}")
             if b == 0:
                 nc.scalar.activation(y_out[:], y[:], ACT.Copy, scale=recip[:])

@@ -34,7 +34,6 @@ def tile_attend_x_cap_sink_kernel(tc, qT, kT, vT, vs, sink, offs, out):
         tc.tile_pool(name="held", bufs=1) as held,
         tc.tile_pool(name="after_q", bufs=1) as after_q,
         tc.tile_pool(name="after_scores", bufs=1) as after_scores,
-        tc.tile_pool(name="after_w", bufs=1) as after_w,
         tc.tile_pool(name="after_a", bufs=1) as after_a,
         tc.tile_pool(name="after_b", bufs=1) as after_b,
         tc.tile_pool(name="after_c", bufs=1) as after_c,
@@ -163,42 +162,39 @@ def tile_attend_x_cap_sink_kernel(tc, qT, kT, vT, vs, sink, offs, out):
             multiply(score[:], q_codes[:], q_scales[:], k_codes[:], k_scales[:], True, True)
             nc.scalar.activation(capped[:, first:last], score[:], ACT.Tanh, scale=0.5)
 
-        lifted = after_scores.tile([NQ, N], F32, align_bytes=64, offset=0, name="lifted")
+        early = after_scores.tile([NQ, 3 * PIECE], F32, align_bytes=64, offset=0, name="early")
+        half_max = after_a.tile([NQ, 1], F32, align_bytes=64, offset=0, name="half_max")
+        late = after_a.tile([NQ, PIECE], F32, align_bytes=64, offset=0, name="late")
+        lifted = [early[:, piece(i)] for i in range(3)] + [late[:]]
         terms = held.tile([NQ, PIECES], F32, name="terms")
-        for i in range(PIECES):
-            nc.scalar.activation(
-                lifted[:, piece(i)], capped[:, piece(i)], ACT.Exp, scale=2.0, accum_out=terms[:, i : i + 1]
-            )
+
+        def lift(i):
+            nc.scalar.activation(lifted[i], capped[:, piece(i)], ACT.Exp, scale=2.0, accum_out=terms[:, i : i + 1])
+
+        for i in (0, 2, 1):
+            lift(i)
 
         a_picked = held.tile([P, N], BF16, name="a_picked")
         gather(deal(a_picked[:]), a_pool, 0, N)
 
-        half_max = after_a.tile([NQ, 1], F32, align_bytes=64, offset=0, name="half_max")
         shrink = held.tile([NQ, 1], F32, name="shrink")
         sink_term = held.tile([NQ, 1], F32, name="sink_term")
         nc.vector.tensor_reduce(half_max[:], capped[:], mybir.AxisListType.X, ALU.max)
         nc.scalar.activation(shrink[:], half_max[:], ACT.Exp, scale=-2.0)
         nc.scalar.activation(sink_term[:], half_max[:], ACT.Exp, scale=-2.0, bias=sink_col[:])
+        lift(3)
 
         def token_scales(i):
             g, u = divmod(i, PAIR)
             return vs_spread[g][:, u].rearrange("q s i -> q (s i)")
 
-        w_rows = [
-            after_w.tile([NQ, PIECE], BF16, align_bytes=64, offset=3 * PIECE, name="w_rows1")
-            if i == 1
-            else held.tile([NQ, PIECE], BF16, name=f"w_rows{i}")
-            for i in range(PIECES)
-        ]
-        for i in (0, 2, 1, 3):
-            if i == 1:
-                nc.vector.scalar_tensor_tensor(
-                    w_rows[i][:], lifted[:, piece(i)], shrink[:], token_scales(i), ALU.mult, ALU.mult
-                )
-                continue
-            scaled = after_a.tile([NQ, PIECE], F32, align_bytes=64, offset=64 + 4 * PIECE * i, name=f"scaled{i}")
-            nc.vector.tensor_tensor(scaled[:], lifted[:, piece(i)], token_scales(i), ALU.mult)
+        w_rows = [held.tile([NQ, PIECE], BF16, name=f"w_rows{i}") for i in range(PIECES)]
+        for i in (0, 2):
+            scaled = after_a.tile([NQ, PIECE], F32, align_bytes=64, offset=4 * PIECE * (i + 1), name=f"scaled{i}")
+            nc.vector.tensor_tensor(scaled[:], lifted[i], token_scales(i), ALU.mult)
             nc.scalar.activation(w_rows[i][:], scaled[:], ACT.Copy, scale=shrink[:])
+        for i in (1, 3):
+            nc.vector.scalar_tensor_tensor(w_rows[i][:], lifted[i], shrink[:], token_scales(i), ALU.mult, ALU.mult)
 
         term_pairs = held.tile([NQ, 2], F32, name="term_pairs")
         lifted_sum = held.tile([NQ, 1], F32, name="lifted_sum")
@@ -207,17 +203,19 @@ def tile_attend_x_cap_sink_kernel(tc, qT, kT, vT, vs, sink, offs, out):
         nc.gpsimd.tensor_tensor(lifted_sum[:], term_pairs[:, 0:1], term_pairs[:, 1:2], ALU.add)
         nc.gpsimd.tensor_scalar(total[:], lifted_sum[:], shrink[:], sink_term[:], ALU.mult, ALU.add)
 
-        ac_grouped = [
-            after_w.tile([P, PASS], BF16, align_bytes=64, offset=2 * PASS * g, name=f"ac_grouped{g}")
-            for g in range(PASSES)
-        ]
-        w0_grouped = held.tile([P, PASS], BF16, align_bytes=64, name="w0_grouped")
+        aw_grouped = held.tile([P, 2 * PASS], BF16, align_bytes=64, name="aw_grouped")
         b0_grouped = held.tile([P, PASS], BF16, align_bytes=64, name="b0_grouped")
         wb1_grouped = held.tile([P, 2 * PASS], BF16, align_bytes=64, name="wb1_grouped")
-        turn([w_rows[u][:] for u in range(PAIR)], w0_grouped[:], "bank0", 1)
-        for g in range(PASSES):
-            halves = [a_picked[:, piece(PAIR * g + u)] for u in range(PAIR)]
-            turn(halves, ac_grouped[g][:, 0:PIECE], f"bank{6 + g}", 2)
+        c_grouped = [held.tile([P, PIECE], BF16, align_bytes=64, name=f"c_grouped{g}") for g in range(PASSES)]
+        a_turned = banks.tile([P, PASSES, PAIR, P], F32, tag="bank6", name="a_turned")
+        for i in range(PIECES):
+            g, u = divmod(i, PAIR)
+            nc.tensor.transpose(a_turned[:, g, u, :], a_picked[:, piece(i)].bitcast(F32), ident[:])
+        nc.scalar.copy(
+            aw_grouped[:, 0:PASS].bitcast(F32).rearrange("p (g e u) -> p g e u", g=PASSES, u=PAIR),
+            a_turned[:, :, :, 0:P:2].rearrange("p g u e -> p g e u"),
+        )
+        turn([w_rows[u][:] for u in range(PAIR)], aw_grouped[:, PASS : 2 * PASS], "bank0", 1)
         turn([w_rows[PAIR + u][:] for u in range(PAIR)], wb1_grouped[:, 0:PASS], "bank1", 1)
 
         b_picked = held.tile([P, N], BF16, name="b_picked")
@@ -226,40 +224,44 @@ def tile_attend_x_cap_sink_kernel(tc, qT, kT, vT, vs, sink, offs, out):
             turn([b_picked[:, piece(PAIR * g + u)] for u in range(PAIR)], grouped, f"bank{2 + g}", 1)
 
         recip = after_b.tile([NQ, 1], F32, align_bytes=64, offset=0, name="recip")
-        w0_codes = after_b.tile([P, P], U32, align_bytes=64, offset=64, name="w0_codes")
-        w0_scales = held.tile([P, P], U8, align_bytes=64, name="w0_scales")
+        aw_codes = after_b.tile([P, 2 * P], U32, align_bytes=64, offset=64, name="aw_codes")
+        aw_scales = held.tile([P, 2 * P], U8, align_bytes=64, name="aw_scales")
         nc.vector.reciprocal(recip[:], total[:])
-        quantise(w0_codes[:], w0_scales[:], w0_grouped[:])
+        quantise(aw_codes[:], aw_scales[:], aw_grouped[:])
 
         c_picked = [held.tile([P, PASS], BF16, name=f"c_picked{g}") for g in range(PASSES)]
         for g in range(PASSES):
             gather(deal(c_picked[g][:]), c_pool, g * PASS, PASS)
         for g in range(PASSES):
-            turn([c_picked[g][:, piece(u)] for u in range(PAIR)], ac_grouped[g][:, PIECE:PASS], f"bank{4 + g}", 2)
+            turn([c_picked[g][:, piece(u)] for u in range(PAIR)], c_grouped[g][:], f"bank{4 + g}", 2)
 
-        b0_codes = after_c.tile([P, P], U32, align_bytes=64, offset=0, name="b0_codes")
-        b0_scales = held.tile([P, P], U8, align_bytes=64, name="b0_scales")
-        wb1_codes = after_c.tile([P, 2 * P], U32, align_bytes=64, offset=4 * P, name="wb1_codes")
-        wb1_scales = held.tile([P, 2 * P], U8, align_bytes=64, name="wb1_scales")
-        ac_codes = [held.tile([P, P], U32, align_bytes=64, name=f"ac_codes{g}") for g in range(PASSES)]
-        ac_scales = [held.tile([P, P], U8, align_bytes=64, name=f"ac_scales{g}") for g in range(PASSES)]
-        quantise(b0_codes[:], b0_scales[:], b0_grouped[:])
-        quantise(wb1_codes[:], wb1_scales[:], wb1_grouped[:])
-        for g in range(PASSES):
-            quantise(ac_codes[g][:], ac_scales[g][:], ac_grouped[g][:])
+        late_codes = after_c.tile([P, 4 * P], U32, align_bytes=64, offset=0, name="late_codes")
+        late_scales = held.tile([P, 4 * P], U8, align_bytes=64, name="late_scales")
 
-        weights = [(w0_codes[:], w0_scales[:]), (wb1_codes[:, 0:P], wb1_scales[:, 0:P])]
-        values = [
-            [(b0_codes[:], b0_scales[:]), (wb1_codes[:, P : 2 * P], wb1_scales[:, P : 2 * P])],
-            [(ac_codes[g][:], ac_scales[g][:]) for g in range(PASSES)],
-        ]
-        for b in range(DV // P):
-            y = banks.tile([NQ, P], F32, tag=f"bank{6 + b}", name="y")
-            for g in range(PASSES):
-                multiply(y[:], *weights[g], *values[b][g], g == 0, g == PASSES - 1)
-            y_out = held.tile([NQ, P], F32, name=f"y_out{b}")
-            if b == 0:
-                nc.scalar.activation(y_out[:], y[:], ACT.Copy, scale=recip[:])
-            else:
-                nc.vector.tensor_scalar(y_out[:], y[:], recip[:], None, ALU.mult)
-            nc.sync.dma_start(out[0][:, b * P : (b + 1) * P], y_out[:])
+        def early_columns(first, count=P):
+            return aw_codes[:, first : first + count], aw_scales[:, first : first + count]
+
+        def late_columns(first, count=P):
+            return late_codes[:, first : first + count], late_scales[:, first : first + count]
+
+        quantise(*late_columns(P), b0_grouped[:])
+        quantise(*late_columns(2 * P, 2 * P), wb1_grouped[:])
+        quantise(*late_columns(HALF, HALF), c_grouped[0][:])
+        quantise(*late_columns(0, HALF), c_grouped[1][:])
+
+        weights = [early_columns(P), late_columns(2 * P)]
+        y_ba = banks.tile([NQ, 2 * P], F32, tag="bank7", name="y_ba")
+        multiply(y_ba[:, P : 2 * P], *weights[0], *early_columns(0), True, False)
+        multiply(y_ba[:, 0:P], *weights[0], *late_columns(P), False, False)
+        multiply(y_ba[:, 0:P], *weights[1], *late_columns(3 * P), False, False)
+        multiply(y_ba[:, P : 2 * P], *weights[1], *early_columns(HALF), False, True)
+        ba_out = held.tile([NQ, P + HALF], F32, name="ba_out")
+        nc.scalar.activation(ba_out[:], y_ba[:, 0 : P + HALF], ACT.Copy, scale=recip[:])
+        nc.sync.dma_start(out[0][:, 0 : P + HALF], ba_out[:])
+
+        y_c = banks.tile([NQ, P], F32, tag="bank6", name="y_c")
+        multiply(y_c[:], *weights[0], *late_columns(HALF), True, False)
+        multiply(y_c[:], *weights[1], *late_columns(0), False, True)
+        c_out = held.tile([NQ, HALF], F32, name="c_out")
+        nc.vector.tensor_scalar(c_out[:], y_c[:, 0:HALF], recip[:], None, ALU.mult)
+        nc.sync.dma_start(out[0][:, P + HALF : DV], c_out[:])

@@ -1,3 +1,5 @@
+import math
+
 import concourse.mybir as mybir
 from concourse.masks import make_identity
 
@@ -34,6 +36,7 @@ def tile_attend_x_cap_sink_kernel(tc, qT, kT, vT, vs, sink, offs, out):
         tc.tile_pool(name="held", bufs=1) as held,
         tc.tile_pool(name="after_q", bufs=1) as after_q,
         tc.tile_pool(name="after_scores", bufs=1) as after_scores,
+        tc.tile_pool(name="after_max", bufs=1) as after_max,
         tc.tile_pool(name="after_a", bufs=1) as after_a,
         tc.tile_pool(name="after_b", bufs=1) as after_b,
         tc.tile_pool(name="after_c", bufs=1) as after_c,
@@ -129,8 +132,10 @@ def tile_attend_x_cap_sink_kernel(tc, qT, kT, vT, vs, sink, offs, out):
 
         gather(k_late[:, :, 0, :].rearrange("p g (u s i) -> p g s u i", u=PAIR, i=PAIR), k_pool[2], 0, N)
 
-        capped = held.tile([NQ, N + 1], F32, name="capped")
+        capped = after_max.tile([NQ, N + 1], F32, align_bytes=64, offset=0, name="capped")
+        sink_less = held.tile([NQ, 1], F32, name="sink_less")
         nc.gpsimd.tensor_scalar(capped[:, N : N + 1], sink_col[:], 0.5, 0.0, ALU.mult, ALU.add)
+        nc.gpsimd.tensor_scalar(sink_less[:], sink_col[:], 1.0, -math.log(PIECES), ALU.mult, ALU.add)
 
         for g in range(PASSES):
             gather(deal(k_late[:, g, 1, :]), k_pool[3], g * PASS, PASS)
@@ -162,27 +167,21 @@ def tile_attend_x_cap_sink_kernel(tc, qT, kT, vT, vs, sink, offs, out):
             multiply(score[:], q_codes[:], q_scales[:], k_codes[:], k_scales[:], True, True)
             nc.scalar.activation(capped[:, first:last], score[:], ACT.Tanh, scale=0.5)
 
-        early = after_scores.tile([NQ, 3 * PIECE], F32, align_bytes=64, offset=0, name="early")
-        half_max = after_a.tile([NQ, 1], F32, align_bytes=64, offset=0, name="half_max")
-        late = after_a.tile([NQ, PIECE], F32, align_bytes=64, offset=0, name="late")
-        lifted = [early[:, piece(i)] for i in range(3)] + [late[:]]
+        lifted_all = after_scores.tile([NQ, N], F32, align_bytes=64, offset=0, name="lifted_all")
+        lifted = [lifted_all[:, piece(i)] for i in range(PIECES)]
         terms = held.tile([NQ, PIECES], F32, name="terms")
-
-        def lift(i):
+        for i in (0, 2, 1, 3):
             nc.scalar.activation(lifted[i], capped[:, piece(i)], ACT.Exp, scale=2.0, accum_out=terms[:, i : i + 1])
-
-        for i in (0, 2, 1):
-            lift(i)
 
         a_picked = held.tile([P, N], BF16, name="a_picked")
         gather(deal(a_picked[:]), a_pool, 0, N)
 
+        half_max = after_a.tile([NQ, 1], F32, align_bytes=64, offset=0, name="half_max")
         shrink = held.tile([NQ, 1], F32, name="shrink")
-        sink_term = held.tile([NQ, 1], F32, name="sink_term")
+        sink_share = held.tile([NQ, 1], F32, name="sink_share")
         nc.vector.tensor_reduce(half_max[:], capped[:], mybir.AxisListType.X, ALU.max)
         nc.scalar.activation(shrink[:], half_max[:], ACT.Exp, scale=-2.0)
-        nc.scalar.activation(sink_term[:], half_max[:], ACT.Exp, scale=-2.0, bias=sink_col[:])
-        lift(3)
+        nc.scalar.activation(sink_share[:], half_max[:], ACT.Exp, scale=-2.0, bias=sink_less[:])
 
         def token_scales(i):
             g, u = divmod(i, PAIR)
@@ -196,14 +195,13 @@ def tile_attend_x_cap_sink_kernel(tc, qT, kT, vT, vs, sink, offs, out):
         for i in (1, 3):
             nc.vector.scalar_tensor_tensor(w_rows[i][:], lifted[i], shrink[:], token_scales(i), ALU.mult, ALU.mult)
 
-        term_pairs = held.tile([NQ, 2], F32, name="term_pairs")
-        lifted_sum = held.tile([NQ, 1], F32, name="lifted_sum")
+        shares = held.tile([NQ, PIECES], F32, name="shares")
         total = held.tile([NQ, 1], F32, name="total")
-        nc.gpsimd.tensor_tensor(term_pairs[:], terms[:, 0:2], terms[:, 2:4], ALU.add)
-        nc.gpsimd.tensor_tensor(lifted_sum[:], term_pairs[:, 0:1], term_pairs[:, 1:2], ALU.add)
-        nc.gpsimd.tensor_scalar(total[:], lifted_sum[:], shrink[:], sink_term[:], ALU.mult, ALU.add)
+        nc.scalar.activation(
+            shares[:], terms[:], ACT.Identity, scale=shrink[:], bias=sink_share[:], accum_out=total[:]
+        )
 
-        aw_grouped = held.tile([P, 2 * PASS], BF16, align_bytes=64, name="aw_grouped")
+        aw_grouped = after_max.tile([P, 2 * PASS], BF16, align_bytes=64, offset=0, name="aw_grouped")
         b0_grouped = held.tile([P, PASS], BF16, align_bytes=64, name="b0_grouped")
         wb1_grouped = held.tile([P, 2 * PASS], BF16, align_bytes=64, name="wb1_grouped")
         c_grouped = [held.tile([P, PIECE], BF16, align_bytes=64, name=f"c_grouped{g}") for g in range(PASSES)]

@@ -16,6 +16,7 @@ QUARTERS = 4
 PORT_ROWS = 4
 HALF = P // 2
 SHARE = 640
+BURST = 256
 
 FLOPS = 2 * NQ * N * (D + DV)
 BYTES = 4 * (D * T + DV * T + D * NQ + T + NQ + NQ * DV) + 2 * P * (N // LIST_ROWS)
@@ -43,12 +44,12 @@ def tile_attend_x_cap_sink_kernel(tc, qT, kT, vT, vs, sink, offs, out):
         tc.psum_pool(name="banks", bufs=1) as banks,
     ):
         offsets = held.tile([P, N // LIST_ROWS], U16, name="offsets")
-        k_pool = [held.tile([P, T], F32, name=f"k_pool{j}") for j in range(PACK)]
-        a_pool = after_a.tile([P, T], F32, align_bytes=64, offset=0, name="a_pool")
-        b_pool = after_b.tile([P, T], F32, align_bytes=64, offset=0, name="b_pool")
-        c_pool = after_c.tile([P, T], F32, align_bytes=64, offset=0, name="c_pool")
-        vs_pool = held.tile([P, T], F32, name="vs_pool")
-        q_raw = after_q.tile([P, PACK, NQ], F32, align_bytes=64, offset=0, name="q_raw")
+        k_pool = [held.tile([P, T], F32, align_bytes=BURST, name=f"k_pool{j}") for j in range(PACK)]
+        a_pool = after_a.tile([P, T], F32, align_bytes=BURST, offset=0, name="a_pool")
+        b_pool = after_b.tile([P, T], F32, align_bytes=BURST, offset=0, name="b_pool")
+        c_pool = after_c.tile([P, T], F32, align_bytes=BURST, offset=0, name="c_pool")
+        vs_pool = held.tile([P, T], F32, align_bytes=BURST, name="vs_pool")
+        q_raw = after_q.tile([P, PACK, NQ], F32, align_bytes=BURST, offset=0, name="q_raw")
         sink_col = held.tile([P, 1], F32, name="sink_col")
         ident = held.tile([P, P], F32, name="ident")
 
@@ -253,13 +254,13 @@ def tile_attend_x_cap_sink_kernel(tc, qT, kT, vT, vs, sink, offs, out):
         multiply(y_ba[:, 0:P], *weights[0], *late_columns(P), False, False)
         multiply(y_ba[:, 0:P], *weights[1], *late_columns(3 * P), False, False)
         multiply(y_ba[:, P : 2 * P], *weights[1], *early_columns(HALF), False, True)
-        ba_out = held.tile([NQ, P + HALF], F32, name="ba_out")
+        ba_out = held.tile([NQ, P + HALF], F32, align_bytes=BURST, name="ba_out")
         nc.scalar.activation(ba_out[:], y_ba[:, 0 : P + HALF], ACT.Copy, scale=recip[:])
         nc.sync.dma_start(out[0][:, 0 : P + HALF], ba_out[:])
 
         y_c = banks.tile([NQ, P], F32, tag="bank6", name="y_c")
         multiply(y_c[:], *weights[0], *late_columns(HALF), True, False)
         multiply(y_c[:], *weights[1], *late_columns(0), False, True)
-        c_out = held.tile([NQ, HALF], F32, name="c_out")
+        c_out = held.tile([NQ, HALF], F32, align_bytes=BURST, name="c_out")
         nc.vector.tensor_scalar(c_out[:], y_c[:, 0:HALF], recip[:], None, ALU.mult)
         nc.sync.dma_start(out[0][:, P + HALF : DV], c_out[:])

@@ -17,6 +17,8 @@ PORT_ROWS = 4
 HALF = P // 2
 SHARE = 640
 BURST = 256
+RUN = 16
+BLOCKS = PASS // (PAIR * RUN)
 
 FLOPS = 2 * NQ * N * (D + DV)
 BYTES = 4 * (D * T + DV * T + D * NQ + T + NQ + NQ * DV) + 2 * P * (N // LIST_ROWS)
@@ -77,7 +79,7 @@ def tile_attend_x_cap_sink_kernel(tc, qT, kT, vT, vs, sink, offs, out):
             nc.vector.tensor_copy(dealt, window[:].indirect(offsets[:, first // LIST_ROWS : (first + count) // LIST_ROWS]))
 
         def deal(columns):
-            return columns.rearrange("p (g u s i) -> p g s u i", u=PAIR, s=P, i=PAIR)
+            return columns.rearrange("p (g u b j) -> p g b u j", u=PAIR, b=BLOCKS, j=RUN)
 
         def quantise(codes, scales, grouped):
             nc.vector.quantize_mx(out=codes.bitcast(FP8X4), scales=scales, in_=grouped)
@@ -120,18 +122,18 @@ def tile_attend_x_cap_sink_kernel(tc, qT, kT, vT, vs, sink, offs, out):
         for g in range(PASSES):
             vs_turned = banks.tile([P, PACK, P], F32, tag=f"bank{6 + g}", name="vs_turned")
             for t in range(PACK):
-                nc.tensor.transpose(vs_turned[:, t, :], vs_picked[:, g * PASS + t : (g + 1) * PASS : PACK], ident[:])
+                nc.tensor.transpose(vs_turned[:, t, :], vs_picked[:, g * PASS + t * P : g * PASS + (t + 1) * P], ident[:])
             nc.scalar.copy(vs_parts[:, g], vs_turned[:, :, 0 : QUARTERS * PORT_ROWS : PORT_ROWS])
         nc.gpsimd.tensor_tensor(vs_pairs[:], vs_parts[:, :, :, 0:2], vs_parts[:, :, :, 2:4], ALU.add)
         nc.gpsimd.tensor_tensor(vs_cols[:], vs_pairs[:, :, :, 0], vs_pairs[:, :, :, 1], ALU.add)
         vs_spread = []
         for g in range(PASSES):
-            vs_spread.append(banks.tile([NQ, PAIR, P, PAIR], F32, tag=f"bank{4 + g}", name="vs_spread"))
+            vs_spread.append(banks.tile([NQ, PASS], F32, tag=f"bank{4 + g}", name="vs_spread"))
+            by_page = vs_spread[g][:].rearrange("q (u t b j) -> q t b u j", u=PAIR, t=PACK, j=RUN)
             for t in range(PACK):
-                u, i = divmod(t, PAIR)
-                nc.tensor.transpose(vs_spread[g][:, u, :, i], vs_cols[:, g, t : t + 1].to_broadcast([P, NQ]), ident[:])
+                nc.tensor.transpose(by_page[:, t], vs_cols[:, g, t : t + 1].to_broadcast([P, NQ]), ident[:])
 
-        gather(k_late[:, :, 0, :].rearrange("p g (u s i) -> p g s u i", u=PAIR, i=PAIR), k_pool[2], 0, N)
+        gather(k_late[:, :, 0, :].rearrange("p g (u b j) -> p g b u j", u=PAIR, j=RUN), k_pool[2], 0, N)
 
         capped = after_max.tile([NQ, N + 1], F32, align_bytes=64, offset=0, name="capped")
         sink_less = held.tile([NQ, 1], F32, name="sink_less")
@@ -186,7 +188,7 @@ def tile_attend_x_cap_sink_kernel(tc, qT, kT, vT, vs, sink, offs, out):
 
         def token_scales(i):
             g, u = divmod(i, PAIR)
-            return vs_spread[g][:, u].rearrange("q s i -> q (s i)")
+            return vs_spread[g][:, piece(u)]
 
         w_rows = [held.tile([NQ, PIECE], BF16, name=f"w_rows{i}") for i in range(PIECES)]
         for i in (0, 2):

@@ -45,7 +45,7 @@ def tile_attend_x_cap_sink_kernel(tc, qT, kT, vT, vs, sink, offs, out):
         tc.tile_pool(name="after_c", bufs=1) as after_c,
         tc.psum_pool(name="banks", bufs=1) as banks,
     ):
-        offsets = held.tile([P, N // LIST_ROWS], U16, name="offsets")
+        offsets = held.tile([P, N // LIST_ROWS], U16, align_bytes=BURST, name="offsets")
         k_pool = [held.tile([P, T], F32, align_bytes=BURST, name=f"k_pool{j}") for j in range(PACK)]
         a_pool = after_a.tile([P, T], F32, align_bytes=BURST, offset=0, name="a_pool")
         b_pool = after_b.tile([P, T], F32, align_bytes=BURST, offset=0, name="b_pool")
@@ -53,7 +53,7 @@ def tile_attend_x_cap_sink_kernel(tc, qT, kT, vT, vs, sink, offs, out):
         vs_pool = held.tile([P, T], F32, align_bytes=BURST, name="vs_pool")
         q_raw = after_q.tile([P, PACK, NQ], F32, align_bytes=BURST, offset=0, name="q_raw")
         sink_col = held.tile([P, 1], F32, name="sink_col")
-        ident = held.tile([P, P], F32, name="ident")
+        ident = held.tile([P, P], F32, align_bytes=BURST, name="ident")
 
         for window in (vs_pool, a_pool):
             nc.vector.memset(window[:], 0.0)
@@ -205,9 +205,9 @@ def tile_attend_x_cap_sink_kernel(tc, qT, kT, vT, vs, sink, offs, out):
         )
 
         aw_grouped = after_max.tile([P, 2 * PASS], BF16, align_bytes=64, offset=0, name="aw_grouped")
-        b0_grouped = held.tile([P, PASS], BF16, align_bytes=64, name="b0_grouped")
-        wb1_grouped = held.tile([P, 2 * PASS], BF16, align_bytes=64, name="wb1_grouped")
-        c_grouped = [held.tile([P, PIECE], BF16, align_bytes=64, name=f"c_grouped{g}") for g in range(PASSES)]
+        b0_grouped = held.tile([P, PASS], BF16, align_bytes=BURST, name="b0_grouped")
+        wb1_grouped = held.tile([P, 2 * PASS], BF16, align_bytes=BURST, name="wb1_grouped")
+        c_grouped = [held.tile([P, PIECE], BF16, align_bytes=BURST, name=f"c_grouped{g}") for g in range(PASSES)]
         a_turned = banks.tile([P, PASSES, PAIR, P], F32, tag="bank6", name="a_turned")
         for i in range(PIECES):
             g, u = divmod(i, PAIR)
@@ -225,19 +225,19 @@ def tile_attend_x_cap_sink_kernel(tc, qT, kT, vT, vs, sink, offs, out):
             turn([b_picked[:, piece(PAIR * g + u)] for u in range(PAIR)], grouped, f"bank{2 + g}", 1)
 
         recip = after_b.tile([NQ, 1], F32, align_bytes=64, offset=0, name="recip")
-        aw_codes = after_b.tile([P, 2 * P], U32, align_bytes=64, offset=64, name="aw_codes")
-        aw_scales = held.tile([P, 2 * P], U8, align_bytes=64, name="aw_scales")
+        aw_codes = after_b.tile([P, 2 * P], U32, align_bytes=BURST, offset=BURST, name="aw_codes")
+        aw_scales = held.tile([P, 2 * P], U8, align_bytes=BURST, name="aw_scales")
         nc.vector.reciprocal(recip[:], total[:])
         quantise(aw_codes[:], aw_scales[:], aw_grouped[:])
 
-        c_picked = [held.tile([P, PASS], BF16, name=f"c_picked{g}") for g in range(PASSES)]
+        c_picked = [held.tile([P, PASS], BF16, align_bytes=BURST, name=f"c_picked{g}") for g in range(PASSES)]
         for g in range(PASSES):
             gather(deal(c_picked[g][:]), c_pool, g * PASS, PASS)
         for g in range(PASSES):
             turn([c_picked[g][:, piece(u)] for u in range(PAIR)], c_grouped[g][:], f"bank{4 + g}", 2)
 
         late_codes = after_c.tile([P, 4 * P], U32, align_bytes=64, offset=0, name="late_codes")
-        late_scales = held.tile([P, 4 * P], U8, align_bytes=64, name="late_scales")
+        late_scales = held.tile([P, 4 * P], U8, align_bytes=BURST, name="late_scales")
 
         def early_columns(first, count=P):
             return aw_codes[:, first : first + count], aw_scales[:, first : first + count]

@@ -17,8 +17,6 @@ PORT_ROWS = 4
 HALF = P // 2
 SHARE = 640
 BURST = 256
-RUN = 16
-BLOCKS = PASS // (PAIR * RUN)
 
 FLOPS = 2 * NQ * N * (D + DV)
 BYTES = 4 * (D * T + DV * T + D * NQ + T + NQ + NQ * DV) + 2 * P * (N // LIST_ROWS)
@@ -75,11 +73,14 @@ def tile_attend_x_cap_sink_kernel(tc, qT, kT, vT, vs, sink, offs, out):
         nc.sync.dma_start(b_pool[:], vT[0:P, :])
         nc.sync.dma_start(c_pool[0:P:2, :], vT[P + HALF : DV, :])
 
-        def gather(dealt, window, first, count):
-            nc.vector.tensor_copy(dealt, window[:].indirect(offsets[:, first // LIST_ROWS : (first + count) // LIST_ROWS]))
+        def listed(window, first, count):
+            return window[:].indirect(offsets[:, first // LIST_ROWS : (first + count) // LIST_ROWS])
 
-        def deal(columns):
-            return columns.rearrange("p (g u b j) -> p g b u j", u=PAIR, b=BLOCKS, j=RUN)
+        def vector_gather(picked, window, first, count):
+            nc.vector.tensor_copy(picked, listed(window, first, count))
+
+        def scalar_gather(picked, window, first, count):
+            nc.scalar.activation(picked, listed(window, first, count), ACT.Copy)
 
         def quantise(codes, scales, grouped):
             nc.vector.quantize_mx(out=codes.bitcast(FP8X4), scales=scales, in_=grouped)
@@ -95,10 +96,14 @@ def tile_attend_x_cap_sink_kernel(tc, qT, kT, vT, vs, sink, offs, out):
                 stop=stop,
             )
 
-        def turn(dealt, grouped, bank, step):
-            turned = banks.tile([P, PAIR, P], F32, tag=bank, name="turned")
+        def turn_words(turned, rows):
+            words = rows.bitcast(F32)
             for u in range(PAIR):
-                nc.tensor.transpose(turned[:, u, :], dealt[u].bitcast(F32), ident[:])
+                nc.tensor.transpose(turned[:, u, :], words[:, u : PASS // PAIR : PAIR], ident[:])
+
+        def turn(rows, grouped, bank, step):
+            turned = banks.tile([P, PAIR, P], F32, tag=bank, name="turned")
+            turn_words(turned, rows)
             nc.scalar.copy(
                 grouped.bitcast(F32).rearrange("p (e u) -> p e u", u=PAIR),
                 turned[:, :, 0:P:step].rearrange("p u e -> p e u"),
@@ -111,7 +116,7 @@ def tile_attend_x_cap_sink_kernel(tc, qT, kT, vT, vs, sink, offs, out):
         k_early = held.tile([P, PAIR, N], BF16, name="k_early")
         k_late = held.tile([P, PASSES, PAIR, PASS], BF16, name="k_late")
         for j in range(PAIR):
-            gather(deal(k_early[:, j, :]), k_pool[j], 0, N)
+            vector_gather(k_early[:, j, :], k_pool[j], 0, N)
         nc.scalar.copy(k_grouped[:, :, 0:PAIR], k_early[:].rearrange("p j s -> p s j"))
 
         vs_picked = held.tile([P, N], F32, name="vs_picked")
@@ -129,19 +134,18 @@ def tile_attend_x_cap_sink_kernel(tc, qT, kT, vT, vs, sink, offs, out):
         vs_spread = []
         for g in range(PASSES):
             vs_spread.append(banks.tile([NQ, PASS], F32, tag=f"bank{4 + g}", name="vs_spread"))
-            by_page = vs_spread[g][:].rearrange("q (u t b j) -> q t b u j", u=PAIR, t=PACK, j=RUN)
             for t in range(PACK):
-                nc.tensor.transpose(by_page[:, t], vs_cols[:, g, t : t + 1].to_broadcast([P, NQ]), ident[:])
+                nc.tensor.transpose(vs_spread[g][:, t * P : (t + 1) * P], vs_cols[:, g, t : t + 1].to_broadcast([P, NQ]), ident[:])
 
-        gather(k_late[:, :, 0, :].rearrange("p g (u b j) -> p g b u j", u=PAIR, j=RUN), k_pool[2], 0, N)
+        vector_gather(k_late[:, :, 0, :], k_pool[2], 0, N)
 
         capped = after_max.tile([NQ, N + 1], F32, align_bytes=64, offset=0, name="capped")
         sink_less = held.tile([NQ, 1], F32, name="sink_less")
         nc.gpsimd.tensor_scalar(capped[:, N : N + 1], sink_col[:], 0.5, 0.0, ALU.mult, ALU.add)
-        nc.gpsimd.tensor_scalar(sink_less[:], sink_col[:], 1.0, -math.log(PIECES), ALU.mult, ALU.add)
+        nc.gpsimd.tensor_scalar(sink_less[:], sink_col[:], 1.0, -math.log(PAIR), ALU.mult, ALU.add)
 
         for g in range(PASSES):
-            gather(deal(k_late[:, g, 1, :]), k_pool[3], g * PASS, PASS)
+            vector_gather(k_late[:, g, 1, :], k_pool[3], g * PASS, PASS)
 
         q_grouped = held.tile([P, NQ, PACK], BF16, align_bytes=64, name="q_grouped")
         q_codes = held.tile([P, NQ], U32, align_bytes=64, name="q_codes")
@@ -161,7 +165,7 @@ def tile_attend_x_cap_sink_kernel(tc, qT, kT, vT, vs, sink, offs, out):
         runs = [(0, PIECE), (3 * PIECE, N), (SHARE, 3 * PIECE), (PIECE, PASS), (PASS, SHARE)]
         for i, (first, last) in enumerate(runs):
             if i == len(runs) - 1:
-                k_codes = after_scores.tile([P, last - first], U32, align_bytes=64, offset=0, name="k_codes_last")
+                k_codes = after_scores.tile([P, last - first], U32, align_bytes=64, offset=4 * PASS - BURST, name="k_codes_last")
             else:
                 k_codes = held.tile([P, last - first], U32, align_bytes=64, name=f"k_codes{i}")
             k_scales = after_q.tile([P, last - first], U8, align_bytes=64, offset=first, name=f"k_scales{i}")
@@ -170,14 +174,23 @@ def tile_attend_x_cap_sink_kernel(tc, qT, kT, vT, vs, sink, offs, out):
             multiply(score[:], q_codes[:], q_scales[:], k_codes[:], k_scales[:], True, True)
             nc.scalar.activation(capped[:, first:last], score[:], ACT.Tanh, scale=0.5)
 
-        lifted_all = after_scores.tile([NQ, N], F32, align_bytes=64, offset=0, name="lifted_all")
-        lifted = [lifted_all[:, piece(i)] for i in range(PIECES)]
-        terms = held.tile([NQ, PIECES], F32, name="terms")
-        for i in (0, 2, 1, 3):
-            nc.scalar.activation(lifted[i], capped[:, piece(i)], ACT.Exp, scale=2.0, accum_out=terms[:, i : i + 1])
+        halves = [
+            after_scores.tile([NQ, PASSES, PIECE], F32, align_bytes=64, offset=4 * PASS * u, name=f"lifted{u}")
+            for u in range(PAIR)
+        ]
+        lifted = [halves[i % PAIR][:, i // PAIR, :] for i in range(PIECES)]
+        terms = held.tile([NQ, PAIR], F32, name="terms")
+        for u in range(PAIR):
+            nc.scalar.activation(
+                halves[u][:],
+                capped[:, 0:N].rearrange("q (g u s) -> q g u s", g=PASSES, u=PAIR)[:, :, u, :],
+                ACT.Exp,
+                scale=2.0,
+                accum_out=terms[:, u : u + 1],
+            )
 
         a_picked = held.tile([P, N], BF16, name="a_picked")
-        gather(deal(a_picked[:]), a_pool, 0, N)
+        vector_gather(a_picked[:], a_pool, 0, N)
 
         half_max = after_a.tile([NQ, 1], F32, align_bytes=64, offset=0, name="half_max")
         shrink = held.tile([NQ, 1], F32, name="shrink")
@@ -190,53 +203,58 @@ def tile_attend_x_cap_sink_kernel(tc, qT, kT, vT, vs, sink, offs, out):
             g, u = divmod(i, PAIR)
             return vs_spread[g][:, piece(u)]
 
-        w_rows = [held.tile([NQ, PIECE], BF16, name=f"w_rows{i}") for i in range(PIECES)]
+        w_pass = [held.tile([NQ, PASS], BF16, align_bytes=64, name=f"w_pass{g}") for g in range(PASSES)]
+        w_rows = [w_pass[i // PAIR][:, piece(i % PAIR)] for i in range(PIECES)]
         for i in (0, 2):
             scaled = after_a.tile([NQ, PIECE], F32, align_bytes=64, offset=4 * PIECE * (i + 1), name=f"scaled{i}")
             nc.vector.tensor_tensor(scaled[:], lifted[i], token_scales(i), ALU.mult)
-            nc.scalar.activation(w_rows[i][:], scaled[:], ACT.Copy, scale=shrink[:])
+            nc.scalar.activation(w_rows[i], scaled[:], ACT.Copy, scale=shrink[:])
         for i in (1, 3):
-            nc.vector.scalar_tensor_tensor(w_rows[i][:], lifted[i], shrink[:], token_scales(i), ALU.mult, ALU.mult)
+            nc.vector.scalar_tensor_tensor(w_rows[i], lifted[i], shrink[:], token_scales(i), ALU.mult, ALU.mult)
 
-        shares = held.tile([NQ, PIECES], F32, name="shares")
+        shares = held.tile([NQ, PAIR], F32, name="shares")
         total = held.tile([NQ, 1], F32, name="total")
         nc.scalar.activation(
             shares[:], terms[:], ACT.Identity, scale=shrink[:], bias=sink_share[:], accum_out=total[:]
         )
 
-        aw_grouped = after_max.tile([P, 2 * PASS], BF16, align_bytes=64, offset=0, name="aw_grouped")
-        b0_grouped = held.tile([P, PASS], BF16, align_bytes=BURST, name="b0_grouped")
-        wb1_grouped = held.tile([P, 2 * PASS], BF16, align_bytes=BURST, name="wb1_grouped")
+        aw_grouped = after_b.tile([P, 2 * PASS], BF16, align_bytes=BURST, offset=BURST, name="aw_grouped")
+        w1_grouped = after_b.tile([P, PASS], BF16, align_bytes=BURST, offset=BURST + 4 * PASS, name="w1_grouped")
+        b_grouped = [
+            after_c.tile([P, PASS], BF16, align_bytes=BURST, offset=2 * PASS * (2 + g), name=f"b_grouped{g}")
+            for g in range(PASSES)
+        ]
         c_grouped = [held.tile([P, PIECE], BF16, align_bytes=BURST, name=f"c_grouped{g}") for g in range(PASSES)]
         a_turned = banks.tile([P, PASSES, PAIR, P], F32, tag="bank6", name="a_turned")
-        for i in range(PIECES):
-            g, u = divmod(i, PAIR)
-            nc.tensor.transpose(a_turned[:, g, u, :], a_picked[:, piece(i)].bitcast(F32), ident[:])
+        for g in range(PASSES):
+            turn_words(a_turned[:, g], a_picked[:, g * PASS : (g + 1) * PASS])
         nc.scalar.copy(
             aw_grouped[:, 0:PASS].bitcast(F32).rearrange("p (g e u) -> p g e u", g=PASSES, u=PAIR),
             a_turned[:, :, :, 0:P:2].rearrange("p g u e -> p g e u"),
         )
-        turn([w_rows[u][:] for u in range(PAIR)], aw_grouped[:, PASS : 2 * PASS], "bank0", 1)
-        turn([w_rows[PAIR + u][:] for u in range(PAIR)], wb1_grouped[:, 0:PASS], "bank1", 1)
+        b_picked = [held.tile([P, PASS], BF16, align_bytes=BURST, name=f"b_picked{g}") for g in range(PASSES)]
+        vector_gather(b_picked[0][:], b_pool, 0, PASS)
+        scalar_gather(b_picked[1][:], b_pool, PASS, PASS)
 
-        b_picked = held.tile([P, N], BF16, name="b_picked")
-        gather(deal(b_picked[:]), b_pool, 0, N)
-        for g, grouped in enumerate((b0_grouped[:], wb1_grouped[:, PASS : 2 * PASS])):
-            turn([b_picked[:, piece(PAIR * g + u)] for u in range(PAIR)], grouped, f"bank{2 + g}", 1)
+        turn(w_pass[0][:], aw_grouped[:, PASS : 2 * PASS], "bank0", 1)
+        turn(w_pass[1][:], w1_grouped[:], "bank1", 1)
+        for g in range(PASSES):
+            turn(b_picked[g][:], b_grouped[g][:], f"bank{2 + g}", 1)
 
         recip = after_b.tile([NQ, 1], F32, align_bytes=64, offset=0, name="recip")
-        aw_codes = after_b.tile([P, 2 * P], U32, align_bytes=BURST, offset=BURST, name="aw_codes")
+        aw_codes = held.tile([P, 2 * P], U32, align_bytes=BURST, name="aw_codes")
         aw_scales = held.tile([P, 2 * P], U8, align_bytes=BURST, name="aw_scales")
         nc.vector.reciprocal(recip[:], total[:])
         quantise(aw_codes[:], aw_scales[:], aw_grouped[:])
 
         c_picked = [held.tile([P, PASS], BF16, align_bytes=BURST, name=f"c_picked{g}") for g in range(PASSES)]
         for g in range(PASSES):
-            gather(deal(c_picked[g][:]), c_pool, g * PASS, PASS)
+            vector_gather(c_picked[g][:, piece(0)], c_pool, g * PASS, PIECE)
+            scalar_gather(c_picked[g][:, piece(1)], c_pool, g * PASS + PIECE, PIECE)
         for g in range(PASSES):
-            turn([c_picked[g][:, piece(u)] for u in range(PAIR)], c_grouped[g][:], f"bank{4 + g}", 2)
+            turn(c_picked[g][:], c_grouped[g][:], f"bank{4 + g}", 2)
 
-        late_codes = after_c.tile([P, 4 * P], U32, align_bytes=64, offset=0, name="late_codes")
+        late_codes = after_c.tile([P, 4 * P], U32, align_bytes=BURST, offset=0, name="late_codes")
         late_scales = held.tile([P, 4 * P], U8, align_bytes=BURST, name="late_scales")
 
         def early_columns(first, count=P):
@@ -245,17 +263,18 @@ def tile_attend_x_cap_sink_kernel(tc, qT, kT, vT, vs, sink, offs, out):
         def late_columns(first, count=P):
             return late_codes[:, first : first + count], late_scales[:, first : first + count]
 
-        quantise(*late_columns(P), b0_grouped[:])
-        quantise(*late_columns(2 * P, 2 * P), wb1_grouped[:])
+        quantise(*late_columns(3 * P), w1_grouped[:])
+        for g in range(PASSES):
+            quantise(*late_columns((1 + g) * P), b_grouped[g][:])
         quantise(*late_columns(HALF, HALF), c_grouped[0][:])
         quantise(*late_columns(0, HALF), c_grouped[1][:])
 
-        weights = [early_columns(P), late_columns(2 * P)]
+        weights = [early_columns(P), late_columns(3 * P)]
         y_ba = banks.tile([NQ, 2 * P], F32, tag="bank7", name="y_ba")
         multiply(y_ba[:, P : 2 * P], *weights[0], *early_columns(0), True, False)
+        multiply(y_ba[:, P : 2 * P], *weights[1], *early_columns(HALF), False, False)
         multiply(y_ba[:, 0:P], *weights[0], *late_columns(P), False, False)
-        multiply(y_ba[:, 0:P], *weights[1], *late_columns(3 * P), False, False)
-        multiply(y_ba[:, P : 2 * P], *weights[1], *early_columns(HALF), False, True)
+        multiply(y_ba[:, 0:P], *weights[1], *late_columns(2 * P), False, True)
         ba_out = held.tile([NQ, P + HALF], F32, align_bytes=BURST, name="ba_out")
         nc.scalar.activation(ba_out[:], y_ba[:, 0 : P + HALF], ACT.Copy, scale=recip[:])
         nc.sync.dma_start(out[0][:, 0 : P + HALF], ba_out[:])

@@ -53,10 +53,10 @@ def tile_attend_x_cap_sink_kernel(tc, qT, kT, vT, vs, sink, offs, out):
         sink_col = held.tile([P, 1], F32, name="sink_col")
         ident = held.tile([P, P], F32, align_bytes=BURST, name="ident")
 
-        for window in (vs_pool, a_pool):
-            nc.vector.memset(window[:], 0.0)
+        nc.vector.memset(vs_pool[:], 0.0)
         make_identity(nc, ident[:])
-        nc.gpsimd.memset(c_pool[:], 0.0)
+        for window in (a_pool, c_pool):
+            nc.gpsimd.memset(window[:], 0.0)
 
         k_rows = kT.rearrange("(p j) t -> p j t", j=PACK)
         nc.sync.dma_start(k_pool[0][:], k_rows[:, 0, :])
@@ -101,10 +101,10 @@ def tile_attend_x_cap_sink_kernel(tc, qT, kT, vT, vs, sink, offs, out):
             for u in range(PAIR):
                 nc.tensor.transpose(turned[:, u, :], words[:, u : PASS // PAIR : PAIR], ident[:])
 
-        def turn(rows, grouped, bank, step):
+        def turn(rows, grouped, bank, step, copy):
             turned = banks.tile([P, PAIR, P], F32, tag=bank, name="turned")
             turn_words(turned, rows)
-            nc.scalar.copy(
+            copy(
                 grouped.bitcast(F32).rearrange("p (e u) -> p e u", u=PAIR),
                 turned[:, :, 0:P:step].rearrange("p u e -> p e u"),
             )
@@ -115,8 +115,8 @@ def tile_attend_x_cap_sink_kernel(tc, qT, kT, vT, vs, sink, offs, out):
         k_grouped = held.tile([P, N, PACK], BF16, align_bytes=64, name="k_grouped")
         k_early = held.tile([P, PAIR, N], BF16, name="k_early")
         k_late = held.tile([P, PASSES, PAIR, PASS], BF16, name="k_late")
-        for j in range(PAIR):
-            vector_gather(k_early[:, j, :], k_pool[j], 0, N)
+        scalar_gather(k_early[:, 0, :], k_pool[0], 0, N)
+        vector_gather(k_early[:, 1, :], k_pool[1], 0, N)
         nc.scalar.copy(k_grouped[:, :, 0:PAIR], k_early[:].rearrange("p j s -> p s j"))
 
         vs_picked = held.tile([P, N], F32, name="vs_picked")
@@ -218,41 +218,42 @@ def tile_attend_x_cap_sink_kernel(tc, qT, kT, vT, vs, sink, offs, out):
             shares[:], terms[:], ACT.Identity, scale=shrink[:], bias=sink_share[:], accum_out=total[:]
         )
 
-        aw_grouped = after_b.tile([P, 2 * PASS], BF16, align_bytes=BURST, offset=BURST, name="aw_grouped")
-        w1_grouped = after_b.tile([P, PASS], BF16, align_bytes=BURST, offset=BURST + 4 * PASS, name="w1_grouped")
-        b_grouped = [
-            after_c.tile([P, PASS], BF16, align_bytes=BURST, offset=2 * PASS * (2 + g), name=f"b_grouped{g}")
+        a_grouped = held.tile([P, PASS], BF16, align_bytes=BURST, name="a_grouped")
+        w_grouped = [
+            after_b.tile([P, PASS], BF16, align_bytes=BURST, offset=BURST + 2 * PASS * g, name=f"w_grouped{g}")
             for g in range(PASSES)
         ]
+        b_grouped = after_c.tile([P, N], BF16, align_bytes=BURST, offset=4 * PASS, name="b_grouped")
         c_grouped = [held.tile([P, PIECE], BF16, align_bytes=BURST, name=f"c_grouped{g}") for g in range(PASSES)]
-        a_turned = banks.tile([P, PASSES, PAIR, P], F32, tag="bank6", name="a_turned")
+        a_turned = banks.tile([P, PASSES, PAIR, P], F32, tag="bank7", name="a_turned")
         for g in range(PASSES):
             turn_words(a_turned[:, g], a_picked[:, g * PASS : (g + 1) * PASS])
         nc.scalar.copy(
-            aw_grouped[:, 0:PASS].bitcast(F32).rearrange("p (g e u) -> p g e u", g=PASSES, u=PAIR),
+            a_grouped[:].bitcast(F32).rearrange("p (g e u) -> p g e u", g=PASSES, u=PAIR),
             a_turned[:, :, :, 0:P:2].rearrange("p g u e -> p g e u"),
         )
         b_picked = [held.tile([P, PASS], BF16, align_bytes=BURST, name=f"b_picked{g}") for g in range(PASSES)]
         vector_gather(b_picked[0][:], b_pool, 0, PASS)
         scalar_gather(b_picked[1][:], b_pool, PASS, PASS)
 
-        turn(w_pass[0][:], aw_grouped[:, PASS : 2 * PASS], "bank0", 1)
-        turn(w_pass[1][:], w1_grouped[:], "bank1", 1)
         for g in range(PASSES):
-            turn(b_picked[g][:], b_grouped[g][:], f"bank{2 + g}", 1)
+            turn(w_pass[g][:], w_grouped[g][:], f"bank{g}", 1, nc.scalar.copy)
 
         recip = after_b.tile([NQ, 1], F32, align_bytes=64, offset=0, name="recip")
         aw_codes = held.tile([P, 2 * P], U32, align_bytes=BURST, name="aw_codes")
         aw_scales = held.tile([P, 2 * P], U8, align_bytes=BURST, name="aw_scales")
         nc.vector.reciprocal(recip[:], total[:])
-        quantise(aw_codes[:], aw_scales[:], aw_grouped[:])
+        quantise(aw_codes[:, 0:P], aw_scales[:, 0:P], a_grouped[:])
+        quantise(aw_codes[:, P : 2 * P], aw_scales[:, P : 2 * P], w_grouped[0][:])
 
         c_picked = [held.tile([P, PASS], BF16, align_bytes=BURST, name=f"c_picked{g}") for g in range(PASSES)]
         for g in range(PASSES):
             vector_gather(c_picked[g][:, piece(0)], c_pool, g * PASS, PIECE)
             scalar_gather(c_picked[g][:, piece(1)], c_pool, g * PASS + PIECE, PIECE)
+        for g, copy in enumerate((nc.scalar.copy, nc.vector.tensor_copy)):
+            turn(b_picked[g][:], b_grouped[:, g * PASS : (g + 1) * PASS], f"bank{2 + g}", 1, copy)
         for g in range(PASSES):
-            turn(c_picked[g][:], c_grouped[g][:], f"bank{4 + g}", 2)
+            turn(c_picked[g][:], c_grouped[g][:], f"bank{4 + g}", 2, nc.scalar.copy)
 
         late_codes = after_c.tile([P, 4 * P], U32, align_bytes=BURST, offset=0, name="late_codes")
         late_scales = held.tile([P, 4 * P], U8, align_bytes=BURST, name="late_scales")
@@ -263,9 +264,8 @@ def tile_attend_x_cap_sink_kernel(tc, qT, kT, vT, vs, sink, offs, out):
         def late_columns(first, count=P):
             return late_codes[:, first : first + count], late_scales[:, first : first + count]
 
-        quantise(*late_columns(3 * P), w1_grouped[:])
-        for g in range(PASSES):
-            quantise(*late_columns((1 + g) * P), b_grouped[g][:])
+        quantise(*late_columns(3 * P), w_grouped[1][:])
+        quantise(*late_columns(P, 2 * P), b_grouped[:])
         quantise(*late_columns(HALF, HALF), c_grouped[0][:])
         quantise(*late_columns(0, HALF), c_grouped[1][:])
 

@@ -15,7 +15,6 @@ LIST_ROWS = 16
 QUARTERS = 4
 PORT_ROWS = 4
 HALF = P // 2
-SHARE = 640
 BURST = 256
 
 FLOPS = 2 * NQ * N * (D + DV)
@@ -101,7 +100,7 @@ def tile_attend_x_cap_sink_kernel(tc, qT, kT, vT, vs, sink, offs, out):
             for u in range(PAIR):
                 nc.tensor.transpose(turned[:, u, :], words[:, u : PASS // PAIR : PAIR], ident[:])
 
-        def turn(rows, grouped, bank, step, copy):
+        def turn(rows, grouped, bank, step, copy=nc.scalar.copy):
             turned = banks.tile([P, PAIR, P], F32, tag=bank, name="turned")
             turn_words(turned, rows)
             copy(
@@ -124,11 +123,11 @@ def tile_attend_x_cap_sink_kernel(tc, qT, kT, vT, vs, sink, offs, out):
         vs_pairs = held.tile([P, PASSES, PACK, 2], F32, name="vs_pairs")
         vs_cols = held.tile([P, PASSES, PACK], F32, name="vs_cols")
         nc.vector.tensor_copy(vs_picked[:], vs_pool[:].indirect(offsets[:]))
-        for g in range(PASSES):
-            vs_turned = banks.tile([P, PACK, P], F32, tag=f"bank{6 + g}", name="vs_turned")
-            for t in range(PACK):
-                nc.tensor.transpose(vs_turned[:, t, :], vs_picked[:, g * PASS + t * P : g * PASS + (t + 1) * P], ident[:])
-            nc.scalar.copy(vs_parts[:, g], vs_turned[:, :, 0 : QUARTERS * PORT_ROWS : PORT_ROWS])
+        used = QUARTERS * PORT_ROWS
+        vs_turned = banks.tile([P, PASS], F32, tag="bank6", name="vs_turned")
+        for page in range(N // P):
+            nc.tensor.transpose(vs_turned[:, page * used : page * used + P], vs_picked[:, page * P : (page + 1) * P], ident[:])
+        nc.scalar.copy(vs_parts[:].rearrange("p g t r -> p (g t r)"), vs_turned[:, 0 : N // P * used : PORT_ROWS])
         nc.gpsimd.tensor_tensor(vs_pairs[:], vs_parts[:, :, :, 0:2], vs_parts[:, :, :, 2:4], ALU.add)
         nc.gpsimd.tensor_tensor(vs_cols[:], vs_pairs[:, :, :, 0], vs_pairs[:, :, :, 1], ALU.add)
         vs_spread = []
@@ -144,25 +143,25 @@ def tile_attend_x_cap_sink_kernel(tc, qT, kT, vT, vs, sink, offs, out):
         nc.gpsimd.tensor_scalar(capped[:, N : N + 1], sink_col[:], 0.5, 0.0, ALU.mult, ALU.add)
         nc.gpsimd.tensor_scalar(sink_less[:], sink_col[:], 1.0, -math.log(PAIR), ALU.mult, ALU.add)
 
-        for g in range(PASSES):
-            vector_gather(k_late[:, g, 1, :], k_pool[3], g * PASS, PASS)
+        scalar_gather(k_late[:, 0, 1, :], k_pool[3], 0, PASS)
+        vector_gather(k_late[:, 1, 1, :], k_pool[3], PASS, PASS)
 
         q_grouped = held.tile([P, NQ, PACK], BF16, align_bytes=64, name="q_grouped")
         q_codes = held.tile([P, NQ], U32, align_bytes=64, name="q_codes")
         q_scales = held.tile([P, NQ], U8, align_bytes=64, name="q_scales")
-        nc.gpsimd.tensor_scalar(q_grouped[:], q_raw[:].rearrange("p j w -> p w j"), 1.0, 0.0, ALU.mult, ALU.add)
-        quantise(q_codes[:], q_scales[:], q_grouped[:].rearrange("p w j -> p (w j)"))
+        nc.vector.tensor_copy(q_grouped[:], q_raw[:].rearrange("p j w -> p w j"))
 
         def place(copy, first, last):
             g = first // PASS
             late = k_late[:, g, :, first - g * PASS : last - g * PASS]
             copy(k_grouped[:, first:last, PAIR:PACK], late.rearrange("p j s -> p s j"))
 
-        for first, last in ((0, PIECE), (PIECE, PASS), (PASS, SHARE)):
+        for first, last in ((0, PIECE), (PIECE, PASS)):
             place(nc.scalar.copy, first, last)
-        place(nc.vector.tensor_copy, SHARE, N)
+        place(nc.vector.tensor_copy, PASS, N)
+        quantise(q_codes[:], q_scales[:], q_grouped[:].rearrange("p w j -> p (w j)"))
 
-        runs = [(0, PIECE), (3 * PIECE, N), (SHARE, 3 * PIECE), (PIECE, PASS), (PASS, SHARE)]
+        runs = [(0, PIECE), (PASS, 3 * PIECE), (3 * PIECE, N), (PIECE, PASS)]
         for i, (first, last) in enumerate(runs):
             if i == len(runs) - 1:
                 k_codes = after_scores.tile([P, last - first], U32, align_bytes=64, offset=4 * PASS - BURST, name="k_codes_last")
@@ -170,7 +169,7 @@ def tile_attend_x_cap_sink_kernel(tc, qT, kT, vT, vs, sink, offs, out):
                 k_codes = held.tile([P, last - first], U32, align_bytes=64, name=f"k_codes{i}")
             k_scales = after_q.tile([P, last - first], U8, align_bytes=64, offset=first, name=f"k_scales{i}")
             quantise(k_codes[:], k_scales[:], k_grouped[:, first:last, :].rearrange("p s j -> p (s j)"))
-            score = banks.tile([NQ, last - first], F32, tag=f"bank{(0, 1, 2, 3, 7)[i]}", name="score")
+            score = banks.tile([NQ, last - first], F32, tag=f"bank{(0, 1, 2, 7)[i]}", name="score")
             multiply(score[:], q_codes[:], q_scales[:], k_codes[:], k_scales[:], True, True)
             nc.scalar.activation(capped[:, first:last], score[:], ACT.Tanh, scale=0.5)
 
@@ -219,11 +218,9 @@ def tile_attend_x_cap_sink_kernel(tc, qT, kT, vT, vs, sink, offs, out):
         )
 
         a_grouped = held.tile([P, PASS], BF16, align_bytes=BURST, name="a_grouped")
-        w_grouped = [
-            after_b.tile([P, PASS], BF16, align_bytes=BURST, offset=BURST + 2 * PASS * g, name=f"w_grouped{g}")
-            for g in range(PASSES)
-        ]
-        b_grouped = after_c.tile([P, N], BF16, align_bytes=BURST, offset=4 * PASS, name="b_grouped")
+        w0_grouped = after_b.tile([P, PASS], BF16, align_bytes=BURST, offset=BURST, name="w0_grouped")
+        wb_grouped = after_b.tile([P, N], BF16, align_bytes=BURST, offset=BURST + 2 * PASS, name="wb_grouped")
+        b1_grouped = after_c.tile([P, PASS], BF16, align_bytes=BURST, offset=4 * PASS, name="b1_grouped")
         c_grouped = [held.tile([P, PIECE], BF16, align_bytes=BURST, name=f"c_grouped{g}") for g in range(PASSES)]
         a_turned = banks.tile([P, PASSES, PAIR, P], F32, tag="bank7", name="a_turned")
         for g in range(PASSES):
@@ -233,27 +230,28 @@ def tile_attend_x_cap_sink_kernel(tc, qT, kT, vT, vs, sink, offs, out):
             a_turned[:, :, :, 0:P:2].rearrange("p g u e -> p g e u"),
         )
         b_picked = [held.tile([P, PASS], BF16, align_bytes=BURST, name=f"b_picked{g}") for g in range(PASSES)]
-        vector_gather(b_picked[0][:], b_pool, 0, PASS)
-        scalar_gather(b_picked[1][:], b_pool, PASS, PASS)
-
         for g in range(PASSES):
-            turn(w_pass[g][:], w_grouped[g][:], f"bank{g}", 1, nc.scalar.copy)
+            vector_gather(b_picked[g][:, piece(0)], b_pool, g * PASS, PIECE)
+            scalar_gather(b_picked[g][:, piece(1)], b_pool, g * PASS + PIECE, PIECE)
+
+        turn(w_pass[0][:], w0_grouped[:], "bank0", 1)
+        turn(w_pass[1][:], wb_grouped[:, PASS:N], "bank1", 1, nc.vector.tensor_copy)
+        turn(b_picked[0][:], wb_grouped[:, 0:PASS], "bank2", 1)
 
         recip = after_b.tile([NQ, 1], F32, align_bytes=64, offset=0, name="recip")
         aw_codes = held.tile([P, 2 * P], U32, align_bytes=BURST, name="aw_codes")
         aw_scales = held.tile([P, 2 * P], U8, align_bytes=BURST, name="aw_scales")
         nc.vector.reciprocal(recip[:], total[:])
         quantise(aw_codes[:, 0:P], aw_scales[:, 0:P], a_grouped[:])
-        quantise(aw_codes[:, P : 2 * P], aw_scales[:, P : 2 * P], w_grouped[0][:])
+        quantise(aw_codes[:, P : 2 * P], aw_scales[:, P : 2 * P], w0_grouped[:])
 
         c_picked = [held.tile([P, PASS], BF16, align_bytes=BURST, name=f"c_picked{g}") for g in range(PASSES)]
         for g in range(PASSES):
             vector_gather(c_picked[g][:, piece(0)], c_pool, g * PASS, PIECE)
             scalar_gather(c_picked[g][:, piece(1)], c_pool, g * PASS + PIECE, PIECE)
-        for g, copy in enumerate((nc.scalar.copy, nc.vector.tensor_copy)):
-            turn(b_picked[g][:], b_grouped[:, g * PASS : (g + 1) * PASS], f"bank{2 + g}", 1, copy)
+        turn(b_picked[1][:], b1_grouped[:], "bank3", 1)
         for g in range(PASSES):
-            turn(c_picked[g][:], c_grouped[g][:], f"bank{4 + g}", 2, nc.scalar.copy)
+            turn(c_picked[g][:], c_grouped[g][:], f"bank{4 + g}", 2)
 
         late_codes = after_c.tile([P, 4 * P], U32, align_bytes=BURST, offset=0, name="late_codes")
         late_scales = held.tile([P, 4 * P], U8, align_bytes=BURST, name="late_scales")
@@ -264,17 +262,17 @@ def tile_attend_x_cap_sink_kernel(tc, qT, kT, vT, vs, sink, offs, out):
         def late_columns(first, count=P):
             return late_codes[:, first : first + count], late_scales[:, first : first + count]
 
-        quantise(*late_columns(3 * P), w_grouped[1][:])
-        quantise(*late_columns(P, 2 * P), b_grouped[:])
+        quantise(*late_columns(P, 2 * P), wb_grouped[:])
+        quantise(*late_columns(3 * P), b1_grouped[:])
         quantise(*late_columns(HALF, HALF), c_grouped[0][:])
         quantise(*late_columns(0, HALF), c_grouped[1][:])
 
-        weights = [early_columns(P), late_columns(3 * P)]
+        weights = [early_columns(P), late_columns(2 * P)]
         y_ba = banks.tile([NQ, 2 * P], F32, tag="bank7", name="y_ba")
         multiply(y_ba[:, P : 2 * P], *weights[0], *early_columns(0), True, False)
-        multiply(y_ba[:, P : 2 * P], *weights[1], *early_columns(HALF), False, False)
         multiply(y_ba[:, 0:P], *weights[0], *late_columns(P), False, False)
-        multiply(y_ba[:, 0:P], *weights[1], *late_columns(2 * P), False, True)
+        multiply(y_ba[:, P : 2 * P], *weights[1], *early_columns(HALF), False, False)
+        multiply(y_ba[:, 0:P], *weights[1], *late_columns(3 * P), False, True)
         ba_out = held.tile([NQ, P + HALF], F32, align_bytes=BURST, name="ba_out")
         nc.scalar.activation(ba_out[:], y_ba[:, 0 : P + HALF], ACT.Copy, scale=recip[:])
         nc.sync.dma_start(out[0][:, 0 : P + HALF], ba_out[:])

@@ -162,12 +162,14 @@ def tile_attend_x_cap_sink_kernel(tc, qT, kT, vT, vs, sink, offs, out):
         quantise(q_codes[:], q_scales[:], q_grouped[:].rearrange("p w j -> p (w j)"))
 
         runs = [(0, PIECE), (PASS, 3 * PIECE), (3 * PIECE, N), (PIECE, PASS)]
+        key_tiles = []
         for i, (first, last) in enumerate(runs):
             if i == len(runs) - 1:
                 k_codes = after_scores.tile([P, last - first], U32, align_bytes=64, offset=4 * PASS - BURST, name="k_codes_last")
             else:
                 k_codes = held.tile([P, last - first], U32, align_bytes=64, name=f"k_codes{i}")
             k_scales = after_q.tile([P, last - first], U8, align_bytes=64, offset=first, name=f"k_scales{i}")
+            key_tiles.append((k_codes, k_scales))
             quantise(k_codes[:], k_scales[:], k_grouped[:, first:last, :].rearrange("p s j -> p (s j)"))
             score = banks.tile([NQ, last - first], F32, tag=f"bank{(0, 1, 2, 7)[i]}", name="score")
             multiply(score[:], q_codes[:], q_scales[:], k_codes[:], k_scales[:], True, True)
@@ -218,9 +220,9 @@ def tile_attend_x_cap_sink_kernel(tc, qT, kT, vT, vs, sink, offs, out):
         )
 
         a_grouped = held.tile([P, PASS], BF16, align_bytes=BURST, name="a_grouped")
-        w0_grouped = after_b.tile([P, PASS], BF16, align_bytes=BURST, offset=BURST, name="w0_grouped")
+        w1_grouped = after_b.tile([P, PASS], BF16, align_bytes=BURST, offset=BURST, name="w1_grouped")
         wb_grouped = after_b.tile([P, N], BF16, align_bytes=BURST, offset=BURST + 2 * PASS, name="wb_grouped")
-        b1_grouped = after_c.tile([P, PASS], BF16, align_bytes=BURST, offset=4 * PASS, name="b1_grouped")
+        b1_grouped = after_c.tile([P, PASS], BF16, align_bytes=BURST, offset=6 * PASS, name="b1_grouped")
         c_grouped = [held.tile([P, PIECE], BF16, align_bytes=BURST, name=f"c_grouped{g}") for g in range(PASSES)]
         a_turned = banks.tile([P, PASSES, PAIR, P], F32, tag="bank7", name="a_turned")
         for g in range(PASSES):
@@ -234,16 +236,14 @@ def tile_attend_x_cap_sink_kernel(tc, qT, kT, vT, vs, sink, offs, out):
             vector_gather(b_picked[g][:, piece(0)], b_pool, g * PASS, PIECE)
             scalar_gather(b_picked[g][:, piece(1)], b_pool, g * PASS + PIECE, PIECE)
 
-        turn(w_pass[0][:], w0_grouped[:], "bank0", 1)
-        turn(w_pass[1][:], wb_grouped[:, PASS:N], "bank1", 1, nc.vector.tensor_copy)
+        turn(w_pass[0][:], wb_grouped[:, PASS:N], "bank0", 1)
+        turn(w_pass[1][:], w1_grouped[:], "bank1", 1, nc.vector.tensor_copy)
         turn(b_picked[0][:], wb_grouped[:, 0:PASS], "bank2", 1)
 
         recip = after_b.tile([NQ, 1], F32, align_bytes=64, offset=0, name="recip")
-        aw_codes = held.tile([P, 2 * P], U32, align_bytes=BURST, name="aw_codes")
-        aw_scales = held.tile([P, 2 * P], U8, align_bytes=BURST, name="aw_scales")
+        a_codes, a_scales = key_tiles[0]
         nc.vector.reciprocal(recip[:], total[:])
-        quantise(aw_codes[:, 0:P], aw_scales[:, 0:P], a_grouped[:])
-        quantise(aw_codes[:, P : 2 * P], aw_scales[:, P : 2 * P], w0_grouped[:])
+        quantise(a_codes[:, 0:P], a_scales[:, 0:P], a_grouped[:])
 
         c_picked = [held.tile([P, PASS], BF16, align_bytes=BURST, name=f"c_picked{g}") for g in range(PASSES)]
         for g in range(PASSES):
@@ -253,24 +253,25 @@ def tile_attend_x_cap_sink_kernel(tc, qT, kT, vT, vs, sink, offs, out):
         for g in range(PASSES):
             turn(c_picked[g][:], c_grouped[g][:], f"bank{4 + g}", 2)
 
-        late_codes = after_c.tile([P, 4 * P], U32, align_bytes=BURST, offset=0, name="late_codes")
-        late_scales = held.tile([P, 4 * P], U8, align_bytes=BURST, name="late_scales")
+        late_codes = after_c.tile([P, 5 * P], U32, align_bytes=BURST, offset=0, name="late_codes")
+        late_scales = held.tile([P, 5 * P], U8, align_bytes=BURST, name="late_scales")
 
         def early_columns(first, count=P):
-            return aw_codes[:, first : first + count], aw_scales[:, first : first + count]
+            return a_codes[:, first : first + count], a_scales[:, first : first + count]
 
         def late_columns(first, count=P):
             return late_codes[:, first : first + count], late_scales[:, first : first + count]
 
         quantise(*late_columns(P, 2 * P), wb_grouped[:])
+        quantise(*late_columns(4 * P), w1_grouped[:])
         quantise(*late_columns(3 * P), b1_grouped[:])
         quantise(*late_columns(HALF, HALF), c_grouped[0][:])
         quantise(*late_columns(0, HALF), c_grouped[1][:])
 
-        weights = [early_columns(P), late_columns(2 * P)]
+        weights = [late_columns(2 * P), late_columns(4 * P)]
         y_ba = banks.tile([NQ, 2 * P], F32, tag="bank7", name="y_ba")
-        multiply(y_ba[:, P : 2 * P], *weights[0], *early_columns(0), True, False)
-        multiply(y_ba[:, 0:P], *weights[0], *late_columns(P), False, False)
+        multiply(y_ba[:, 0:P], *weights[0], *late_columns(P), True, False)
+        multiply(y_ba[:, P : 2 * P], *weights[0], *early_columns(0), False, False)
         multiply(y_ba[:, P : 2 * P], *weights[1], *early_columns(HALF), False, False)
         multiply(y_ba[:, 0:P], *weights[1], *late_columns(3 * P), False, True)
         ba_out = held.tile([NQ, P + HALF], F32, align_bytes=BURST, name="ba_out")

@@ -16,6 +16,7 @@ QUARTERS = 4
 PORT_ROWS = 4
 HALF = P // 2
 BURST = 256
+SHARE = 640
 
 FLOPS = 2 * NQ * N * (D + DV)
 BYTES = 4 * (D * T + DV * T + D * NQ + T + NQ + NQ * DV) + 2 * P * (N // LIST_ROWS)
@@ -113,7 +114,7 @@ def tile_attend_x_cap_sink_kernel(tc, qT, kT, vT, vs, sink, offs, out):
 
         k_grouped = held.tile([P, N, PACK], BF16, align_bytes=64, name="k_grouped")
         k_early = held.tile([P, PAIR, N], BF16, name="k_early")
-        k_late = held.tile([P, PASSES, PAIR, PASS], BF16, name="k_late")
+        k_late = held.tile([P, PAIR, N], BF16, name="k_late")
         scalar_gather(k_early[:, 0, :], k_pool[0], 0, N)
         vector_gather(k_early[:, 1, :], k_pool[1], 0, N)
         nc.scalar.copy(k_grouped[:, :, 0:PAIR], k_early[:].rearrange("p j s -> p s j"))
@@ -127,7 +128,7 @@ def tile_attend_x_cap_sink_kernel(tc, qT, kT, vT, vs, sink, offs, out):
         vs_turned = banks.tile([P, PASS], F32, tag="bank6", name="vs_turned")
         for page in range(N // P):
             nc.tensor.transpose(vs_turned[:, page * used : page * used + P], vs_picked[:, page * P : (page + 1) * P], ident[:])
-        nc.scalar.copy(vs_parts[:].rearrange("p g t r -> p (g t r)"), vs_turned[:, 0 : N // P * used : PORT_ROWS])
+        nc.vector.tensor_copy(vs_parts[:].rearrange("p g t r -> p (g t r)"), vs_turned[:, 0 : N // P * used : PORT_ROWS])
         nc.gpsimd.tensor_tensor(vs_pairs[:], vs_parts[:, :, :, 0:2], vs_parts[:, :, :, 2:4], ALU.add)
         nc.gpsimd.tensor_tensor(vs_cols[:], vs_pairs[:, :, :, 0], vs_pairs[:, :, :, 1], ALU.add)
         vs_spread = []
@@ -136,15 +137,15 @@ def tile_attend_x_cap_sink_kernel(tc, qT, kT, vT, vs, sink, offs, out):
             for t in range(PACK):
                 nc.tensor.transpose(vs_spread[g][:, t * P : (t + 1) * P], vs_cols[:, g, t : t + 1].to_broadcast([P, NQ]), ident[:])
 
-        vector_gather(k_late[:, :, 0, :], k_pool[2], 0, N)
+        vector_gather(k_late[:, 0, :], k_pool[2], 0, N)
 
         capped = after_max.tile([NQ, N + 1], F32, align_bytes=64, offset=0, name="capped")
         sink_less = held.tile([NQ, 1], F32, name="sink_less")
         nc.gpsimd.tensor_scalar(capped[:, N : N + 1], sink_col[:], 0.5, 0.0, ALU.mult, ALU.add)
         nc.gpsimd.tensor_scalar(sink_less[:], sink_col[:], 1.0, -math.log(PAIR), ALU.mult, ALU.add)
 
-        scalar_gather(k_late[:, 0, 1, :], k_pool[3], 0, PASS)
-        vector_gather(k_late[:, 1, 1, :], k_pool[3], PASS, PASS)
+        scalar_gather(k_late[:, 1, 0:SHARE], k_pool[3], 0, SHARE)
+        vector_gather(k_late[:, 1, SHARE:N], k_pool[3], SHARE, N - SHARE)
 
         q_grouped = held.tile([P, NQ, PACK], BF16, align_bytes=64, name="q_grouped")
         q_codes = held.tile([P, NQ], U32, align_bytes=64, name="q_codes")
@@ -152,16 +153,14 @@ def tile_attend_x_cap_sink_kernel(tc, qT, kT, vT, vs, sink, offs, out):
         nc.vector.tensor_copy(q_grouped[:], q_raw[:].rearrange("p j w -> p w j"))
 
         def place(copy, first, last):
-            g = first // PASS
-            late = k_late[:, g, :, first - g * PASS : last - g * PASS]
-            copy(k_grouped[:, first:last, PAIR:PACK], late.rearrange("p j s -> p s j"))
+            copy(k_grouped[:, first:last, PAIR:PACK], k_late[:, :, first:last].rearrange("p j s -> p s j"))
 
-        for first, last in ((0, PIECE), (PIECE, PASS)):
+        for first, last in ((0, PIECE), (PASS, SHARE), (PIECE, PASS)):
             place(nc.scalar.copy, first, last)
-        place(nc.vector.tensor_copy, PASS, N)
+        place(nc.vector.tensor_copy, SHARE, N)
         quantise(q_codes[:], q_scales[:], q_grouped[:].rearrange("p w j -> p (w j)"))
 
-        runs = [(0, PIECE), (PASS, 3 * PIECE), (3 * PIECE, N), (PIECE, PASS)]
+        runs = [(0, PIECE), (3 * PIECE, N), (PASS, 3 * PIECE), (PIECE, PASS)]
         key_tiles = []
         for i, (first, last) in enumerate(runs):
             if i == len(runs) - 1:

@@ -16,7 +16,7 @@ QUARTERS = 4
 PORT_ROWS = 4
 HALF = P // 2
 BURST = 256
-SHARE = 640
+SHARE = 576
 
 FLOPS = 2 * NQ * N * (D + DV)
 BYTES = 4 * (D * T + DV * T + D * NQ + T + NQ + NQ * DV) + 2 * P * (N // LIST_ROWS)

@@ -36,7 +36,6 @@ def tile_attend_x_cap_sink_kernel(tc, qT, kT, vT, vs, sink, offs, out):
     with (
         tc.tile_pool(name="held", bufs=1) as held,
         tc.tile_pool(name="after_q", bufs=1) as after_q,
-        tc.tile_pool(name="after_scores", bufs=1) as after_scores,
         tc.tile_pool(name="after_max", bufs=1) as after_max,
         tc.tile_pool(name="after_a", bufs=1) as after_a,
         tc.tile_pool(name="after_b", bufs=1) as after_b,
@@ -96,14 +95,21 @@ def tile_attend_x_cap_sink_kernel(tc, qT, kT, vT, vs, sink, offs, out):
                 stop=stop,
             )
 
-        def turn_words(turned, rows):
+        def listed_halves(rows):
             words = rows.bitcast(F32)
-            for u in range(PAIR):
-                nc.tensor.transpose(turned[:, u, :], words[:, u : PASS // PAIR : PAIR], ident[:])
+            return [words[:, u : PASS // PAIR : PAIR] for u in range(PAIR)]
 
-        def turn(rows, grouped, bank, step, copy=nc.scalar.copy):
+        def dealt_halves(rows):
+            words = rows.bitcast(F32)
+            return [words[:, u * P : (u + 1) * P] for u in range(PAIR)]
+
+        def turn_words(turned, halves):
+            for u in range(PAIR):
+                nc.tensor.transpose(turned[:, u, :], halves[u], ident[:])
+
+        def turn(halves, grouped, bank, step, copy=nc.scalar.copy):
             turned = banks.tile([P, PAIR, P], F32, tag=bank, name="turned")
-            turn_words(turned, rows)
+            turn_words(turned, halves)
             copy(
                 grouped.bitcast(F32).rearrange("p (e u) -> p e u", u=PAIR),
                 turned[:, :, 0:P:step].rearrange("p u e -> p e u"),
@@ -126,8 +132,10 @@ def tile_attend_x_cap_sink_kernel(tc, qT, kT, vT, vs, sink, offs, out):
         nc.vector.tensor_copy(vs_picked[:], vs_pool[:].indirect(offsets[:]))
         used = QUARTERS * PORT_ROWS
         vs_turned = banks.tile([P, PASS], F32, tag="bank6", name="vs_turned")
-        for page in range(N // P):
-            nc.tensor.transpose(vs_turned[:, page * used : page * used + P], vs_picked[:, page * P : (page + 1) * P], ident[:])
+        for g in range(PASSES):
+            for t in range(PACK):
+                at = (g * PACK + t) * used
+                nc.tensor.transpose(vs_turned[:, at : at + P], vs_picked[:, g * PASS + t : (g + 1) * PASS : PACK], ident[:])
         nc.vector.tensor_copy(vs_parts[:].rearrange("p g t r -> p (g t r)"), vs_turned[:, 0 : N // P * used : PORT_ROWS])
         nc.gpsimd.tensor_tensor(vs_pairs[:], vs_parts[:, :, :, 0:2], vs_parts[:, :, :, 2:4], ALU.add)
         nc.gpsimd.tensor_tensor(vs_cols[:], vs_pairs[:, :, :, 0], vs_pairs[:, :, :, 1], ALU.add)
@@ -135,7 +143,9 @@ def tile_attend_x_cap_sink_kernel(tc, qT, kT, vT, vs, sink, offs, out):
         for g in range(PASSES):
             vs_spread.append(banks.tile([NQ, PASS], F32, tag=f"bank{4 + g}", name="vs_spread"))
             for t in range(PACK):
-                nc.tensor.transpose(vs_spread[g][:, t * P : (t + 1) * P], vs_cols[:, g, t : t + 1].to_broadcast([P, NQ]), ident[:])
+                u, e = divmod(t, PAIR)
+                spread = vs_spread[g][:, u * PIECE + e : (u + 1) * PIECE : PAIR]
+                nc.tensor.transpose(spread, vs_cols[:, g, t : t + 1].to_broadcast([P, NQ]), ident[:])
 
         vector_gather(k_late[:, 0, :], k_pool[2], 0, N)
 
@@ -163,27 +173,22 @@ def tile_attend_x_cap_sink_kernel(tc, qT, kT, vT, vs, sink, offs, out):
         runs = [(0, PIECE), (3 * PIECE, N), (PASS, 3 * PIECE), (PIECE, PASS)]
         key_tiles = []
         for i, (first, last) in enumerate(runs):
-            if i == len(runs) - 1:
-                k_codes = after_scores.tile([P, last - first], U32, align_bytes=64, offset=4 * PASS - BURST, name="k_codes_last")
-            else:
-                k_codes = held.tile([P, last - first], U32, align_bytes=64, name=f"k_codes{i}")
+            k_codes = held.tile([P, last - first], U32, align_bytes=64, name=f"k_codes{i}")
             k_scales = after_q.tile([P, last - first], U8, align_bytes=64, offset=first, name=f"k_scales{i}")
             key_tiles.append((k_codes, k_scales))
             quantise(k_codes[:], k_scales[:], k_grouped[:, first:last, :].rearrange("p s j -> p (s j)"))
             score = banks.tile([NQ, last - first], F32, tag=f"bank{(0, 1, 2, 7)[i]}", name="score")
             multiply(score[:], q_codes[:], q_scales[:], k_codes[:], k_scales[:], True, True)
-            nc.scalar.activation(capped[:, first:last], score[:], ACT.Tanh, scale=0.5)
+            dealt = capped[:, first:last].rearrange("q (u s e) -> q u s e", u=PAIR, e=PAIR)
+            nc.scalar.activation(dealt, score[:].rearrange("q (s u e) -> q u s e", u=PAIR, e=PAIR), ACT.Tanh, scale=0.5)
 
-        halves = [
-            after_scores.tile([NQ, PASSES, PIECE], F32, align_bytes=64, offset=4 * PASS * u, name=f"lifted{u}")
-            for u in range(PAIR)
-        ]
+        halves = [held.tile([NQ, PASSES, PIECE], F32, align_bytes=64, name=f"lifted{u}") for u in range(PAIR)]
         lifted = [halves[i % PAIR][:, i // PAIR, :] for i in range(PIECES)]
         terms = held.tile([NQ, PAIR], F32, name="terms")
         for u in range(PAIR):
             nc.scalar.activation(
-                halves[u][:],
-                capped[:, 0:N].rearrange("q (g u s) -> q g u s", g=PASSES, u=PAIR)[:, :, u, :],
+                halves[u][:].rearrange("q g (h s) -> q (g h) s", h=PAIR),
+                capped[:, 0:N].rearrange("q (r u s) -> q r u s", r=PIECES, u=PAIR)[:, :, u, :],
                 ACT.Exp,
                 scale=2.0,
                 accum_out=terms[:, u : u + 1],
@@ -225,7 +230,7 @@ def tile_attend_x_cap_sink_kernel(tc, qT, kT, vT, vs, sink, offs, out):
         c_grouped = [held.tile([P, PIECE], BF16, align_bytes=BURST, name=f"c_grouped{g}") for g in range(PASSES)]
         a_turned = banks.tile([P, PASSES, PAIR, P], F32, tag="bank7", name="a_turned")
         for g in range(PASSES):
-            turn_words(a_turned[:, g], a_picked[:, g * PASS : (g + 1) * PASS])
+            turn_words(a_turned[:, g], listed_halves(a_picked[:, g * PASS : (g + 1) * PASS]))
         nc.scalar.copy(
             a_grouped[:].bitcast(F32).rearrange("p (g e u) -> p g e u", g=PASSES, u=PAIR),
             a_turned[:, :, :, 0:P:2].rearrange("p g u e -> p g e u"),
@@ -235,9 +240,9 @@ def tile_attend_x_cap_sink_kernel(tc, qT, kT, vT, vs, sink, offs, out):
             vector_gather(b_picked[g][:, piece(0)], b_pool, g * PASS, PIECE)
             scalar_gather(b_picked[g][:, piece(1)], b_pool, g * PASS + PIECE, PIECE)
 
-        turn(w_pass[0][:], wb_grouped[:, PASS:N], "bank0", 1)
-        turn(w_pass[1][:], w1_grouped[:], "bank1", 1, nc.vector.tensor_copy)
-        turn(b_picked[0][:], wb_grouped[:, 0:PASS], "bank2", 1)
+        turn(dealt_halves(w_pass[0][:]), wb_grouped[:, PASS:N], "bank0", 1)
+        turn(dealt_halves(w_pass[1][:]), w1_grouped[:], "bank1", 1, nc.vector.tensor_copy)
+        turn(listed_halves(b_picked[0][:]), wb_grouped[:, 0:PASS], "bank2", 1)
 
         recip = after_b.tile([NQ, 1], F32, align_bytes=64, offset=0, name="recip")
         a_codes, a_scales = key_tiles[0]
@@ -248,9 +253,9 @@ def tile_attend_x_cap_sink_kernel(tc, qT, kT, vT, vs, sink, offs, out):
         for g in range(PASSES):
             vector_gather(c_picked[g][:, piece(0)], c_pool, g * PASS, PIECE)
             scalar_gather(c_picked[g][:, piece(1)], c_pool, g * PASS + PIECE, PIECE)
-        turn(b_picked[1][:], b1_grouped[:], "bank3", 1)
+        turn(listed_halves(b_picked[1][:]), b1_grouped[:], "bank3", 1)
         for g in range(PASSES):
-            turn(c_picked[g][:], c_grouped[g][:], f"bank{4 + g}", 2)
+            turn(listed_halves(c_picked[g][:]), c_grouped[g][:], f"bank{4 + g}", 2)
 
         late_codes = after_c.tile([P, 5 * P], U32, align_bytes=BURST, offset=0, name="late_codes")
         late_scales = held.tile([P, 5 * P], U8, align_bytes=BURST, name="late_scales")

@@ -47,7 +47,7 @@ def tile_attend_x_cap_sink_kernel(tc, qT, kT, vT, vs, sink, offs, out):
         a_pool = after_a.tile([P, T], F32, align_bytes=BURST, offset=0, name="a_pool")
         b_pool = after_b.tile([P, T], F32, align_bytes=BURST, offset=0, name="b_pool")
         c_pool = after_c.tile([P, T], F32, align_bytes=BURST, offset=0, name="c_pool")
-        vs_pool = held.tile([P, T], F32, align_bytes=BURST, name="vs_pool")
+        vs_pool = after_b.tile([P, T], F32, align_bytes=BURST, offset=2 * T, name="vs_pool")
         q_raw = after_q.tile([P, PACK, NQ], F32, align_bytes=BURST, offset=0, name="q_raw")
         sink_col = held.tile([P, 1], F32, name="sink_col")
         ident = held.tile([P, P], F32, align_bytes=BURST, name="ident")

import math

import concourse.mybir as mybir
from concourse.masks import make_identity

NQ, D, DV, T, N = 128, 512, 256, 4096, 1024
P = 128
PACK = 4
PASS = P * PACK
PASSES = N // PASS
PAIR = 2
PIECE = P * PAIR
PIECES = N // PIECE
LIST_ROWS = 16
QUARTERS = 4
PORT_ROWS = 4
HALF = P // 2
BURST = 256
SHARE = 576

FLOPS = 2 * NQ * N * (D + DV)
BYTES = 4 * (D * T + DV * T + D * NQ + T + NQ + NQ * DV) + 2 * P * (N // LIST_ROWS)

F32 = mybir.dt.float32
BF16 = mybir.dt.bfloat16
U32 = mybir.dt.uint32
U16 = mybir.dt.uint16
U8 = mybir.dt.uint8
FP8X4 = mybir.dt.float8_e4m3fn_x4
ACT = mybir.ActivationFunctionType
ALU = mybir.AluOpType


def tile_attend_x_cap_sink_kernel(tc, qT, kT, vT, vs, sink, offs, out):
    nc = tc.nc
    with (
        tc.tile_pool(name="held", bufs=1) as held,
        tc.tile_pool(name="after_q", bufs=1) as after_q,
        tc.tile_pool(name="after_max", bufs=1) as after_max,
        tc.tile_pool(name="after_a", bufs=1) as after_a,
        tc.tile_pool(name="after_b", bufs=1) as after_b,
        tc.tile_pool(name="after_c", bufs=1) as after_c,
        tc.psum_pool(name="banks", bufs=1) as banks,
    ):
        offsets = held.tile([P, N // LIST_ROWS], U16, align_bytes=BURST, name="offsets")
        k_pool = [held.tile([P, T], F32, align_bytes=BURST, name=f"k_pool{j}") for j in range(PACK)]
        a_pool = after_a.tile([P, T], F32, align_bytes=BURST, offset=0, name="a_pool")
        b_pool = after_b.tile([P, T], F32, align_bytes=BURST, offset=0, name="b_pool")
        c_pool = after_c.tile([P, T], F32, align_bytes=BURST, offset=0, name="c_pool")
        vs_pool = after_b.tile([P, T], F32, align_bytes=BURST, offset=2 * T, name="vs_pool")
        q_raw = after_q.tile([P, PACK, NQ], F32, align_bytes=BURST, offset=0, name="q_raw")
        sink_col = held.tile([P, 1], F32, name="sink_col")
        ident = held.tile([P, P], F32, align_bytes=BURST, name="ident")

        nc.vector.memset(vs_pool[:], 0.0)
        make_identity(nc, ident[:])
        for window in (a_pool, c_pool):
            nc.gpsimd.memset(window[:], 0.0)

        k_rows = kT.rearrange("(p j) t -> p j t", j=PACK)
        nc.sync.dma_start(k_pool[0][:], k_rows[:, 0, :])
        nc.sync.dma_start(offsets[:], offs)
        nc.sync.dma_start(k_pool[1][:], k_rows[:, 1, :])
        nc.sync.dma_start(sink_col[:], sink[0])
        for r in range(QUARTERS):
            part = slice(r * T // QUARTERS, (r + 1) * T // QUARTERS)
            nc.sync.dma_start(vs_pool[PORT_ROWS * r : PORT_ROWS * r + 1, part], vs[r : r + 1, part])
        nc.sync.dma_start(k_pool[2][:], k_rows[:, 2, :])
        nc.sync.dma_start(k_pool[3][:], k_rows[:, 3, :])
        nc.sync.dma_start(q_raw[:], qT[0].rearrange("(p j) w -> p j w", j=PACK))
        nc.sync.dma_start(a_pool[0:P:2, :], vT[P : P + HALF, :])
        nc.sync.dma_start(b_pool[:], vT[0:P, :])
        nc.sync.dma_start(c_pool[0:P:2, :], vT[P + HALF : DV, :])

        def listed(window, first, count):
            return window[:].indirect(offsets[:, first // LIST_ROWS : (first + count) // LIST_ROWS])

        def vector_gather(picked, window, first, count):
            nc.vector.tensor_copy(picked, listed(window, first, count))

        def scalar_gather(picked, window, first, count):
            nc.scalar.activation(picked, listed(window, first, count), ACT.Copy)

        def quantise(codes, scales, grouped):
            nc.vector.quantize_mx(out=codes.bitcast(FP8X4), scales=scales, in_=grouped)

        def multiply(sums, left, left_scales, right, right_scales, start, stop):
            nc.tensor.matmul_mx(
                out=sums,
                lhsT=left.bitcast(FP8X4),
                lhsT_scale=left_scales,
                rhs=right.bitcast(FP8X4),
                rhs_scale=right_scales,
                start=start,
                stop=stop,
            )

        def listed_halves(rows):
            words = rows.bitcast(F32)
            return [words[:, u : PASS // PAIR : PAIR] for u in range(PAIR)]

        def dealt_halves(rows):
            words = rows.bitcast(F32)
            return [words[:, u * P : (u + 1) * P] for u in range(PAIR)]

        def turn_words(turned, halves):
            for u in range(PAIR):
                nc.tensor.transpose(turned[:, u, :], halves[u], ident[:])

        def turn(halves, grouped, bank, step, copy=nc.scalar.copy):
            turned = banks.tile([P, PAIR, P], F32, tag=bank, name="turned")
            turn_words(turned, halves)
            copy(
                grouped.bitcast(F32).rearrange("p (e u) -> p e u", u=PAIR),
                turned[:, :, 0:P:step].rearrange("p u e -> p e u"),
            )

        def piece(i):
            return slice(i * PIECE, (i + 1) * PIECE)

        k_grouped = held.tile([P, N, PACK], BF16, align_bytes=64, name="k_grouped")
        k_early = held.tile([P, PAIR, N], BF16, name="k_early")
        k_late = held.tile([P, PAIR, N], BF16, name="k_late")
        scalar_gather(k_early[:, 0, :], k_pool[0], 0, N)
        vector_gather(k_early[:, 1, :], k_pool[1], 0, N)
        nc.scalar.copy(k_grouped[:, :, 0:PAIR], k_early[:].rearrange("p j s -> p s j"))

        vs_picked = held.tile([P, N], F32, name="vs_picked")
        vs_parts = held.tile([P, PASSES, PACK, QUARTERS], F32, name="vs_parts")
        vs_pairs = held.tile([P, PASSES, PACK, 2], F32, name="vs_pairs")
        vs_cols = held.tile([P, PASSES, PACK], F32, name="vs_cols")
        nc.vector.tensor_copy(vs_picked[:], vs_pool[:].indirect(offsets[:]))
        used = QUARTERS * PORT_ROWS
        vs_turned = banks.tile([P, PASS], F32, tag="bank6", name="vs_turned")
        for g in range(PASSES):
            for t in range(PACK):
                at = (g * PACK + t) * used
                nc.tensor.transpose(vs_turned[:, at : at + P], vs_picked[:, g * PASS + t : (g + 1) * PASS : PACK], ident[:])
        nc.vector.tensor_copy(vs_parts[:].rearrange("p g t r -> p (g t r)"), vs_turned[:, 0 : N // P * used : PORT_ROWS])
        nc.gpsimd.tensor_tensor(vs_pairs[:], vs_parts[:, :, :, 0:2], vs_parts[:, :, :, 2:4], ALU.add)
        nc.gpsimd.tensor_tensor(vs_cols[:], vs_pairs[:, :, :, 0], vs_pairs[:, :, :, 1], ALU.add)
        vs_spread = []
        for g in range(PASSES):
            vs_spread.append(banks.tile([NQ, PASS], F32, tag=f"bank{4 + g}", name="vs_spread"))
            for t in range(PACK):
                u, e = divmod(t, PAIR)
                spread = vs_spread[g][:, u * PIECE + e : (u + 1) * PIECE : PAIR]
                nc.tensor.transpose(spread, vs_cols[:, g, t : t + 1].to_broadcast([P, NQ]), ident[:])

        vector_gather(k_late[:, 0, :], k_pool[2], 0, N)

        capped = after_max.tile([NQ, N + 1], F32, align_bytes=64, offset=0, name="capped")
        sink_less = held.tile([NQ, 1], F32, name="sink_less")
        nc.gpsimd.tensor_scalar(capped[:, N : N + 1], sink_col[:], 0.5, 0.0, ALU.mult, ALU.add)
        nc.gpsimd.tensor_scalar(sink_less[:], sink_col[:], 1.0, -math.log(PAIR), ALU.mult, ALU.add)

        scalar_gather(k_late[:, 1, 0:SHARE], k_pool[3], 0, SHARE)
        vector_gather(k_late[:, 1, SHARE:N], k_pool[3], SHARE, N - SHARE)

        q_grouped = held.tile([P, NQ, PACK], BF16, align_bytes=64, name="q_grouped")
        q_codes = held.tile([P, NQ], U32, align_bytes=64, name="q_codes")
        q_scales = held.tile([P, NQ], U8, align_bytes=64, name="q_scales")
        nc.vector.tensor_copy(q_grouped[:], q_raw[:].rearrange("p j w -> p w j"))

        def place(copy, first, last):
            copy(k_grouped[:, first:last, PAIR:PACK], k_late[:, :, first:last].rearrange("p j s -> p s j"))

        for first, last in ((0, PIECE), (PASS, SHARE), (PIECE, PASS)):
            place(nc.scalar.copy, first, last)
        place(nc.vector.tensor_copy, SHARE, N)
        quantise(q_codes[:], q_scales[:], q_grouped[:].rearrange("p w j -> p (w j)"))

        runs = [(0, PIECE), (3 * PIECE, N), (PASS, 3 * PIECE), (PIECE, PASS)]
        key_tiles = []
        for i, (first, last) in enumerate(runs):
            k_codes = held.tile([P, last - first], U32, align_bytes=64, name=f"k_codes{i}")
            k_scales = after_q.tile([P, last - first], U8, align_bytes=64, offset=first, name=f"k_scales{i}")
            key_tiles.append((k_codes, k_scales))
            quantise(k_codes[:], k_scales[:], k_grouped[:, first:last, :].rearrange("p s j -> p (s j)"))
            score = banks.tile([NQ, last - first], F32, tag=f"bank{(0, 1, 2, 7)[i]}", name="score")
            multiply(score[:], q_codes[:], q_scales[:], k_codes[:], k_scales[:], True, True)
            dealt = capped[:, first:last].rearrange("q (u s e) -> q u s e", u=PAIR, e=PAIR)
            nc.scalar.activation(dealt, score[:].rearrange("q (s u e) -> q u s e", u=PAIR, e=PAIR), ACT.Tanh, scale=0.5)

        halves = [held.tile([NQ, PASSES, PIECE], F32, align_bytes=64, name=f"lifted{u}") for u in range(PAIR)]
        lifted = [halves[i % PAIR][:, i // PAIR, :] for i in range(PIECES)]
        terms = held.tile([NQ, PAIR], F32, name="terms")
        for u in range(PAIR):
            nc.scalar.activation(
                halves[u][:].rearrange("q g (h s) -> q (g h) s", h=PAIR),
                capped[:, 0:N].rearrange("q (r u s) -> q r u s", r=PIECES, u=PAIR)[:, :, u, :],
                ACT.Exp,
                scale=2.0,
                accum_out=terms[:, u : u + 1],
            )

        a_picked = held.tile([P, N], BF16, name="a_picked")
        vector_gather(a_picked[:], a_pool, 0, N)

        half_max = after_a.tile([NQ, 1], F32, align_bytes=64, offset=0, name="half_max")
        shrink = held.tile([NQ, 1], F32, name="shrink")
        sink_share = held.tile([NQ, 1], F32, name="sink_share")
        nc.vector.tensor_reduce(half_max[:], capped[:], mybir.AxisListType.X, ALU.max)
        nc.scalar.activation(shrink[:], half_max[:], ACT.Exp, scale=-2.0)
        nc.scalar.activation(sink_share[:], half_max[:], ACT.Exp, scale=-2.0, bias=sink_less[:])

        def token_scales(i):
            g, u = divmod(i, PAIR)
            return vs_spread[g][:, piece(u)]

        w_pass = [held.tile([NQ, PASS], BF16, align_bytes=64, name=f"w_pass{g}") for g in range(PASSES)]
        w_rows = [w_pass[i // PAIR][:, piece(i % PAIR)] for i in range(PIECES)]
        for i in (0, 2):
            scaled = after_a.tile([NQ, PIECE], F32, align_bytes=64, offset=4 * PIECE * (i + 1), name=f"scaled{i}")
            nc.vector.tensor_tensor(scaled[:], lifted[i], token_scales(i), ALU.mult)
            nc.scalar.activation(w_rows[i], scaled[:], ACT.Copy, scale=shrink[:])
        for i in (1, 3):
            nc.vector.scalar_tensor_tensor(w_rows[i], lifted[i], shrink[:], token_scales(i), ALU.mult, ALU.mult)

        shares = held.tile([NQ, PAIR], F32, name="shares")
        total = held.tile([NQ, 1], F32, name="total")
        nc.scalar.activation(
            shares[:], terms[:], ACT.Identity, scale=shrink[:], bias=sink_share[:], accum_out=total[:]
        )

        a_grouped = held.tile([P, PASS], BF16, align_bytes=BURST, name="a_grouped")
        w1_grouped = after_b.tile([P, PASS], BF16, align_bytes=BURST, offset=BURST, name="w1_grouped")
        wb_grouped = after_b.tile([P, N], BF16, align_bytes=BURST, offset=BURST + 2 * PASS, name="wb_grouped")
        b1_grouped = after_c.tile([P, PASS], BF16, align_bytes=BURST, offset=6 * PASS, name="b1_grouped")
        c_grouped = [held.tile([P, PIECE], BF16, align_bytes=BURST, name=f"c_grouped{g}") for g in range(PASSES)]
        a_turned = banks.tile([P, PASSES, PAIR, P], F32, tag="bank7", name="a_turned")
        for g in range(PASSES):
            turn_words(a_turned[:, g], listed_halves(a_picked[:, g * PASS : (g + 1) * PASS]))
        nc.scalar.copy(
            a_grouped[:].bitcast(F32).rearrange("p (g e u) -> p g e u", g=PASSES, u=PAIR),
            a_turned[:, :, :, 0:P:2].rearrange("p g u e -> p g e u"),
        )
        b_picked = [held.tile([P, PASS], BF16, align_bytes=BURST, name=f"b_picked{g}") for g in range(PASSES)]
        for g in range(PASSES):
            vector_gather(b_picked[g][:, piece(0)], b_pool, g * PASS, PIECE)
            scalar_gather(b_picked[g][:, piece(1)], b_pool, g * PASS + PIECE, PIECE)

        turn(dealt_halves(w_pass[0][:]), wb_grouped[:, PASS:N], "bank0", 1)
        turn(dealt_halves(w_pass[1][:]), w1_grouped[:], "bank1", 1, nc.vector.tensor_copy)
        turn(listed_halves(b_picked[0][:]), wb_grouped[:, 0:PASS], "bank2", 1)

        recip = after_b.tile([NQ, 1], F32, align_bytes=64, offset=0, name="recip")
        a_codes, a_scales = key_tiles[0]
        nc.vector.reciprocal(recip[:], total[:])
        quantise(a_codes[:, 0:P], a_scales[:, 0:P], a_grouped[:])

        c_picked = [held.tile([P, PASS], BF16, align_bytes=BURST, name=f"c_picked{g}") for g in range(PASSES)]
        for g in range(PASSES):
            vector_gather(c_picked[g][:, piece(0)], c_pool, g * PASS, PIECE)
            scalar_gather(c_picked[g][:, piece(1)], c_pool, g * PASS + PIECE, PIECE)
        turn(listed_halves(b_picked[1][:]), b1_grouped[:], "bank3", 1)
        for g in range(PASSES):
            turn(listed_halves(c_picked[g][:]), c_grouped[g][:], f"bank{4 + g}", 2)

        late_codes = after_c.tile([P, 5 * P], U32, align_bytes=BURST, offset=0, name="late_codes")
        late_scales = held.tile([P, 5 * P], U8, align_bytes=BURST, name="late_scales")

        def early_columns(first, count=P):
            return a_codes[:, first : first + count], a_scales[:, first : first + count]

        def late_columns(first, count=P):
            return late_codes[:, first : first + count], late_scales[:, first : first + count]

        quantise(*late_columns(P, 2 * P), wb_grouped[:])
        quantise(*late_columns(4 * P), w1_grouped[:])
        quantise(*late_columns(3 * P), b1_grouped[:])
        quantise(*late_columns(HALF, HALF), c_grouped[0][:])
        quantise(*late_columns(0, HALF), c_grouped[1][:])

        weights = [late_columns(2 * P), late_columns(4 * P)]
        y_ba = banks.tile([NQ, 2 * P], F32, tag="bank7", name="y_ba")
        multiply(y_ba[:, 0:P], *weights[0], *late_columns(P), True, False)
        multiply(y_ba[:, P : 2 * P], *weights[0], *early_columns(0), False, False)
        multiply(y_ba[:, P : 2 * P], *weights[1], *early_columns(HALF), False, False)
        multiply(y_ba[:, 0:P], *weights[1], *late_columns(3 * P), False, True)
        ba_out = held.tile([NQ, P + HALF], F32, align_bytes=BURST, name="ba_out")
        nc.scalar.activation(ba_out[:], y_ba[:, 0 : P + HALF], ACT.Copy, scale=recip[:])
        nc.sync.dma_start(out[0][:, 0 : P + HALF], ba_out[:])

        y_c = banks.tile([NQ, P], F32, tag="bank6", name="y_c")
        multiply(y_c[:], *weights[0], *late_columns(HALF), True, False)
        multiply(y_c[:], *weights[1], *late_columns(0), False, True)
        c_out = held.tile([NQ, HALF], F32, align_bytes=BURST, name="c_out")
        nc.vector.tensor_scalar(c_out[:], y_c[:, 0:HALF], recip[:], None, ALU.mult)
        nc.sync.dma_start(out[0][:, P + HALF : DV], c_out[:])
